import numpy as np, ml_dtypes
CORES = [40,41,42,43,44,45,46,47]
N = 8
import mx_ref
BF = ml_dtypes.bfloat16
def gentries(a):
    return np.ascontiguousarray(a.reshape(8, 16, -1).transpose(0, 2, 1)).reshape(8, -1)
def gtable(e):
    e = np.asarray(e); return np.ascontiguousarray(e.reshape(8, -1, 16).transpose(0, 2, 1)).reshape(128, -1).astype(np.int32)
def gcols(t, e):
    v = np.concatenate([t.reshape(8, 16, -1, 4), np.zeros((8, 16, 1, 4), BF)], axis=2)
    return np.ascontiguousarray(np.stack([v[g][:, e[g]] for g in range(8)])).reshape(128, -1)
def cut(t, i, w=512):
    return t[:, w * i:w * i + w]
def pick(q, e):
    c = np.concatenate([q[0].reshape(128, -1, 4), np.zeros((128, 1, 4), np.uint8)], axis=1); s = np.concatenate([q[1], np.ones((16, 1), np.uint8)], axis=1)
    return (np.ascontiguousarray(c[:, e].reshape(128, -1)), np.ascontiguousarray(s[:, e]))
def join(*qs):
    return (np.concatenate([q[0] for q in qs], axis=1), np.concatenate([q[1] for q in qs], axis=1))
def put(q, e, v):
    c, s = q[0].reshape(128, -1, 4).copy(), q[1].copy(); c[:, e] = v[0].reshape(128, -1, 4); s[:, e] = v[1]
    return (c.reshape(128, -1), s)
def pk(c, s):
    return (np.ascontiguousarray(c), mx_ref.live(s))
def emit(q):
    return q[0], q[1]
def packed(v, rng):
    q = [mx_ref.quantize(np.ascontiguousarray(v[r])) for r in range(N)]
    return np.stack([a for a, b in q]), np.stack([mx_ref.plane(b, rng) for a, b in q])
def values_of_codes():
    e, c = np.zeros((128, 128, 4), np.float32), np.zeros((128, 2, 4), np.uint8)
    e[np.arange(128), np.arange(128), 0] = 1
    c[:127, :, 0] = np.arange(256).reshape(2, 128).T[:127]
    return mx_ref.matmul(mx_ref.quantize(e.reshape(128, 512).astype(BF)), (c.reshape(128, 8), np.full((16, 2), 127, np.uint8))).T.reshape(-1).astype(np.float64)
CODE_VALUE, SCALE_VALUE = values_of_codes(), 2.0 ** (np.arange(256) - 127.0)
def decode(q):
    return (CODE_VALUE[q[0]].reshape(16, 8, -1, 4) * SCALE_VALUE[q[1]][:, None, :, None] + 0.0).reshape(128, -1).astype(np.float32)
def f(rng, *shape):
    return mx_ref.flush((rng.standard_normal(shape, dtype=np.float32) * np.exp2(rng.integers(-2, 3, shape[:-1] + (1,)))).astype(BF))
def wide(rng, *shape, cols=0):
    v = rng.standard_normal(shape, dtype=np.float32) * np.exp2(rng.integers(-12, 13, shape)).astype(np.float32)
    if cols: v *= np.repeat(np.exp2(rng.integers(-cols, cols + 1, shape[:-2] + (1, shape[-1] // 4))) * (rng.random(shape[:-2] + (1, shape[-1] // 4)) > 0.0625), 4, axis=-1).astype(np.float32)
    return mx_ref.flush(v.astype(BF))
C, E, B, NB, P, R = 320, 64, 64, 4, 256, 3
def big(v):
    v = v.astype(np.float32)
    v[np.abs(v) < np.float32(2.0 ** -16)] = 0
    return v.astype(BF)
def dominators(a, b, lost):
    dom = np.zeros((8, C, C), bool)
    dom[:, np.arange(C), np.arange(C)] = True
    d = np.full((8, P), -1)
    for k in range(NB):
        i = B * k + np.arange(B)
        one = np.take_along_axis(dom, a[:, i, None], axis=1)
        two = np.take_along_axis(dom, b[:, i, None], axis=1)
        both = one & (two | lost[:, i, None])
        d[:, i] = np.max(np.where(both, np.arange(C), -1), axis=2)
        dom[:, E + i] = dom[:, E + i] | both
    return d, np.sum(dom, axis=1)
def numbers_of(rng):
    return {"x": big(f(rng, N, 128, 4 * C)), "u": np.array(f(rng, N, 128, 512)), "v": np.array(f(rng, N, 128, 512))}
def lists_of(rng):
    n = E + B * (np.arange(P) // B)
    w = 2 ** rng.integers(0, 6, (N, 8, 1))
    e = np.argsort(rng.random((N, 8, E)), axis=2)
    l = []
    for k in range(2):
        p = rng.integers(0, n, (N, 8, P))
        l.append(np.where(p < E, np.take_along_axis(e, p % w, axis=2), p))
    return l
def stored(a, b):
    return {"pa": np.stack([gtable(e) for e in a]), "pb": np.stack([gtable(e) for e in b])}
def packedw(w, rng):
    c, p = packed(w, rng)
    return {"wc": c, "ws": p}
def weights(rng, q=-1):
    w = np.array(f(rng, N, 128, 2048)).reshape(N, 128, 4, 128, 4)
    if q >= 0:
        w[:, 16 * q:16 * q + 8] = 0
        w[:, :, :, 16 * q:16 * q + 8] = 0
    return packedw(w.reshape(N, 128, 2048), rng)
def setup_inputs(rng):
    return {**numbers_of(rng), **stored(*lists_of(rng)), **weights(rng)}
def setup_inputs_cuts(rng):
    d = numbers_of(rng)
    q = int(rng.integers(8))
    o, z = rng.permutation(N), rng.permutation(N) % 4
    size = np.array([2.0 ** -30, 2.0 ** -12, 1.0, 2.0 ** 29])[z]
    one = np.where(z % 2 == 0, 2.0 ** -30, 1.0).astype(np.float32).astype(BF)
    less = np.where(z == 0, -2.0 ** -30, 0.0).astype(np.float32).astype(BF)
    k = rng.integers(-1, 2, (N, 8, C, 4))
    k[:, :, :, 3] = 0
    for r in range(N):
        if o[r] == 0:
            k[r, :, :, 0] = np.abs(k[r, :, :, 0])
            k[r, :, :, 1] = -1
        if o[r] == 1:
            k[r, :, :, 0] = -1
            k[r, :, :, 1] = 0
        if o[r] == 2: k[r, :, :, 2] = np.arange(8)[:, None] % 2 * 2 - 1
    mark = np.where((z == 0)[:, None, None, None], 1.5 + 0.125 * k, k)
    x = d["x"].reshape(N, 8, 16, C, 4)
    x[:, q, :8] = (mark * size[:, None, None, None]).astype(np.float32).astype(BF)
    u = d["u"].reshape(N, 128, 128, 4)
    for t in range(R):
        u[:, :, t::16] = 0
        for g in range(8):
            u[:, 16 * q + g, 16 * g + t, t] = one
            u[:, 16 * q + g, 16 * g + t, 3] = less
    return {"x": x.reshape(N, 128, 4 * C), "u": u.reshape(N, 128, 512), "v": d["v"], **stored(*lists_of(rng)), **weights(rng, q)}
def column(j, i):
    return np.where(j < 0, i % E, E + B * j + i)
def setup_inputs_trees(rng):
    d = numbers_of(rng)
    a, b = lists_of(rng)
    o = rng.permutation(N)
    i, j = np.arange(P) % B, np.arange(P) // B
    for r in range(N):
        for g in range(8):
            k = (g + o[r]) % 8
            e = E // 2 + rng.permutation(E // 2)
            if k == 0:
                n = np.full(P, e[0])
                if o[r] % 2: n[rng.permutation(P)[255:]] = e[1]
                a[r, g], b[r, g] = n, n
            if k == 1:
                n = column(j - 1, np.concatenate([rng.permutation(B) for m in range(NB)]))
                a[r, g], b[r, g] = n, n
            if k == 2: a[r, g], b[r, g] = column(j - 1, i), column(rng.integers(-1, j, P), i)
            if k == 3: a[r, g], b[r, g] = column(j - 1, i), column(j - 1, i ^ 1)
            if k == 4:
                a[r, g] = np.where(j == 0, e[0], column(j - 1, rng.integers(0, B, P)))
                b[r, g] = np.where(j == 0, e[0], column(j - 1, rng.integers(0, B, P)))
            if k == 5: a[r, g], b[r, g] = column(j - 1, B - 1 + 0 * i), column(j - 1, 0 * i)
            if k == 6:
                n = np.where(j == 0, e[0], column(j - 1, i))
                a[r, g], b[r, g] = n, np.where(j == NB - 1, column(j - 1, i ^ 1), n)
            if k == 7 and o[r] % 2 == 0:
                n = np.where(rng.permutation(P) < P // 2 - 1, min(e[0], e[1]), max(e[0], e[1]))
                a[r, g], b[r, g] = n, n
    return {**d, **stored(a, b), **weights(rng)}
def setup_inputs_huge(rng):
    d = numbers_of(rng)
    a, b = lists_of(rng)
    e = int(rng.integers(N))
    x = 2.0 ** 28 * (1.7 + 0.15 * rng.random((N, 128, C, 4)))
    c = np.stack([rng.permutation(C) % 2 * 2.0 - 1.0 for r in range(N)])
    c[e] = 0
    c[(e + 1) % N] = -1
    c[(e + 2) % N] = -1
    x *= c[:, None, :, None]
    s = np.stack([rng.permutation(8 * R) % 2 * 2.0 - 1.0 for r in range(N)]).reshape(N, 1, 8, R, 1)
    k, m = [int(g) for g in rng.permutation(8)[:2]]
    i, j = [int(n) for n in rng.permutation(E - 1)[:2]]
    for r in ((e + 1) % N, (e + 2) % N):
        a[r, k] = i
        b[r, k] = j
        x[r, 16 * k:16 * k + 16, i] = -2.0 ** 30
        x[r, 16 * k:16 * k + 16, j] = -2.0 ** 30
        s[r, 0, k] = -1
    r = (e + 2) % N
    a[r, m] = np.where(np.arange(P) < B, i, E)
    b[r, m] = E - 1
    x[r, 16 * m:16 * m + 16, E - 1] = 2.0 ** 30
    s[r, 0, m] = 1
    h = (2.0 ** 30 * (1 - 0.1 * rng.random((N, 128, 8, R, 4))) * s).astype(np.float32).astype(BF)
    u = d["u"].reshape(N, 128, 128, 4)
    for t in range(R): u[:, :, t::16] = h[:, :, :, t]
    w = np.zeros((N, 128, 4, 128, 4), np.float32)
    p = np.arange(128)
    for n in range(4): w[:, p, n, p, n] = 1 - 2 * (p % 2)
    return {"x": x.astype(np.float32).reshape(N, 128, 4 * C).astype(BF), "u": u.reshape(N, 128, 512), "v": d["v"], **stored(a, b), **packedw(w.reshape(N, 128, 2048).astype(BF), rng)}
def setup_inputs_spread(rng):
    d = setup_inputs(rng)
    d["x"] = big(wide(rng, N, 128, 4 * C, cols=6))
    return d
def check_inputs(d):
    b = []
    for k in ("x", "u", "v"):
        a = np.abs(d[k].astype(np.float32))
        if not (np.isfinite(a).all() and ((a == 0) | (a >= 2.0 ** -30) & (a <= 2.0 ** 30)).all()): b.append("a value of " + k)
    n = E + B * (np.arange(P) // B)
    for k in ("pa", "pb"):
        for r in range(N):
            e = gentries(d[k][r])
            if ((e < 0) | (e >= n)).any(): b.append("an entry of " + k)
    if ((d["wc"] == 0x7F) | (d["wc"] == 0xFF)).any(): b.append("a code of wc that is no number")
    return b
def reference(x, u, v, pa, pb, wc, ws):
    qu = [mx_ref.quantize(u[r]) for r in range(N)]
    lay = [pk(wc[r], ws[r]) for r in range(N)]
    a = [gentries(pa[r]).astype(np.int64) for r in range(N)]
    b = [gentries(pb[r]).astype(np.int64) for r in range(N)]
    now = [x[r] for r in range(N)]
    od = np.zeros((N, 8, P), np.float32)
    for t in range(R):
        nodes, feed = [], []
        for r in range(N):
            s = mx_ref.matmul(qu[r], mx_ref.quantize(now[r]))[t::16]
            lost = s[:, E:] + np.float32(0.0) < 0
            d, n = dominators(a[r], b[r], lost)
            h = np.argsort(-n, axis=1, kind="stable")[:, :E]
            feed.append(mx_ref.quantize(gcols(now[r], h)))
            one = gcols(now[r], a[r]).astype(np.float32)
            two = gcols(now[r], np.where(lost, a[r], b[r])).astype(np.float32)
            m = (np.maximum(one, two) + gcols(now[r], d).astype(np.float32)).astype(BF)
            q = mx_ref.quantize(m)
            z = [np.maximum(mx_ref.matmul(pick(lay[r], np.arange(128 * i, 128 * i + 128)), q), np.float32(0.0)) * np.float32(0.015625) for i in range(4)]
            nodes.append((now[r][:, 4 * E:].astype(np.float32) + np.stack(z, axis=2).reshape(128, -1)).astype(BF))
            od[r] = d
        came = decode(join(*feed))
        for r in range(N):
            entry = np.maximum(now[r][:, :4 * E].astype(np.float32), cut(came, (r - 1) % N, 4 * E)).astype(BF)
            now[r] = np.ascontiguousarray(np.concatenate([entry, nodes[r]], axis=1))
    y = np.zeros((N, 128, C), np.float32)
    oc, osc = np.zeros((N, 128, 4 * C), np.uint8), np.zeros((N, 16, C), np.uint8)
    for r in range(N):
        q = mx_ref.quantize(now[r])
        y[r] = mx_ref.matmul(mx_ref.quantize(v[r]), q)
        oc[r], osc[r] = emit(q)
    return {"y": y, "od": od, "oc": oc, "osc": osc}

@@ -1,0 +1,553 @@
+from concourse.mybir import dt, AluOpType, AxisListType, ActivationFunctionType
+
+A = AluOpType
+F = ActivationFunctionType
+C, E, P, R = 320, 64, 256, 3
+X0 = 16
+XN = X0 + 4 * E
+XEND = X0 + 4 * C
+LOST = 2.0 ** 19
+BASE = 160000.0
+MAGIC = 1.5 * 2.0 ** 35
+Q4, U8, U16, F32, BF, I32 = "float8_e4m3fn_x4", "uint8", "uint16", "float32", "bfloat16", "int32"
+
+
+def sb(n, d):
+    return ("sbuf", [128, n], d)
+
+
+SCRATCH = {
+    "xb": sb(XEND, BF), "ub": sb(512, BF), "vb": sb(512, BF), "pab": sb(32, I32),
+    "wq": sb(512, Q4), "wp": sb(512, U8),
+    "qu": sb(128, Q4), "su": sb(128, U8), "qup": sb(384, Q4), "sup": sb(384, U8),
+    "qv": sb(128, Q4), "sv": sb(128, U8), "qc": sb(512, Q4), "sc": sb(512, U8),
+    "qn": sb(1024, Q4), "sn": sb(1024, U8), "qe": sb(512, Q4), "se": sb(512, U8),
+    "qm": sb(256, Q4), "sm": sb(256, U8), "lq": sb(768, Q4), "ls": sb(768, U8),
+    "hout": sb(48, U16), "hin": sb(48, U16),
+    "pi": sb(4, I32), "pj": sb(8, I32), "pf": sb(8, F32), "ps": sb(8, F32),
+    "k64": sb(64, F32), "sf": sb(4, F32), "cf": sb(4, F32), "thr": sb(4, F32), "th2": sb(4, F32), "own": sb(192, F32),
+    "cj": sb(64, F32), "tie": sb(256, F32), "wv": sb(256, F32), "cwi": sb(16, F32), "cw": sb(16, F32),
+    "itab": sb(272, F32), "y16": sb(256, BF), "e1": sb(256, BF), "cs16": sb(256, BF),
+    "y4": sb(64, F32), "f1": sb(64, F32), "cs4": sb(64, F32),
+    "ebig": sb(528, BF), "gt": sb(288, F32), "keep": sb(512, BF), "rb": sb(512, BF),
+    "ul": sb(24, U16), "trl": sb(8, U16), "kl": sb(16, U16), "abl": sb(32, U16), "a4": sb(64, U16),
+    "oab": sb(128, F32), "dd": sb(16, F32), "dab": sb(16, F32), "cb": sb(16, F32),
+    "lost": sb(256, BF), "sg": sb(256, BF), "tw": sb(336, F32), "ga": sb(256, F32), "gb": sb(256, F32),
+    "tr": sb(544, F32), "g1": sb(64, F32), "val": sb(64, F32), "loff": sb(64, U16),
+    "dm1": sb(32, F32), "dm2": sb(16, F32), "d4": sb(64, U16), "dl": sb(16, U16), "drow": sb(256, F32),
+    "lsc": sb(256, BF), "lu": sb(16, F32), "lqv": sb(16, F32), "lr": sb(16, F32), "b4": sb(64, U16),
+    "ma": sb(1024, BF), "mb": sb(1024, BF), "mm": sb(1024, BF), "rz": sb(1024, F32),
+    "junk": sb(24 * 256, BF), "hs": sb(8, F32), "hh": sb(8, F32), "rs": sb(512, BF), "rt": sb(512, BF),
+    "nk": sb(16, F32), "key": sb(256, F32), "rk": sb(16, F32), "roff": sb(16, U16),
+    "hw": sb(256, F32), "h4": sb(64, F32), "dx": sb(1024, BF), "ys": sb(C, F32),
+    "pz": ("psum", [128, 2048], F32), "pd": ("psum", [128, 2048], F32),
+}
+NPOOL = {"c": 84, "h": 30, "s": 12}
+SEMAPHORES = (["sent"] + ["arq%d" % t for t in range(R)] + ["arh%d" % t for t in range(R)]
+              + ["%s%d" % (k, i) for k in ("c", "h", "s") for i in range(NPOOL[k])])
+
+PARAMS = {"rank_v": (1, 0, 3), "dx_v": (0, 0, 0), "hist_v": (0, 0, 2), "a3_s": (0, 1, 0), "lost_s": (2, 4, 2)}
+COSTS = {"cyc": 1.04, "gather": 1.56, "scatter": 3.8, "wake": 100.0, "dma": 2000.0, "remote": 2200.0, "pe": 0.7,
+         "tt16": 1.0, "act": 0.0, "issue": 60.0}
+ORDER = [
+    0,1,8,36,2,4,50,3,10,66,12,25,16,18,14,11,9,15,60,13,17,26,20,19,41,39,21,67,22,68,24,40,23,51,55,69,27,44,42,43,61,45,72,71,53,46,
+    54,62,52,78,28,70,58,47,59,56,49,48,29,82,57,30,31,65,5,37,181,6,7,38,94,32,33,95,83,96,100,97,63,101,64,98,102,99,175,103,126,104,
+    127,178,74,108,107,106,172,109,105,76,113,90,112,73,91,111,92,114,93,110,79,116,75,115,128,88,117,77,35,129,118,133,119,131,132,138,
+    120,130,121,179,134,173,137,141,124,182,135,200,176,140,139,180,136,87,142,207,125,144,143,122,208,145,123,147,146,148,183,157,161,
+    177,151,149,163,174,154,155,80,184,153,85,162,188,34,185,156,150,191,189,194,86,84,203,186,190,201,192,205,158,187,152,195,193,159,
+    164,196,160,165,166,197,81,204,167,198,214,168,199,215,216,217,218,219,202,206,169,220,170,221,171,223,222,246,224,247,227,228,248,
+    229,249,232,233,231,230,234,225,226,236,209,235,210,237,299,253,238,252,240,211,290,251,239,212,241,250,213,242,293,244,245,243,291,
+    296,294,254,300,261,297,260,256,295,318,257,321,325,301,255,319,323,298,259,258,292,322,262,326,302,320,263,264,306,265,303,307,312,
+    266,267,304,309,313,268,310,308,278,280,305,281,284,314,279,270,311,282,277,315,275,89,316,332,274,317,333,334,338,335,339,336,341,
+    337,283,340,271,342,345,276,346,269,347,344,273,351,350,272,343,348,324,352,349,353,354,285,355,356,357,286,385,387,383,374,287,382,
+    375,288,388,289,376,358,377,386,390,380,389,384,391,378,359,381,363,360,392,362,394,393,361,395,379,397,396,398,327,328,411,408,399,
+    430,401,329,415,403,330,331,402,427,404,424,400,431,433,428,406,425,410,417,434,450,409,455,457,413,429,451,405,453,432,412,416,435,
+    407,414,426,456,418,458,436,452,419,364,437,420,443,438,446,444,440,447,441,421,365,422,439,423,454,372,445,367,366,371,368,370,373,
+    369,448,442,449,459,460,462,465,468,466,467,469,463,461,464,470,472,474,473,476,475,471,477,478]
+
+
+def r(name, a=0, b=None, s=1, p=None):
+    return (name, a, SCRATCH[name][1][1] if b is None else b, s, p)
+
+
+def bits(ref):
+    name, a, b, s, p = ref
+    if name in ("pz", "pd"):
+        a, b, s = a // 512 * 512, (b + 511) // 512 * 512, 1
+    if s == 1:
+        return (1 << b) - (1 << a)
+    m = 0
+    for c in range(a, b, s):
+        m |= 1 << c
+    return m
+
+
+def width(ref):
+    return len(range(ref[1], ref[2], ref[3]))
+
+
+def narrow(*refs):
+    return all(SCRATCH[x[0]][2] in (BF, U16) for x in refs)
+
+
+def program(par, cm):
+    ops = []
+    cyc = cm["cyc"]
+
+    def op(q, call, args, reads, writes, cost, hold=None, grp=None, cls="c", after=None, tag=None):
+        reads = [x for x in reads if isinstance(x, tuple) and x[0] in SCRATCH]
+        writes = [x for x in writes if x[0] in SCRATCH]
+        ops.append({"q": q, "call": call, "args": args, "reads": reads, "writes": writes, "cost": cost,
+                    "hold": cost if hold is None else hold, "grp": grp, "cls": cls, "after": after, "tag": tag})
+
+    def plain(out, ins):
+        return max(64.0, width(out) * (0.5 if narrow(out, *ins) else 1.0)) * cyc
+
+    def gath(out):
+        return 50 + width(out) * cm["gather"] * cyc
+
+    def memset(out, v, **k):
+        op("v", "memset", (out, v), [], [out], plain(out, []), **k)
+
+    def copy(out, in_, **k):
+        op("v", "copy", (out, in_), [in_], [out], plain(out, [in_]), **k)
+
+    def ts(out, in0, s1, s2, o0, o1=None, **k):
+        op("v", "ts", (out, in0, s1, s2, o0, o1), [in0, s1, s2], [out], plain(out, [in0]), **k)
+
+    def tt(out, in0, in1, o, **k):
+        f = cm["tt16"] if narrow(out, in0, in1) else 1.0
+        op("v", "tt", (out, in0, in1, o), [in0, in1], [out], max(64.0, 2 * f * width(out)) * cyc, **k)
+
+    def ttg(out, win, off, in1, o, **k):
+        op("v", "ttg", (out, win, off, in1, o), [win, off, in1], [out], gath(out), **k)
+
+    def gather(out, win, off, **k):
+        op("v", "gather", (out, win, off), [win, off], [out], gath(out), **k)
+
+    def scan(out, d0, d1, o0, o1, **k):
+        op("v", "scan", (out, d0, d1, o0, o1), [d0, d1], [out], plain(out, [d0, d1]), **k)
+
+    def turn(out, in_, **k):
+        op("v", "turn", (out, in_), [in_], [out], plain(out, [in_]), **k)
+
+    def quant(q, s, in_, **k):
+        op("v", "quant", (q, s, in_), [in_], [q, s], (12 + 0.22 * width(in_)) * cyc / 0.83, **k)
+
+    def act(out, in_, f, scale=1.0, bias=None, acc=None, off=None, **k):
+        c = (65 + width(out) * cm["gather"] * cyc) if off else max(64.0, width(out)) * cyc + cm["act"]
+        op("a", "act", (out, in_, f, scale, bias, acc, off), [in_, scale, bias, off],
+           [out] + ([acc] if acc else []), c + (20 if acc else 0), **k)
+
+    def mm(out, lq, ls, rq, rs, **k):
+        op("t", "mm", (out, lq, ls, rq, rs), [lq, ls, rq, rs], [out], (width(out) + 16) * cm["pe"], **k)
+
+    def iota(out, pat, base, mult=0, **k):
+        op("g", "iota", (out, pat, base, mult), [], [out], 130 + 2 * width(out) * cyc, **k)
+
+    def dma(q, out, in_, kb, **k):
+        op(q, "dma", (out, in_), [in_], [out], cm["dma"] + kb * 5, hold=cm["issue"], cls="s" if q == "g" else "h", **k)
+
+    def send(out, in_, sem, kb, tag):
+        op("g", "send", (out, in_, sem), [in_], [], cm["remote"] + kb * 8, hold=2 * cm["issue"], cls="r", tag=tag)
+
+    def arrive(sem, n, refs, tags):
+        op(None, "arrive", (sem, n), [], refs, 0, cls="r", after=tags)
+
+    def col(name, j):
+        return r(name, j, j + 1)
+
+    dma("a", r("ub"), ("u", 0, 512, 1, None), 128)
+    dma("y", r("xb", XN, XEND), ("x", 4 * E, 4 * C, 1, None), 256, tag="x")
+    dma("a", r("pab", 0, 16), ("pa", 0, 16, 1, None), 8, grp="pab")
+    dma("a", r("pab", 16, 32), ("pb", 0, 16, 1, None), 8, grp="pab")
+    dma("y", r("xb", X0, XN), ("x", 0, 4 * E, 1, None), 64)
+    dma("y", r("wq"), ("wc", 0, 2048, 1, None), 256, grp="w", after=["x"])
+    dma("y", r("wp"), ("ws", 0, 512, 1, None), 64, grp="w", after=["x"])
+    dma("y", r("vb"), ("v", 0, 512, 1, None), 128, after=["x"])
+
+    iota(col("pi", 0), [[0, 1]], 0, 1)
+    iota(col("pi", 1), [[0, 1]], 0, 16)
+    iota(col("pi", 2), [[0, 1]], 0, 17)
+    for j, m in enumerate((3, 4)):
+        ts(col("pj", j), col("pi", 0), m, None, A.bitwise_and, grp="pj")
+    copy(r("pf", 0, 2), r("pj", 0, 2))
+    for j, m in ((2, 15), (3, 31)):
+        ts(col("pj", j), col("pi", 0), m, None, A.bitwise_and, grp="pk")
+    ts(col("pj", 4), col("pi", 0), 2, 3, A.logical_shift_right, A.bitwise_and, grp="pk")
+    ts(col("pj", 5), col("pi", 1), 255, None, A.bitwise_and, grp="pk")
+    ts(col("pj", 6), col("pi", 2), 4, 1, A.logical_shift_right, A.bitwise_and, grp="pk")
+    copy(r("pf", 2, 7), r("pj", 2, 7))
+    lev, flag, pi16, p32, sel, i16, par2 = [col("pf", j) for j in range(7)]
+    slope, tbase, off16, jm, cwb = [col("ps", j) for j in range(5)]
+    act(slope, flag, F.Identity, scale=-1025.0, bias=2052.0)
+    act(tbase, par2, F.Identity, scale=272.0, bias=i16)
+    act(off16, pi16, F.Identity, scale=-4.0, bias=60.0)
+    act(jm, sel, F.Identity, scale=2048.0, bias=lev)
+    act(cwb, pi16, F.Identity, scale=1.0 / 256, bias=-1.0 / 512)
+
+    iota(r("k64"), [[1, 64]], 0)
+    for t in range(R):
+        ts(r("ul", 8 * t, 8 * t + 8), r("k64", 0, 8), 16.0, float(t), A.mult, A.add)
+    quant(r("qu"), r("su"), r("ub"))
+    for t in range(R):
+        o = r("ul", 8 * t, 8 * t + 8)
+        op("v", "pickq", (r("qup", 128 * t, 128 * t + 128), r("qu"), o), [r("qu"), o],
+           [r("qup", 128 * t, 128 * t + 128)], gath(r("qu")), grp="pick%d" % t)
+        act(r("sup", 128 * t, 128 * t + 128), r("su"), F.Copy, off=o, grp="pick%d" % t)
+    memset(r("xb", 0, X0), 0.0)
+    quant(r("qn", 0, 256), r("sn", 0, 256), r("xb", XN, XEND))
+    quant(r("qe", 0, 128), r("se", 0, 128), r("xb", X0, X0 + 512))
+
+    ts(r("sf"), r("k64", 0, 4), lev, slope, A.is_equal, A.mult, grp="sf")
+    ts(r("cf"), r("k64", 0, 4), lev, BASE, A.is_equal, A.mult, grp="sf")
+    ts(r("thr"), r("k64", 1, 5), lev, 1e29, A.is_equal, A.mult)
+    ts(r("th2"), r("k64", 1, 5), lev, 2 * LOST, A.is_equal, A.mult)
+    act(r("tw", 0, 64), r("k64"), F.Identity, scale=col("sf", 0), bias=col("cf", 0))
+    for l in range(1, 4):
+        act(r("own", 64 * l - 64, 64 * l), r("k64"), F.Identity, scale=col("sf", l), bias=col("cf", l))
+    copy(r("abl"), r("pab"))
+    ttg(r("oab", 0, 64), r("tw", 0, 64), r("abl", 0, 4), r("own", 0, 64), A.max)
+    act(r("oab", 64, 128), r("tw", 0, 64), F.Copy, off=r("abl", 16, 20))
+    memset(r("tw", 320, 336), 0.0)
+    iota(r("cj"), [[256, 4], [0, 16]], int(4 - 2 * BASE))
+    for j in range(1, 4):
+        memset(r("cj", 20 * j - 4, 20 * j), -8 * BASE, grp="cj")
+    ts(r("trl"), r("k64", 0, 8), tbase, None, A.add)
+    for t in range(4):
+        ts(r("a4", 16 * t, 16 * t + 16), r("pab", 0, 16), 4.0, float(X0 + t), A.mult, A.add, grp="a4")
+
+    iota(r("y16"), [[0, 16], [1, 16]], 0)
+    ts(r("e1"), r("y16"), pi16, 132.0, A.not_equal, A.mult)
+    act(r("cs16"), r("e1"), F.Identity, bias=-128.0)
+    tt(r("dd"), r("pab", 16, 32), r("pab", 0, 16), A.subtract)
+    act(r("dab"), r("dd"), F.Identity, scale=4.0)
+    ts(r("cb"), r("pab", 16, 32), 4.0, float(X0), A.mult, A.add)
+
+    memset(r("gt", 0, 17), 0.0)
+    ts(r("gt", 17, 49), r("k64", 0, 32), pi16, None, A.is_equal, grp="gt")
+    ts(r("gt", 49, 81), r("k64", 0, 32), pi16, 4096.0, A.is_equal, A.mult, grp="gt")
+    for j in range(1, 4):
+        act(r("gt", 17 + 64 * j, 81 + 64 * j), r("gt", 17, 81), F.Copy, grp="gt2")
+    iota(r("keep"), [[0, 16], [512, 32]], 0)
+    act(r("rb"), r("keep"), F.Copy, scale=0.0)
+    iota(r("wv"), [[128, 2], [256, 4], [4, 32]], 0)
+    act(r("tie"), r("wv"), F.Identity, scale=-1.0 / 1024, bias=255.0 / 256)
+    iota(r("cwi"), [[32, 2], [64, 4], [16, 2]], -255)
+    act(r("cw"), r("cwi"), F.Identity, scale=1.0 / 256, bias=cwb)
+    ts(r("kl"), r("k64", 0, 16), 32.0, p32, A.mult, A.add)
+    iota(r("y4"), [[0, 16], [1, 4]], 0)
+    ts(r("f1"), r("y4"), sel, 10240.0, A.not_equal, A.mult)
+    act(r("cs4"), r("f1"), F.Identity, bias=-8192.0)
+
+    iota(r("ebig"), [[0, 528]], 1)
+    op("g", "strip", (r("ebig"),), [r("ebig")], [r("ebig")], 170 + 2 * 528 * cyc)
+    for b in range(4):
+        quant(r("qc", 128 * b, 128 * b + 128), r("sc", 128 * b, 128 * b + 128), r("ebig", 3 - b, 515 - b))
+    iota(r("itab", 0, 257), [[1, 257]], -1)
+    quant(r("qv"), r("sv"), r("vb"))
+
+    def send_nodes(t):
+        send(r("lq", 256 * t + 64, 256 * t + 256), r("qn", 256 * t, 256 * t + 192), "arq%d" % t, 96, "nq%d" % t)
+        send(r("ls", 256 * t + 64, 256 * t + 256), r("sn", 256 * t, 256 * t + 192), "arq%d" % t, 24, "ns%d" % t)
+
+    def send_entries(t):
+        send(r("lq", 256 * t, 256 * t + 64), r("qe", 128 * t, 128 * t + 64), "arq%d" % t, 32, "eq%d" % t)
+        send(r("ls", 256 * t, 256 * t + 64), r("se", 128 * t, 128 * t + 64), "arq%d" % t, 8, "es%d" % t)
+
+    send_nodes(0)
+    send_entries(0)
+    xw = r("xb")
+
+    for t in range(R):
+        g_ = lambda s: "%s_%d" % (s, t)
+        qn, sn = r("qn", 256 * t, 256 * t + 256), r("sn", 256 * t, 256 * t + 256)
+        mm(r("pz", 0, 256), r("qup", 128 * t, 128 * t + 128), r("sup", 128 * t, 128 * t + 128), qn, sn)
+        for k in range(4 - par["lost_s"][t]):
+            op("v", "ts", (r("lost", 64 * k, 64 * k + 64), r("pz", 64 * k, 64 * k + 64), col("thr", k), LOST, A.is_lt, A.mult),
+               [col("thr", k), r("pz", 0, 256)], [r("lost", 64 * k, 64 * k + 64)], 64 * cyc)
+        act(r("sg"), r("pz", 0, 256), F.Sign)
+        for k in range(4 - par["lost_s"][t], 4):
+            act(r("lost", 64 * k, 64 * k + 64), r("sg", 64 * k, 64 * k + 64), F.Relu, scale=-LOST, bias=col("th2", k))
+        tt(r("gb", 0, 64), r("oab", 64, 128), r("lost", 0, 64), A.max)
+        tt(r("tw", 64, 128), r("oab", 0, 64), r("gb", 0, 64), A.min)
+        for k in range(1, 4):
+            win, a, b = r("tw", 0, 64 + 64 * k), 64 * k, 64 * k + 64
+            if k < 3:
+                ttg(r("ga", a, b), win, r("abl", 4 * k, 4 * k + 4), r("own", a, b), A.max, grp=g_("ab%d" % k))
+            elif par["a3_s"][t]:
+                act(r("ga", a, b), win, F.Copy, off=r("abl", 4 * k, 4 * k + 4), grp=g_("ab%d" % k))
+            else:
+                gather(r("ga", a, b), win, r("abl", 4 * k, 4 * k + 4), grp=g_("ab%d" % k))
+            ttg(r("gb", a, b), win, r("abl", 16 + 4 * k, 20 + 4 * k), r("lost", a, b), A.max, grp=g_("ab%d" % k))
+            tt(r("tw", 64 + a, 64 + b), r("ga", a, b), r("gb", a, b), A.min)
+            a, b, e = ((0, 128, 128), (128, 192, 192), (192, 256, 288))[k - 1]
+            turn(r("tr", a, b), r("tw", 64 + a, 64 + b), grp=g_("tr"))
+            turn(r("tr", 256 + a, 256 + e), r("tw", 48 + a, 48 + e), grp=g_("tr"))
+        ttg(r("g1"), r("tr"), r("trl", 4, 8), r("cj"), A.add)
+        ttg(r("val"), r("tr"), r("trl", 0, 4), r("g1"), A.add)
+        ts(r("loff"), r("val"), 0.25, 0.0, A.mult, A.max)
+        tt(r("dm1"), r("val", 0, 32), r("val", 32, 64), A.max)
+        tt(r("dm2"), r("dm1", 0, 16), r("dm1", 16, 32), A.max)
+        for e in range(4):
+            ts(r("d4", 16 * e, 16 * e + 16), r("dm2"), float(X0 - 4 + e), 0.0, A.add, A.max)
+        if t == R - 1:
+            ts(r("dl"), r("dm2"), 0.25, 0.0, A.mult, A.max)
+            act(r("drow"), r("itab", 0, 257), F.Copy, off=r("dl"))
+            for k in range(8):
+                dma("y", ("od", 0, 256, 1, (k, k + 1)), r("drow", p=(16 * k, 16 * k + 1)), 1, grp="out_od", tag="end")
+        scan(r("lsc"), r("cs16"), r("sg"), A.add, A.max)
+        ts(r("lu"), r("lsc", 15, 256, 16), off16, 0.0, A.subtract, A.min)
+        tt(r("lqv"), r("lu"), r("dab"), A.mult)
+        tt(r("lr"), r("lqv"), r("cb"), A.add)
+        for e in range(4):
+            ts(r("b4", 16 * e, 16 * e + 16), r("lr"), float(e), None, A.add)
+        for j in range(4):
+            for q in range(2):
+                h, n = 2 * j + q, 256 - 64 * j
+                out, win, off = r("junk", 256 * h, 256 * h + n), r("gt", 16 - 16 * q, 273 - 16 * q), r("loff", 20 * j, 16 * j + 16)
+                if h >= 8 - par["hist_v"][t]:
+                    gather(out, win, off)
+                    op("v", "sum", (col("hs", h), out), [out], [col("hs", h)], max(64, n) * cyc, grp=g_("hist"))
+                else:
+                    act(out, win, F.Identity, acc=col("hs", h), off=off, grp=g_("hist"))
+        ts(r("hh"), r("hs"), MAGIC, MAGIC, A.add, A.subtract)
+        tt(r("rb", 0, 256, 32), r("hs"), r("hh"), A.subtract, grp=g_("rb"))
+        ts(r("rb", 256, 512, 32), r("hh"), 2.0 ** -12, None, A.mult, grp=g_("rb"))
+        scan(r("rs"), r("keep"), r("rb"), A.min, A.add)
+        tt(r("nk"), r("cw"), r("rb", 0, 512, 32), A.subtract)
+        turn(r("rt"), r("rs"))
+        ttg(r("key"), r("rt"), r("kl"), r("tie"), A.add)
+        nv = par["rank_v"][t]
+        for c in range(16):
+            out = r("junk", 256 * (8 + c), 256 * (9 + c))
+            if c < nv:
+                op("v", "ts", (out, r("key"), col("nk", c), 0.0, A.add, A.is_gt), [r("key"), col("nk", c)], [out], 256 * cyc)
+                op("v", "sum", (col("rk", c), out), [out], [col("rk", c)], 256 * cyc, grp=g_("rankv"))
+            else:
+                act(out, r("key"), F.Sign, bias=col("nk", c), acc=col("rk", c), grp=g_("ranka"))
+        if nv:
+            copy(r("roff", 0, nv), r("rk", 0, nv), grp=g_("roff"))
+        ts(r("roff", nv, 16), r("rk", nv, 16), 256.0, 0.5, A.add, A.mult, grp=g_("roff"))
+        op("v", "scatter", (r("hw"), r("roff"), r("wv")), [r("roff"), r("wv")], [r("hw")], 50 + 256 * cm["scatter"] * cyc)
+        scan(r("h4"), r("cs4"), r("hw", 0, 64), A.add, A.max)
+        ho, hi = r("hout", 16 * t, 16 * t + 16), r("hin", 16 * t, 16 * t + 16)
+        ts(ho, r("h4", 3, 64, 4), jm, -6144.0, A.add, A.add)
+        send(hi, ho, "arh%d" % t, 4, "h%d" % t)
+        for e in range(4):
+            a, b = 256 * e, 256 * e + 256
+            act(r("ma", a, b), xw, F.Copy, off=r("a4", 16 * e, 16 * e + 16))
+            ttg(r("mb", a, b), xw, r("b4", 16 * e, 16 * e + 16), r("ma", a, b), A.max)
+            ttg(r("mm", e, 1024, 4), xw, r("d4", 16 * e, 16 * e + 16), r("mb", a, b), A.add, grp=g_("m"))
+        quant(r("qm"), r("sm"), r("mm"))
+        for b in range(4):
+            mm(r("pz", 512 * b, 512 * b + 256), r("wq", 128 * b, 128 * b + 128), r("wp", 128 * b, 128 * b + 128), r("qm"), r("sm"))
+            act(r("rz", 256 * b, 256 * b + 256), r("pz", 512 * b, 512 * b + 256), F.Relu, scale=0.015625)
+            tt(r("xb", XN + b, XEND, 4), r("xb", XN + b, XEND, 4), r("rz", 256 * b, 256 * b + 256), A.add, grp=g_("add"))
+        quant(r("qn", 256 * t + 256, 256 * t + 512), r("sn", 256 * t + 256, 256 * t + 512), r("xb", XN, XEND))
+        if t + 1 < R:
+            send_nodes(t + 1)
+        lq, ls = r("lq", 256 * t, 256 * t + 256), r("ls", 256 * t, 256 * t + 256)
+        arrive("arq%d" % t, 4, [lq, ls], ["nq%d" % t, "ns%d" % t, "eq%d" % t, "es%d" % t])
+        for b in range(4):
+            src = r("pd", 512 * b, 512 * b + 256)
+            mm(src, r("qc", 128 * b, 128 * b + 128), r("sc", 128 * b, 128 * b + 128), lq, ls)
+            if b < par["dx_v"][t]:
+                copy(r("dx", b, 1024, 4), src, grp=g_("dx"))
+            else:
+                act(r("dx", b, 1024, 4), src, F.Copy, grp=g_("dx"))
+        arrive("arh%d" % t, 1, [hi], ["h%d" % t])
+        ttg(r("xb", X0, XN), r("dx"), hi, r("xb", X0, XN), A.max)
+        quant(r("qe", 128 * t + 128, 128 * t + 256), r("se", 128 * t + 128, 128 * t + 256), r("xb", X0, X0 + 512))
+        if t + 1 < R:
+            send_entries(t + 1)
+
+    mm(r("pz", 0, 256), r("qv"), r("sv"), r("qn", 768, 1024), r("sn", 768, 1024))
+    act(r("ys", E, C), r("pz", 0, 256), F.Copy)
+    dma("y", ("y", E, C, 1, None), r("ys", E, C), 128, grp="out_n", tag="end")
+    dma("y", ("oc", 4 * E, 4 * C, 1, None), r("qn", 768, 1024), 128, grp="out_n", tag="end")
+    for k in range(4):
+        dma("y", ("osc", E, C, 1, (4 * k, 4 * k + 4)), r("sn", 768, 1024, p=(32 * k, 32 * k + 4)), 1, grp="out_n", tag="end")
+    mm(r("pz", 512, 640), r("qv"), r("sv"), r("qe", 384, 512), r("se", 384, 512))
+    copy(r("ys", 0, E), r("pz", 512, 512 + E))
+    dma("y", ("oc", 0, 4 * E, 1, None), r("qe", 384, 448), 32, grp="out_e", tag="end")
+    for k in range(4):
+        dma("yaya"[k], ("osc", 0, E, 1, (4 * k, 4 * k + 4)), r("se", 384, 448, p=(32 * k, 32 * k + 4)), 1, grp="out_e", tag="end")
+    dma("a", ("y", 0, E, 1, None), r("ys", 0, E), 32, grp="out_e", tag="end")
+    op("y", "end", (), [], [], 0, after=["end"])
+    return ops
+
+
+def graph(ops):
+    members = {}
+    for i, o in enumerate(ops):
+        o["key"] = o["grp"] if o["grp"] else "op%d" % i
+        members.setdefault(o["key"], []).append(i)
+    seen = {}
+    for i, o in enumerate(ops):
+        deps = set()
+        rd = [(x[0], bits(x)) for x in o["reads"]]
+        wr = [(x[0], bits(x)) for x in o["writes"]]
+        for name, m in rd:
+            deps.update(j for j, w, mj in seen.get(name, [])
+                        if mj & m and (w or name in ("pz", "pd") and ops[j]["q"] != o["q"]))
+        for name, m in wr:
+            deps.update(j for j, w, mj in seen.get(name, []) if mj & m)
+        for name, m in rd:
+            seen.setdefault(name, []).append((i, False, m))
+        for name, m in wr:
+            seen.setdefault(name, []).append((i, True, m))
+        if o["after"]:
+            deps.update(j for j in range(i) if ops[j]["tag"] in o["after"])
+        o["deps"] = set(j for j in deps if ops[j]["key"] != o["key"])
+    for o in ops:
+        full = set()
+        for j in o["deps"]:
+            full.update(members[ops[j]["key"]])
+        o["deps"] = full
+    return members
+
+
+def plan(par, order):
+    ops = program(par, COSTS)
+    members = graph(ops)
+    n = len(ops)
+    place = {i: k for k, i in enumerate(order)}
+    assert len(place) == n and all(place[j] < place[i] for i in range(n) for j in ops[i]["deps"])
+    known, at = {}, [0] * n
+    for i in order:
+        o = ops[i]
+        o["waits"] = []
+        if o["q"] is None:
+            continue
+        k = known.get(o["q"], 0)
+        for j in sorted(o["deps"], key=lambda j: -place[j]):
+            if not k >> j & 1:
+                o["waits"].append(ops[j]["key"])
+                for m in members[ops[j]["key"]]:
+                    k |= 1 << m | at[m]
+        known[o["q"]] = k
+        at[i] = k
+    waited = set(w for o in ops for w in o["waits"])
+    pools = {c: [] for c in NPOOL}
+    sems = {}
+    for i in order:
+        o = ops[i]
+        key = o["key"]
+        if key in sems or key not in waited:
+            continue
+        if o["call"] == "arrive":
+            sems[key] = (o["args"][0], -o["args"][1])
+            continue
+        ms = members[key]
+        common = -1
+        for m in ms:
+            common &= at[m]
+        pool = pools[o["cls"]]
+        slot = None
+        for s in pool:
+            if s[1] & common == s[1]:
+                slot = s
+                break
+        if slot is None:
+            slot = ["%s%d" % (o["cls"], len(pool)), 0, 0]
+            pool.append(slot)
+            assert len(pool) <= NPOOL[o["cls"]]
+        for m in ms:
+            slot[1] |= 1 << m
+        slot[2] += len(ms) * (1 if o["cls"] == "c" else 16)
+        sems[key] = (slot[0], slot[2])
+    return ops, sems
+
+
+PLAN = []
+
+
+def rank_program(g, core, T, topo):
+    rank = T.rank_of(core)
+    if rank is None:
+        return
+    if not PLAN:
+        PLAN.append(plan(PARAMS, ORDER))
+    ops, sems = PLAN[0]
+    n = len(T.cores)
+    nxt, prv = T.cores[(rank + 1) % n], T.cores[(rank - 1) % n]
+    rid, pid = topo.addr(nxt)[:2]
+    mask, out_engines, in_engines = topo.mask(core, nxt), len(topo.engines(core, nxt)), len(topo.engines(prv, core))
+    queue = {"g": g, "v": g.vector, "a": g.scalar, "t": g.tensor, "y": g.sync}
+
+    def ap(x):
+        if not isinstance(x, tuple):
+            return x
+        name, a, b, s, p = x
+        rows = slice(None) if p is None else slice(p[0], p[1])
+        return T[name][rows, a:b] if s == 1 else T[name][rows, a:b:s]
+
+    def raw(x):
+        codes = x[0] in SCRATCH and SCRATCH[x[0]][2] == Q4
+        return ap(x).bitcast(dt.uint8) if codes else ap(x)
+
+    sent = [0]
+    for i in ORDER:
+        o = ops[i]
+        if o["q"] is None:
+            continue
+        q, call, x = queue[o["q"]], o["call"], o["args"]
+        for w in o["waits"]:
+            name, count = sems[w]
+            q.wait_ge(T.sem[name], count if count > 0 else -count * in_engines)
+        ins = None
+        if call == "memset":
+            ins = q.memset(ap(x[0]), x[1])
+        elif call == "copy":
+            ins = q.tensor_copy(ap(x[0]), ap(x[1]))
+        elif call == "ts":
+            if x[5] is None:
+                ins = q.tensor_scalar(ap(x[0]), ap(x[1]), ap(x[2]), None, x[4])
+            else:
+                ins = q.tensor_scalar(ap(x[0]), ap(x[1]), ap(x[2]), ap(x[3]), x[4], x[5])
+        elif call == "tt":
+            ins = q.tensor_tensor(ap(x[0]), ap(x[1]), ap(x[2]), x[3])
+        elif call == "ttg":
+            ins = q.tensor_tensor(ap(x[0]), ap(x[1]).indirect(ap(x[2])), ap(x[3]), x[4])
+        elif call == "gather":
+            ins = q.tensor_copy(ap(x[0]), ap(x[1]).indirect(ap(x[2])))
+        elif call == "scatter":
+            ins = q.tensor_copy(ap(x[0]).indirect(ap(x[1])), ap(x[2]))
+        elif call == "pickq":
+            ins = q.tensor_copy(ap(x[0]).bitcast(dt.uint32), ap(x[1]).bitcast(dt.uint32).indirect(ap(x[2])))
+        elif call == "scan":
+            ins = q.tensor_tensor_scan(ap(x[0]), ap(x[1]), ap(x[2]), 0.0, x[3], x[4])
+        elif call == "turn":
+            ins = q.transpose(ap(x[0]), ap(x[1]))
+        elif call == "sum":
+            ins = q.tensor_reduce(ap(x[0]), ap(x[1]), AxisListType.X, A.add)
+        elif call == "quant":
+            ins = q.quantize_mx(ap(x[0]), ap(x[1]), ap(x[2]))
+        elif call == "act":
+            src = ap(x[1]).indirect(ap(x[6])) if x[6] else ap(x[1])
+            kw = {}
+            if x[3] != 1.0:
+                kw["scale"] = ap(x[3])
+            if x[4] is not None:
+                kw["bias"] = ap(x[4])
+            if x[5]:
+                kw["accum_out"] = ap(x[5])
+            ins = q.activation(ap(x[0]), src, x[2], **kw)
+        elif call == "mm":
+            ins = q.matmul_mx(ap(x[0]), ap(x[1]), ap(x[2]), ap(x[3]), ap(x[4]), True, True)
+        elif call == "iota":
+            if SCRATCH[x[0][0]][2] == I32:
+                ins = q.iota(ap(x[0]), x[1], x[2], x[3])
+            else:
+                ins = q.iota(ap(x[0]), x[1], x[2], x[3], allow_small_or_imprecise_dtypes=True)
+        elif call == "strip":
+            ins = q.affine_select(ap(x[0]), ap(x[0]), [[1, 528]], A.is_equal, 0.0, -3, -4)
+        elif call == "dma":
+            ins = q.dma_start(raw(x[0]), raw(x[1]))
+        elif call == "send":
+            q.remote_dma(raw(x[0]), raw(x[1]), T.sem[x[2]], T.sem["sent"], pid, rid, mask)
+            sent[0] += out_engines
+        if ins is not None and o["key"] in sems:
+            ins.then_inc(T.sem[sems[o["key"]][0]], 1 if o["cls"] == "c" else 16)
+    g.wait_ge(T.sem["sent"], sent[0])

@@ -5,11 +5,13 @@ F = ActivationFunctionType
 C, E, P, R = 320, 64, 256, 3
 X0 = 16
 XN = X0 + 4 * E
-XEND = X0 + 4 * C
+XW = X0 + 4 * C
 LOST = 2.0 ** 19
 BASE = 160000.0
 MAGIC = 1.5 * 2.0 ** 35
+TINY = 1e-37
 Q4, U8, U16, F32, BF, I32 = "float8_e4m3fn_x4", "uint8", "uint16", "float32", "bfloat16", "int32"
+BANKS = ("pz", "pc", "pd")
 
 
 def sb(n, d):
@@ -17,53 +19,47 @@ def sb(n, d):
 
 
 SCRATCH = {
-    "xb": sb(XEND, BF), "ub": sb(512, BF), "vb": sb(512, BF), "pab": sb(32, I32),
+    "xs": sb(4 * XW, BF), "ub": sb(512, BF), "vb": sb(512, BF), "pab": sb(32, I32),
     "wq": sb(512, Q4), "wp": sb(512, U8),
     "qu": sb(128, Q4), "su": sb(128, U8), "qup": sb(384, Q4), "sup": sb(384, U8),
     "qv": sb(128, Q4), "sv": sb(128, U8), "qc": sb(512, Q4), "sc": sb(512, U8),
-    "qn": sb(1024, Q4), "sn": sb(1024, U8), "qe": sb(512, Q4), "se": sb(512, U8),
+    "qx": sb(4 * C, Q4), "sx": sb(4 * C, U8),
     "qm": sb(256, Q4), "sm": sb(256, U8), "lq": sb(768, Q4), "ls": sb(768, U8),
     "hout": sb(48, U16), "hin": sb(48, U16),
-    "pi": sb(4, I32), "pj": sb(8, I32), "pf": sb(8, F32), "ps": sb(8, F32),
-    "k64": sb(64, F32), "sf": sb(4, F32), "cf": sb(4, F32), "thr": sb(4, F32), "th2": sb(4, F32), "own": sb(192, F32),
-    "cj": sb(64, F32), "tie": sb(256, F32), "wv": sb(256, F32), "cwi": sb(16, F32), "cw": sb(16, F32),
-    "itab": sb(272, F32), "y16": sb(256, BF), "e1": sb(256, BF), "cs16": sb(256, BF),
-    "y4": sb(64, F32), "f1": sb(64, F32), "cs4": sb(64, F32),
-    "ebig": sb(528, BF), "gt": sb(288, F32), "keep": sb(512, BF), "rb": sb(512, BF),
-    "ul": sb(24, U16), "trl": sb(8, U16), "kl": sb(16, U16), "abl": sb(32, U16), "a4": sb(64, U16),
-    "oab": sb(128, F32), "dd": sb(16, F32), "dab": sb(16, F32), "cb": sb(16, F32),
-    "lost": sb(256, BF), "sg": sb(256, BF), "tw": sb(336, F32), "ga": sb(256, F32), "gb": sb(256, F32),
-    "tr": sb(544, F32), "g1": sb(64, F32), "val": sb(64, F32), "loff": sb(64, U16),
-    "dm1": sb(32, F32), "dm2": sb(16, F32), "d4": sb(64, U16), "dl": sb(16, U16), "drow": sb(256, F32),
-    "lsc": sb(256, BF), "lu": sb(16, F32), "lqv": sb(16, F32), "lr": sb(16, F32), "b4": sb(64, U16),
+    "pi": sb(2, I32), "pj": sb(8, I32), "pf": sb(8, F32), "ps": sb(10, F32),
+    "k64": sb(64, F32), "sf": sb(4, F32), "cf": sb(4, F32), "thr": sb(4, F32), "own": sb(192, F32),
+    "ra": sb(64, F32), "oa": sb(64, F32), "eq0": sb(64, F32), "thr0": sb(64, F32),
+    "cj": sb(64, F32), "y4": sb(64, F32), "f1": sb(64, F32), "cs4": sb(64, F32),
+    "y16": sb(256, BF), "e1": sb(256, BF), "cs16": sb(256, BF), "ki": sb(36, F32),
+    "mtab": sb(272, BF), "ttab": sb(272, BF), "ktab": sb(272, BF), "sbi": sb(4, F32), "sj": sb(4, F32),
+    "tie": sb(64, F32), "cso": sb(64, F32), "keep": sb(256, BF), "ebig": sb(528, BF), "gt": sb(304, BF),
+    "ul": sb(24, U16), "kl": sb(20, U16),
+    "abl": sb(32, U16), "a4": sb(64, U16), "a4x": sb(16, F32), "dd": sb(16, F32), "econ": sb(64, F32),
+    "a4f": sb(64, F32), "d64": sb(64, F32), "c1": sb(64, F32), "cb": sb(64, F32),
+    "l0": sb(64, F32), "lost": sb(192, BF), "nsg": sb(256, BF), "tw": sb(336, F32), "ga": sb(192, F32), "gb": sb(192, F32),
+    "tr": sb(544, F32), "g1": sb(64, F32), "val": sb(64, F32), "loff": sb(64, U16), "ds": sb(64, F32),
+    "d4": sb(64, U16), "dl": sb(16, U16), "drow": sb(256, F32),
+    "lsc": sb(256, BF), "lqv": sb(64, F32), "lr": sb(64, F32), "b4": sb(64, U16),
     "ma": sb(1024, BF), "mb": sb(1024, BF), "mm": sb(1024, BF), "rz": sb(1024, F32),
-    "junk": sb(24 * 256, BF), "hs": sb(8, F32), "hh": sb(8, F32), "rs": sb(512, BF), "rt": sb(512, BF),
-    "nk": sb(16, F32), "key": sb(256, F32), "rk": sb(16, F32), "roff": sb(16, U16),
-    "hw": sb(256, F32), "h4": sb(64, F32), "dx": sb(1024, BF), "ys": sb(C, F32),
-    "pz": ("psum", [128, 2048], F32), "pd": ("psum", [128, 2048], F32),
+    "junk": sb(14 * 256, BF), "hs": sb(8, F32), "hh": sb(8, F32), "lo": sb(8, F32), "mu": sb(16, U16),
+    "mrow": sb(256, BF), "gq": sb(1, F32), "gu": sb(2, U16), "tau": sb(1, F32), "kr": sb(16, F32), "kk": sb(1, F32),
+    "over": sb(256, BF), "from": sb(256, BF), "bnd": sb(256, BF), "cum": sb(256, BF), "sq": sb(4, F32), "hu": sb(4, U16),
+    "kc": sb(64, F32), "ko": sb(64, F32), "wr": sb(64, F32), "above": sb(256, BF), "rq": sb(256, BF), "ru": sb(4, U16),
+    "hw": sb(64, F32), "h4": sb(64, F32), "dx": sb(1024, BF), "ys": sb(C, F32),
+    "pz": ("psum", [128, 2048], F32), "pc": ("psum", [128, 1024], F32), "pd": ("psum", [128, 1024], F32),
 }
-NPOOL = {"c": 84, "h": 30, "s": 12}
+NPOOL = {"c": 100, "h": 30, "s": 12}
 SEMAPHORES = (["sent"] + ["arq%d" % t for t in range(R)] + ["arh%d" % t for t in range(R)]
               + ["%s%d" % (k, i) for k in ("c", "h", "s") for i in range(NPOOL[k])])
 
-PARAMS = {"rank_v": (1, 0, 3), "dx_v": (0, 0, 0), "hist_v": (0, 0, 2), "a3_s": (0, 1, 0), "lost_s": (2, 4, 2)}
-COSTS = {"cyc": 1.04, "gather": 1.56, "scatter": 3.8, "wake": 100.0, "dma": 2000.0, "remote": 2200.0, "pe": 0.7,
-         "tt16": 1.0, "act": 0.0, "issue": 60.0}
-ORDER = [
-    0,1,8,36,2,4,50,3,10,66,12,25,16,18,14,11,9,15,60,13,17,26,20,19,41,39,21,67,22,68,24,40,23,51,55,69,27,44,42,43,61,45,72,71,53,46,
-    54,62,52,78,28,70,58,47,59,56,49,48,29,82,57,30,31,65,5,37,181,6,7,38,94,32,33,95,83,96,100,97,63,101,64,98,102,99,175,103,126,104,
-    127,178,74,108,107,106,172,109,105,76,113,90,112,73,91,111,92,114,93,110,79,116,75,115,128,88,117,77,35,129,118,133,119,131,132,138,
-    120,130,121,179,134,173,137,141,124,182,135,200,176,140,139,180,136,87,142,207,125,144,143,122,208,145,123,147,146,148,183,157,161,
-    177,151,149,163,174,154,155,80,184,153,85,162,188,34,185,156,150,191,189,194,86,84,203,186,190,201,192,205,158,187,152,195,193,159,
-    164,196,160,165,166,197,81,204,167,198,214,168,199,215,216,217,218,219,202,206,169,220,170,221,171,223,222,246,224,247,227,228,248,
-    229,249,232,233,231,230,234,225,226,236,209,235,210,237,299,253,238,252,240,211,290,251,239,212,241,250,213,242,293,244,245,243,291,
-    296,294,254,300,261,297,260,256,295,318,257,321,325,301,255,319,323,298,259,258,292,322,262,326,302,320,263,264,306,265,303,307,312,
-    266,267,304,309,313,268,310,308,278,280,305,281,284,314,279,270,311,282,277,315,275,89,316,332,274,317,333,334,338,335,339,336,341,
-    337,283,340,271,342,345,276,346,269,347,344,273,351,350,272,343,348,324,352,349,353,354,285,355,356,357,286,385,387,383,374,287,382,
-    375,288,388,289,376,358,377,386,390,380,389,384,391,378,359,381,363,360,392,362,394,393,361,395,379,397,396,398,327,328,411,408,399,
-    430,401,329,415,403,330,331,402,427,404,424,400,431,433,428,406,425,410,417,434,450,409,455,457,413,429,451,405,453,432,412,416,435,
-    407,414,426,456,418,458,436,452,419,364,437,420,443,438,446,444,440,447,441,421,365,422,439,423,454,372,445,367,366,371,368,370,373,
-    369,448,442,449,459,460,462,465,468,466,467,469,463,461,464,470,472,474,473,476,475,471,477,478]
+PARAMS = {"cuts": (2, 2, 2), "layer": (2, 2, 2), "add": ("gg", "kg", "gk"), "relu_v": (0, 0, 0), "pieces": (2, 2, 2),
+          "mrow_v": (0, 0, 1), "g_plain": (0, 0, 0), "hist_v": (0, 0, 2), "seek_v": (0, 0, 0), "dx_v": (0, 0, 0),
+          "ga3_v": (0, 0, 0),
+          "scalar": ("cs16", "gt1", "gt2", "d64", "ra", "sup0", "sup1", "wr", "ys0", "own2", "own3", "tie", "cso", "cs4",
+                     "c1", "sbi", "jm", "o1", "o2", "ni"),
+          "passes": 2500, "shake": 1500.0}
+COSTS = {"cyc": 0.83, "gather": 1.56, "scatter": 3.8, "wake": 180.0, "dma": 1150.0, "gdma": 1450.0, "remote": 1150.0,
+         "pe": 0.7, "issue": 60.0, "gissue": 300.0, "rissue": 150.0, "kb": 4.0, "least": 64.0, "least_a": 224.0}
 
 
 def r(name, a=0, b=None, s=1, p=None):
@@ -72,7 +68,7 @@ def r(name, a=0, b=None, s=1, p=None):
 
 def bits(ref):
     name, a, b, s, p = ref
-    if name in ("pz", "pd"):
+    if name in BANKS:
         a, b, s = a // 512 * 512, (b + 511) // 512 * 512, 1
     if s == 1:
         return (1 << b) - (1 << a)
@@ -101,7 +97,7 @@ def program(par, cm):
                     "hold": cost if hold is None else hold, "grp": grp, "cls": cls, "after": after, "tag": tag})
 
     def plain(out, ins):
-        return max(64.0, width(out) * (0.5 if narrow(out, *ins) else 1.0)) * cyc
+        return max(cm["least"], width(out) * (0.5 if narrow(out, *ins) else 1.0)) * cyc
 
     def gath(out):
         return 50 + width(out) * cm["gather"] * cyc
@@ -109,47 +105,62 @@ def program(par, cm):
     def memset(out, v, **k):
         op("v", "memset", (out, v), [], [out], plain(out, []), **k)
 
-    def copy(out, in_, **k):
-        op("v", "copy", (out, in_), [in_], [out], plain(out, [in_]), **k)
+    def copy(out, in_, off=None, **k):
+        op("v", "copy", (out, in_, off), [in_, off], [out], gath(out) if off else plain(out, [in_]), **k)
 
-    def ts(out, in0, s1, s2, o0, o1=None, **k):
-        op("v", "ts", (out, in0, s1, s2, o0, o1), [in0, s1, s2], [out], plain(out, [in0]), **k)
+    def ts(out, in0, s1, s2, o0, o1=None, off=None, **k):
+        op("v", "ts", (out, in0, s1, s2, o0, o1, off), [in0, s1, s2, off], [out],
+           gath(out) if off else plain(out, [in0]), **k)
 
-    def tt(out, in0, in1, o, **k):
-        f = cm["tt16"] if narrow(out, in0, in1) else 1.0
-        op("v", "tt", (out, in0, in1, o), [in0, in1], [out], max(64.0, 2 * f * width(out)) * cyc, **k)
+    def tt(out, in0, in1, o, off=None, **k):
+        c = gath(out) if off else max(cm["least"], (1 if in0[0] in BANKS else 2) * width(out)) * cyc
+        op("v", "tt", (out, in0, in1, o, off), [in0, in1, off], [out], c, **k)
 
-    def ttg(out, win, off, in1, o, **k):
-        op("v", "ttg", (out, win, off, in1, o), [win, off, in1], [out], gath(out), **k)
-
-    def gather(out, win, off, **k):
-        op("v", "gather", (out, win, off), [win, off], [out], gath(out), **k)
-
-    def scan(out, d0, d1, o0, o1, **k):
-        op("v", "scan", (out, d0, d1, o0, o1), [d0, d1], [out], plain(out, [d0, d1]), **k)
+    def scan(out, d0, d1, o0, o1, init=0.0, **k):
+        op("v", "scan", (out, d0, d1, init, o0, o1), [d0, d1, init], [out], plain(out, [d0, d1]), **k)
 
     def turn(out, in_, **k):
         op("v", "turn", (out, in_), [in_], [out], plain(out, [in_]), **k)
+
+    def reduce(out, in_, o, **k):
+        op("v", "reduce", (out, in_, o), [in_], [out], max(cm["least"], width(in_)) * cyc, **k)
 
     def quant(q, s, in_, **k):
         op("v", "quant", (q, s, in_), [in_], [q, s], (12 + 0.22 * width(in_)) * cyc / 0.83, **k)
 
     def act(out, in_, f, scale=1.0, bias=None, acc=None, off=None, **k):
-        c = (65 + width(out) * cm["gather"] * cyc) if off else max(64.0, width(out)) * cyc + cm["act"]
+        c = (65 + width(out) * cm["gather"] * cyc) if off else max(cm["least_a"], width(out)) * cyc
         op("a", "act", (out, in_, f, scale, bias, acc, off), [in_, scale, bias, off],
            [out] + ([acc] if acc else []), c + (20 if acc else 0), **k)
+
+    def line(name, out, in_, scale=1.0, bias=None, off=None, **k):
+        if name in par["scalar"]:
+            act(out, in_, F.Copy if bias is None else F.Identity, scale=scale, bias=bias, off=off, **k)
+        elif bias is None and scale == 1.0:
+            copy(out, in_, off=off, **k)
+        elif bias is None:
+            ts(out, in_, scale, None, A.mult, off=off, **k)
+        elif scale == 1.0:
+            ts(out, in_, bias, None, A.add, off=off, **k)
+        else:
+            ts(out, in_, scale, bias, A.mult, A.add, off=off, **k)
 
     def mm(out, lq, ls, rq, rs, **k):
         op("t", "mm", (out, lq, ls, rq, rs), [lq, ls, rq, rs], [out], (width(out) + 16) * cm["pe"], **k)
 
     def iota(out, pat, base, mult=0, **k):
-        op("g", "iota", (out, pat, base, mult), [], [out], 130 + 2 * width(out) * cyc, **k)
+        op("g", "iota", (out, pat, base, mult), [], [out], (130 + 1.66 * width(out)) * cyc / 0.83, **k)
 
-    def dma(q, out, in_, kb, **k):
-        op(q, "dma", (out, in_), [in_], [out], cm["dma"] + kb * 5, hold=cm["issue"], cls="s" if q == "g" else "h", **k)
+    def select(out, pat, cmp, fill, base, mult, **k):
+        op("g", "select", (out, pat, cmp, fill, base, mult), [out], [out], (170 + 1.66 * width(out)) * cyc / 0.83, **k)
+
+    def dma(q, out, in_, kb, add=False, **k):
+        op(q, "dma", (out, in_, add), [in_] + ([out] if add else []), [out],
+           cm["gdma" if q == "g" else "dma"] + kb * cm["kb"], hold=cm["gissue" if q == "g" else "issue"],
+           cls="s" if q == "g" else "h", **k)
 
     def send(out, in_, sem, kb, tag):
-        op("g", "send", (out, in_, sem), [in_], [], cm["remote"] + kb * 8, hold=2 * cm["issue"], cls="r", tag=tag)
+        op("g", "send", (out, in_, sem), [in_], [], cm["remote"] + 1.5 * kb * cm["kb"], hold=cm["rissue"], cls="r", tag=tag)
 
     def arrive(sem, n, refs, tags):
         op(None, "arrive", (sem, n), [], refs, 0, cls="r", after=tags)
@@ -157,223 +168,277 @@ def program(par, cm):
     def col(name, j):
         return r(name, j, j + 1)
 
+    def xr(t, a, b, s=1):
+        return r("xs", XW * t + a, XW * t + b, s)
+
+    def quant_x(t, a, b):
+        quant(r("qx", C * t + a, C * t + b), r("sx", C * t + a, C * t + b), xr(t, X0 + 4 * a, X0 + 4 * b))
+
+    def qs(t, a, b):
+        return r("qx", C * t + a, C * t + b), r("sx", C * t + a, C * t + b)
+
+    def quant_nodes(t):
+        n = P // par["cuts"][t]
+        for a in range(E, C, n):
+            quant_x(t, a, a + n)
+
     dma("a", r("ub"), ("u", 0, 512, 1, None), 128)
-    dma("y", r("xb", XN, XEND), ("x", 4 * E, 4 * C, 1, None), 256, tag="x")
+    dma("y", xr(0, XN, XN + 512), ("x", 4 * E, 4 * E + 512, 1, None), 128, tag="x")
+    dma("y", xr(0, XN + 512, XW), ("x", 4 * E + 512, 4 * C, 1, None), 128, tag="x")
     dma("a", r("pab", 0, 16), ("pa", 0, 16, 1, None), 8, grp="pab")
     dma("a", r("pab", 16, 32), ("pb", 0, 16, 1, None), 8, grp="pab")
-    dma("y", r("xb", X0, XN), ("x", 0, 4 * E, 1, None), 64)
-    dma("y", r("wq"), ("wc", 0, 2048, 1, None), 256, grp="w", after=["x"])
-    dma("y", r("wp"), ("ws", 0, 512, 1, None), 64, grp="w", after=["x"])
+    dma("y", xr(0, X0, XN), ("x", 0, 4 * E, 1, None), 64)
+    dma("g", r("wq"), ("wc", 0, 2048, 1, None), 256, after=["x"])
+    dma("y", r("wp"), ("ws", 0, 512, 1, None), 64, after=["x"])
     dma("y", r("vb"), ("v", 0, 512, 1, None), 128, after=["x"])
 
     iota(col("pi", 0), [[0, 1]], 0, 1)
-    iota(col("pi", 1), [[0, 1]], 0, 16)
-    iota(col("pi", 2), [[0, 1]], 0, 17)
+    iota(r("k64"), [[1, 64]], 0)
     for j, m in enumerate((3, 4)):
         ts(col("pj", j), col("pi", 0), m, None, A.bitwise_and, grp="pj")
     copy(r("pf", 0, 2), r("pj", 0, 2))
-    for j, m in ((2, 15), (3, 31)):
+    for j, m in ((2, 15), (3, 16), (4, 7)):
         ts(col("pj", j), col("pi", 0), m, None, A.bitwise_and, grp="pk")
-    ts(col("pj", 4), col("pi", 0), 2, 3, A.logical_shift_right, A.bitwise_and, grp="pk")
-    ts(col("pj", 5), col("pi", 1), 255, None, A.bitwise_and, grp="pk")
-    ts(col("pj", 6), col("pi", 2), 4, 1, A.logical_shift_right, A.bitwise_and, grp="pk")
-    copy(r("pf", 2, 7), r("pj", 2, 7))
-    lev, flag, pi16, p32, sel, i16, par2 = [col("pf", j) for j in range(7)]
-    slope, tbase, off16, jm, cwb = [col("ps", j) for j in range(5)]
-    act(slope, flag, F.Identity, scale=-1025.0, bias=2052.0)
-    act(tbase, par2, F.Identity, scale=272.0, bias=i16)
-    act(off16, pi16, F.Identity, scale=-4.0, bias=60.0)
-    act(jm, sel, F.Identity, scale=2048.0, bias=lev)
-    act(cwb, pi16, F.Identity, scale=1.0 / 256, bias=-1.0 / 512)
+    ts(col("pj", 5), col("pi", 0), 2, 3, A.logical_shift_right, A.bitwise_and, grp="pk")
+    copy(r("pf", 2, 6), r("pj", 2, 6))
+    lev, flag, pi16, p16, p8, sel = [col("pf", j) for j in range(6)]
+    slope, odd, tb1, tbase, jm, i4, b15, o1, o2, ni = [col("ps", j) for j in range(10)]
+    line("slope", slope, flag, -1025.0, 2052.0)
+    ts(odd, flag, 4.0, p16, A.mult, A.not_equal)
+    line("tb1", tb1, sel, 16.0, lev)
+    line("tbase", tbase, odd, 272.0, tb1)
+    line("jm", jm, sel, 2048.0, lev)
+    line("i4", i4, pi16, 4.0)
+    line("b15", b15, p8, 16.0, 15.0)
+    line("o1", o1, pi16, -4.0, 61.0)
+    line("o2", o2, pi16, -512.0, 7680.0)
+    line("ni", ni, pi16, -1.0, -0.5)
 
-    iota(r("k64"), [[1, 64]], 0)
-    for t in range(R):
-        ts(r("ul", 8 * t, 8 * t + 8), r("k64", 0, 8), 16.0, float(t), A.mult, A.add)
+    iota(r("ki", 0, 24), [[1, 3], [16, 8]], 0)
+    iota(r("ki", 24, 32), [[4, 2], [64, 4]], 0)
+    iota(r("ki", 32, 36), [[8, 2], [0, 2]], 0)
+    copy(r("ul"), r("ki", 0, 24))
+    trl, trh, lofl, cl, bl = [r("kl", 4 * j, 4 * j + 4) for j in range(5)]
+    ts(r("kl", 0, 8), r("ki", 24, 32), tbase, None, A.add)
+    ts(lofl, r("k64", 0, 4), i4, None, A.add)
+    ts(cl, r("ki", 32, 36), p8, None, A.add)
+    ts(bl, r("ki", 32, 36), 16.0, b15, A.mult, A.add)
+
     quant(r("qu"), r("su"), r("ub"))
+    for a, b in ((0, 1), (1, R)):
+        o, q = r("ul", 8 * a, 8 * b), r("qup", 128 * a, 128 * b)
+        op("v", "pickq", (q, r("qu"), o), [r("qu"), o], [q], gath(q), grp="pick%d" % a)
+        line("sup%d" % a, r("sup", 128 * a, 128 * b), r("su"), off=o, grp="pick%d" % a)
     for t in range(R):
-        o = r("ul", 8 * t, 8 * t + 8)
-        op("v", "pickq", (r("qup", 128 * t, 128 * t + 128), r("qu"), o), [r("qu"), o],
-           [r("qup", 128 * t, 128 * t + 128)], gath(r("qu")), grp="pick%d" % t)
-        act(r("sup", 128 * t, 128 * t + 128), r("su"), F.Copy, off=o, grp="pick%d" % t)
-    memset(r("xb", 0, X0), 0.0)
-    quant(r("qn", 0, 256), r("sn", 0, 256), r("xb", XN, XEND))
-    quant(r("qe", 0, 128), r("se", 0, 128), r("xb", X0, X0 + 512))
+        iota(xr(t, 0, X0), [[0, X0]], 0)
+    quant_nodes(0)
 
     ts(r("sf"), r("k64", 0, 4), lev, slope, A.is_equal, A.mult, grp="sf")
     ts(r("cf"), r("k64", 0, 4), lev, BASE, A.is_equal, A.mult, grp="sf")
     ts(r("thr"), r("k64", 1, 5), lev, 1e29, A.is_equal, A.mult)
-    ts(r("th2"), r("k64", 1, 5), lev, 2 * LOST, A.is_equal, A.mult)
-    act(r("tw", 0, 64), r("k64"), F.Identity, scale=col("sf", 0), bias=col("cf", 0))
+    line("tw", r("tw", 0, 64), r("k64"), col("sf", 0), col("cf", 0))
     for l in range(1, 4):
-        act(r("own", 64 * l - 64, 64 * l), r("k64"), F.Identity, scale=col("sf", l), bias=col("cf", l))
+        line("own%d" % l, r("own", 64 * l - 64, 64 * l), r("k64"), col("sf", l), col("cf", l))
     copy(r("abl"), r("pab"))
-    ttg(r("oab", 0, 64), r("tw", 0, 64), r("abl", 0, 4), r("own", 0, 64), A.max)
-    act(r("oab", 64, 128), r("tw", 0, 64), F.Copy, off=r("abl", 16, 20))
-    memset(r("tw", 320, 336), 0.0)
-    iota(r("cj"), [[256, 4], [0, 16]], int(4 - 2 * BASE))
-    for j in range(1, 4):
-        memset(r("cj", 20 * j - 4, 20 * j), -8 * BASE, grp="cj")
-    ts(r("trl"), r("k64", 0, 8), tbase, None, A.add)
-    for t in range(4):
-        ts(r("a4", 16 * t, 16 * t + 16), r("pab", 0, 16), 4.0, float(X0 + t), A.mult, A.add, grp="a4")
+    tt(r("oa"), r("tw", 0, 64), r("own", 0, 64), A.max, off=r("abl", 0, 4))
+    line("ra", r("ra"), r("tw", 0, 64), off=r("abl", 0, 4))
+    tt(r("eq0"), r("tw", 0, 64), r("ra"), A.is_equal, off=r("abl", 16, 20))
+    line("thr0", r("thr0"), r("eq0"), 1e29)
+    iota(r("tw", 320, 336), [[0, 16]], 0)
+    iota(r("cj"), [[0, 16], [256, 4]], int(4 - 2 * BASE))
+    select(r("cj"), [[-1, 4], [0, 4], [1, 4]], A.not_equal, -8 * BASE, -1, 0)
+    iota(r("y4"), [[0, 16], [2048, 4]], 0)
 
+    iota(r("econ"), [[0, 2], [1, 4], [0, 8]], X0)
+    ts(r("a4x"), r("pab", 0, 16), 4.0, None, A.mult)
+    tt(r("dd"), r("pab", 16, 32), r("pab", 0, 16), A.subtract)
+    tt(r("a4f"), r("a4x"), r("econ"), A.add, off=cl)
+    copy(r("a4"), r("a4f"))
+    line("d64", r("d64"), r("dd"), 2.0, off=cl)
+    line("c1", r("c1"), r("d64"), o1)
+    tt(r("cb"), r("c1"), r("a4f"), A.add)
     iota(r("y16"), [[0, 16], [1, 16]], 0)
     ts(r("e1"), r("y16"), pi16, 132.0, A.not_equal, A.mult)
-    act(r("cs16"), r("e1"), F.Identity, bias=-128.0)
-    tt(r("dd"), r("pab", 16, 32), r("pab", 0, 16), A.subtract)
-    act(r("dab"), r("dd"), F.Identity, scale=4.0)
-    ts(r("cb"), r("pab", 16, 32), 4.0, float(X0), A.mult, A.add)
+    line("cs16", r("cs16"), r("e1"), 1.0, -128.0)
 
-    memset(r("gt", 0, 17), 0.0)
-    ts(r("gt", 17, 49), r("k64", 0, 32), pi16, None, A.is_equal, grp="gt")
-    ts(r("gt", 49, 81), r("k64", 0, 32), pi16, 4096.0, A.is_equal, A.mult, grp="gt")
-    for j in range(1, 4):
-        act(r("gt", 17 + 64 * j, 81 + 64 * j), r("gt", 17, 81), F.Copy, grp="gt2")
-    iota(r("keep"), [[0, 16], [512, 32]], 0)
-    act(r("rb"), r("keep"), F.Copy, scale=0.0)
-    iota(r("wv"), [[128, 2], [256, 4], [4, 32]], 0)
-    act(r("tie"), r("wv"), F.Identity, scale=-1.0 / 1024, bias=255.0 / 256)
-    iota(r("cwi"), [[32, 2], [64, 4], [16, 2]], -255)
-    act(r("cw"), r("cwi"), F.Identity, scale=1.0 / 256, bias=cwb)
-    ts(r("kl"), r("k64", 0, 16), 32.0, p32, A.mult, A.add)
-    iota(r("y4"), [[0, 16], [1, 4]], 0)
-    ts(r("f1"), r("y4"), sel, 10240.0, A.not_equal, A.mult)
-    act(r("cs4"), r("f1"), F.Identity, bias=-8192.0)
+    iota(r("gt", 0, 112), [[0, 112]], 0)
+    ts(r("gt", 33, 49), r("k64", 0, 16), pi16, None, A.is_equal, grp="gt")
+    ts(r("gt", 49, 65), r("k64", 0, 16), pi16, 4096.0, A.is_equal, A.mult, grp="gt")
+    line("gt1", r("gt", 97, 161), r("gt", 33, 97))
+    line("gt2", r("gt", 161, 289), r("gt", 33, 161))
+    iota(r("mtab", 0, 257), [[1, 257]], 0)
+    iota(r("ttab", 0, 64), [[0, 64]], 1)
+    iota(r("ttab", 64, 257), [[0, 193]], 33)
+    iota(r("ktab", 0, 64), [[-1, 64]], 64)
+    iota(r("ktab", 64, 257), [[0, 193]], 64)
+    line("sbi", r("sbi"), r("k64", 0, 64, 16), -1.0, ni)
+    if any(par["seek_v"]):
+        line("sj", r("sj"), r("sbi"), -1.0)
+    line("tie", r("tie"), r("k64"), -1.0 / 64, 63.0 / 64)
+    line("cso", r("cso"), r("e1", 0, 64), 128.0, -16384.0)
+    iota(r("keep"), [[0, 4], [64, 64]], 0)
+    ts(r("f1"), r("y4"), lev, jm, A.add, A.not_equal)
+    line("cs4", r("cs4"), r("f1"), 10240.0, -8192.0)
 
     iota(r("ebig"), [[0, 528]], 1)
-    op("g", "strip", (r("ebig"),), [r("ebig")], [r("ebig")], 170 + 2 * 528 * cyc)
+    select(r("ebig"), [[1, 528]], A.is_equal, 0.0, -3, -4)
     for b in range(4):
         quant(r("qc", 128 * b, 128 * b + 128), r("sc", 128 * b, 128 * b + 128), r("ebig", 3 - b, 515 - b))
-    iota(r("itab", 0, 257), [[1, 257]], -1)
     quant(r("qv"), r("sv"), r("vb"))
-
-    def send_nodes(t):
-        send(r("lq", 256 * t + 64, 256 * t + 256), r("qn", 256 * t, 256 * t + 192), "arq%d" % t, 96, "nq%d" % t)
-        send(r("ls", 256 * t + 64, 256 * t + 256), r("sn", 256 * t, 256 * t + 192), "arq%d" % t, 24, "ns%d" % t)
-
-    def send_entries(t):
-        send(r("lq", 256 * t, 256 * t + 64), r("qe", 128 * t, 128 * t + 64), "arq%d" % t, 32, "eq%d" % t)
-        send(r("ls", 256 * t, 256 * t + 64), r("se", 128 * t, 128 * t + 64), "arq%d" % t, 8, "es%d" % t)
-
-    send_nodes(0)
-    send_entries(0)
-    xw = r("xb")
 
     for t in range(R):
         g_ = lambda s: "%s_%d" % (s, t)
-        qn, sn = r("qn", 256 * t, 256 * t + 256), r("sn", 256 * t, 256 * t + 256)
-        mm(r("pz", 0, 256), r("qup", 128 * t, 128 * t + 128), r("sup", 128 * t, 128 * t + 128), qn, sn)
-        for k in range(4 - par["lost_s"][t]):
-            op("v", "ts", (r("lost", 64 * k, 64 * k + 64), r("pz", 64 * k, 64 * k + 64), col("thr", k), LOST, A.is_lt, A.mult),
-               [col("thr", k), r("pz", 0, 256)], [r("lost", 64 * k, 64 * k + 64)], 64 * cyc)
-        act(r("sg"), r("pz", 0, 256), F.Sign)
-        for k in range(4 - par["lost_s"][t], 4):
-            act(r("lost", 64 * k, 64 * k + 64), r("sg", 64 * k, 64 * k + 64), F.Relu, scale=-LOST, bias=col("th2", k))
-        tt(r("gb", 0, 64), r("oab", 64, 128), r("lost", 0, 64), A.max)
-        tt(r("tw", 64, 128), r("oab", 0, 64), r("gb", 0, 64), A.min)
+        up = r("qup", 128 * t, 128 * t + 128), r("sup", 128 * t, 128 * t + 128)
+        n = P // par["cuts"][t]
+        score = lambda a, b: r("pc", a // n * 512 + a % n, a // n * 512 + a % n + b - a)
+        for a in range(0, P, n):
+            mm(score(a, a + n), *up, *qs(t, E + a, E + a + n))
+            for k in range(a // 64, (a + n) // 64):
+                if k:
+                    ts(r("lost", 64 * k - 64, 64 * k), score(64 * k, 64 * k + 64), col("thr", k), LOST, A.is_lt, A.mult)
+                else:
+                    tt(r("l0"), score(0, 64), r("thr0"), A.is_lt)
+            act(r("nsg", a, a + n), score(a, a + n), F.Sign, scale=-1.0, bias=-TINY)
+        quant_x(t, 0, 128)
+        send(r("lq", 256 * t, 256 * t + 256), r("qx", C * t, C * t + 256), "arq%d" % t, 128, "q%d" % t)
+        send(r("ls", 256 * t, 256 * t + 256), r("sx", C * t, C * t + 256), "arq%d" % t, 32, "q%d" % t)
+        tt(r("tw", 64, 128), r("oa"), r("l0"), A.mult)
         for k in range(1, 4):
-            win, a, b = r("tw", 0, 64 + 64 * k), 64 * k, 64 * k + 64
+            win, a, b = r("tw", 0, 64 + 64 * k), 64 * k - 64, 64 * k
+            la, lb = r("abl", 4 * k, 4 * k + 4), r("abl", 16 + 4 * k, 20 + 4 * k)
             if k < 3:
-                ttg(r("ga", a, b), win, r("abl", 4 * k, 4 * k + 4), r("own", a, b), A.max, grp=g_("ab%d" % k))
-            elif par["a3_s"][t]:
-                act(r("ga", a, b), win, F.Copy, off=r("abl", 4 * k, 4 * k + 4), grp=g_("ab%d" % k))
+                tt(r("ga", a, b), win, r("own", a + 64, b + 64), A.max, off=la)
+            elif par["ga3_v"][t]:
+                copy(r("ga", a, b), win, off=la)
             else:
-                gather(r("ga", a, b), win, r("abl", 4 * k, 4 * k + 4), grp=g_("ab%d" % k))
-            ttg(r("gb", a, b), win, r("abl", 16 + 4 * k, 20 + 4 * k), r("lost", a, b), A.max, grp=g_("ab%d" % k))
-            tt(r("tw", 64 + a, 64 + b), r("ga", a, b), r("gb", a, b), A.min)
+                act(r("ga", a, b), win, F.Copy, off=la)
+            tt(r("gb", a, b), win, r("lost", a, b), A.max, off=lb)
+            tt(r("tw", 128 + a, 128 + b), r("ga", a, b), r("gb", a, b), A.min)
             a, b, e = ((0, 128, 128), (128, 192, 192), (192, 256, 288))[k - 1]
-            turn(r("tr", a, b), r("tw", 64 + a, 64 + b), grp=g_("tr"))
-            turn(r("tr", 256 + a, 256 + e), r("tw", 48 + a, 48 + e), grp=g_("tr"))
-        ttg(r("g1"), r("tr"), r("trl", 4, 8), r("cj"), A.add)
-        ttg(r("val"), r("tr"), r("trl", 0, 4), r("g1"), A.add)
-        ts(r("loff"), r("val"), 0.25, 0.0, A.mult, A.max)
-        tt(r("dm1"), r("val", 0, 32), r("val", 32, 64), A.max)
-        tt(r("dm2"), r("dm1", 0, 16), r("dm1", 16, 32), A.max)
+            turn(r("tr", a, b), r("tw", 64 + a, 64 + b))
+            turn(r("tr", 256 + a, 256 + e), r("tw", 48 + a, 48 + e))
+        tt(r("g1"), r("tr"), r("cj"), A.add, off=trh)
+        tt(r("val"), r("tr"), r("g1"), A.add, off=trl)
+        scan(r("ds"), r("y4"), r("val"), A.min, A.max)
         for e in range(4):
-            ts(r("d4", 16 * e, 16 * e + 16), r("dm2"), float(X0 - 4 + e), 0.0, A.add, A.max)
+            ts(r("d4", 16 * e, 16 * e + 16), r("ds", 3, 64, 4), float(X0 - 4 + e), None, A.add)
+        ts(r("loff"), r("val"), 0.25, None, A.mult, off=lofl)
         if t == R - 1:
-            ts(r("dl"), r("dm2"), 0.25, 0.0, A.mult, A.max)
-            act(r("drow"), r("itab", 0, 257), F.Copy, off=r("dl"))
+            ts(r("dl"), r("ds", 3, 64, 4), 0.25, None, A.mult)
+            act(r("drow"), r("mtab", 0, 257), F.Identity, bias=-1.0, off=r("dl"))
             for k in range(8):
                 dma("y", ("od", 0, 256, 1, (k, k + 1)), r("drow", p=(16 * k, 16 * k + 1)), 1, grp="out_od", tag="end")
-        scan(r("lsc"), r("cs16"), r("sg"), A.add, A.max)
-        ts(r("lu"), r("lsc", 15, 256, 16), off16, 0.0, A.subtract, A.min)
-        tt(r("lqv"), r("lu"), r("dab"), A.mult)
-        tt(r("lr"), r("lqv"), r("cb"), A.add)
-        for e in range(4):
-            ts(r("b4", 16 * e, 16 * e + 16), r("lr"), float(e), None, A.add)
+        scan(r("lsc"), r("cs16"), r("nsg"), A.add, A.max)
+        tt(r("lqv"), r("lsc"), r("d64"), A.mult, off=bl)
+        tt(r("lr"), r("cb"), r("lqv"), A.subtract)
+        copy(r("b4"), r("lr"))
         for j in range(4):
             for q in range(2):
                 h, n = 2 * j + q, 256 - 64 * j
-                out, win, off = r("junk", 256 * h, 256 * h + n), r("gt", 16 - 16 * q, 273 - 16 * q), r("loff", 20 * j, 16 * j + 16)
+                out, win, off = r("junk", 256 * h, 256 * h + n), r("gt", 32 - 32 * q, 289 - 32 * q), r("loff", 20 * j, 16 * j + 16)
                 if h >= 8 - par["hist_v"][t]:
-                    gather(out, win, off)
-                    op("v", "sum", (col("hs", h), out), [out], [col("hs", h)], max(64, n) * cyc, grp=g_("hist"))
+                    copy(out, win, off=off)
+                    reduce(col("hs", h), out, A.add, grp=g_("hist"))
                 else:
                     act(out, win, F.Identity, acc=col("hs", h), off=off, grp=g_("hist"))
         ts(r("hh"), r("hs"), MAGIC, MAGIC, A.add, A.subtract)
-        tt(r("rb", 0, 256, 32), r("hs"), r("hh"), A.subtract, grp=g_("rb"))
-        ts(r("rb", 256, 512, 32), r("hh"), 2.0 ** -12, None, A.mult, grp=g_("rb"))
-        scan(r("rs"), r("keep"), r("rb"), A.min, A.add)
-        tt(r("nk"), r("cw"), r("rb", 0, 512, 32), A.subtract)
-        turn(r("rt"), r("rs"))
-        ttg(r("key"), r("rt"), r("kl"), r("tie"), A.add)
-        nv = par["rank_v"][t]
-        for c in range(16):
-            out = r("junk", 256 * (8 + c), 256 * (9 + c))
+        ts(r("mu", 1, 16, 2), r("hs"), 2.0 ** -12, None, A.mult)
+        tt(r("lo"), r("hs"), r("hh"), A.subtract)
+        copy(r("mu", 0, 16, 2), r("lo"))
+        mtab = r("mtab", 0, 257)
+        if par["mrow_v"][t]:
+            copy(r("mrow"), mtab, off=r("mu"))
+        else:
+            act(r("mrow"), mtab, F.Copy, off=r("mu"))
+        if par["g_plain"][t]:
+            act(r("junk", 2048, 2304), r("mrow"), F.Sign, bias=col("sbi", 0), acc=r("gq"))
+        else:
+            act(r("junk", 2048, 2304), mtab, F.Sign, bias=col("sbi", 0), acc=r("gq"), off=r("mu"))
+        ts(col("gu", 0), r("gq"), 0.5, 128.0, A.mult, A.add)
+        act(r("junk", 2304, 2320), r("ttab", 0, 257), F.Identity, scale=1.0 / 32, acc=r("tau"), off=col("gu", 0))
+        copy(r("kr"), r("ktab", 0, 257), off=col("gu", 0))
+        reduce(r("kk"), r("kr"), A.min)
+        ts(r("over"), r("mrow"), r("tau"), None, A.is_gt)
+        ts(r("from"), r("mrow"), 1.0, r("tau"), A.add, A.is_gt)
+        scan(r("bnd"), r("over"), r("over"), A.add, A.max, init=r("kk"))
+        scan(r("cum"), r("from"), r("bnd"), A.add, A.min)
+        nv = par["seek_v"][t]
+        for c in range(4):
+            out = r("junk", 2560 + 256 * c, 2816 + 256 * c)
             if c < nv:
-                op("v", "ts", (out, r("key"), col("nk", c), 0.0, A.add, A.is_gt), [r("key"), col("nk", c)], [out], 256 * cyc)
-                op("v", "sum", (col("rk", c), out), [out], [col("rk", c)], 256 * cyc, grp=g_("rankv"))
+                ts(out, r("cum"), col("sj", c), None, A.is_lt)
+                reduce(col("sq", c), out, A.add, grp=g_("seek"))
             else:
-                act(out, r("key"), F.Sign, bias=col("nk", c), acc=col("rk", c), grp=g_("ranka"))
+                act(out, r("cum"), F.Sign, bias=col("sbi", c), acc=col("sq", c), grp=g_("seek"))
         if nv:
-            copy(r("roff", 0, nv), r("rk", 0, nv), grp=g_("roff"))
-        ts(r("roff", nv, 16), r("rk", nv, 16), 256.0, 0.5, A.add, A.mult, grp=g_("roff"))
-        op("v", "scatter", (r("hw"), r("roff"), r("wv")), [r("roff"), r("wv")], [r("hw")], 50 + 256 * cm["scatter"] * cyc)
-        scan(r("h4"), r("cs4"), r("hw", 0, 64), A.add, A.max)
+            copy(r("hu", 0, nv), r("sq", 0, nv), grp=g_("hu"))
+        ts(r("hu", nv, 4), r("sq", nv, 4), -0.5, 128.0, A.mult, A.add, grp=g_("hu"))
+        tt(r("kc"), r("mrow"), r("tie"), A.add, off=r("hu"))
+        line("wr", r("wr"), mtab, 4.0, off=r("hu"))
+        scan(r("ko"), r("cso"), r("kc"), A.add, A.max)
+        for c in range(4):
+            ts(r("above", 64 * c, 64 * c + 64), r("kc"), o2, col("ko", 16 * c + 15), A.add, A.is_gt, grp=g_("rank"))
+        scan(r("rq"), r("keep"), r("above"), A.min, A.add)
+        copy(r("ru"), r("rq", 63, 256, 64))
+        op("v", "scatter", (r("hw"), r("ru"), r("wr")), [r("ru"), r("wr")], [r("hw")], 50 + 64 * cm["scatter"] * cyc)
+        scan(r("h4"), r("cs4"), r("hw"), A.add, A.max)
         ho, hi = r("hout", 16 * t, 16 * t + 16), r("hin", 16 * t, 16 * t + 16)
         ts(ho, r("h4", 3, 64, 4), jm, -6144.0, A.add, A.add)
         send(hi, ho, "arh%d" % t, 4, "h%d" % t)
-        for e in range(4):
-            a, b = 256 * e, 256 * e + 256
-            act(r("ma", a, b), xw, F.Copy, off=r("a4", 16 * e, 16 * e + 16))
-            ttg(r("mb", a, b), xw, r("b4", 16 * e, 16 * e + 16), r("ma", a, b), A.max)
-            ttg(r("mm", e, 1024, 4), xw, r("d4", 16 * e, 16 * e + 16), r("mb", a, b), A.add, grp=g_("m"))
-        quant(r("qm"), r("sm"), r("mm"))
-        for b in range(4):
-            mm(r("pz", 512 * b, 512 * b + 256), r("wq", 128 * b, 128 * b + 128), r("wp", 128 * b, 128 * b + 128), r("qm"), r("sm"))
-            act(r("rz", 256 * b, 256 * b + 256), r("pz", 512 * b, 512 * b + 256), F.Relu, scale=0.015625)
-            tt(r("xb", XN + b, XEND, 4), r("xb", XN + b, XEND, 4), r("rz", 256 * b, 256 * b + 256), A.add, grp=g_("add"))
-        quant(r("qn", 256 * t + 256, 256 * t + 512), r("sn", 256 * t + 256, 256 * t + 512), r("xb", XN, XEND))
+        parts, n = par["layer"][t], 512 // par["pieces"][t]
+        for h in range(2):
+            win = xr(t, 0, XN + 256 + 512 * h)
+            for a in range(512 * h, 512 * h + 512, n):
+                act(r("ma", a, a + n), win, F.Copy, off=r("a4", a // 16, (a + n) // 16))
+                tt(r("mb", a, a + n), win, r("ma", a, a + n), A.max, off=r("b4", a // 16, (a + n) // 16))
+            for e in range(4):
+                tt(r("mm", 512 * h + e, 512 * h + 512, 4), win, r("mb", 512 * h + 128 * e, 512 * h + 128 * e + 128), A.add,
+                   off=r("d4", 16 * e + 8 * h, 16 * e + 8 * h + 8), grp=g_("m%d" % (h * (parts - 1))))
+        n = P // parts
+        for h in range(parts):
+            a, b = 4 * n * h, 4 * n * h + 4 * n
+            qm, sm = r("qm", n * h, n * h + n), r("sm", n * h, n * h + n)
+            quant(qm, sm, r("mm", a, b))
+            old, new = xr(t, XN + a, XN + b), xr(t + 1, XN + a, XN + b)
+            how = par["add"][t][h]
+            if how == "g":
+                dma("y", new, old, n)
+            for k in range(4):
+                z, out = r("pz", 512 * k, 512 * k + n), r("rz", a + k, b, 4)
+                mm(z, r("wq", 128 * k, 128 * k + 128), r("wp", 128 * k, 128 * k + 128), qm, sm)
+                grp = None if how == "k" else g_("rz%d" % h)
+                if k < par["relu_v"][t]:
+                    ts(out, z, 0.0, 0.015625, A.max, A.mult, grp=grp)
+                else:
+                    act(out, z, F.Relu, scale=0.015625, grp=grp)
+                if how == "k":
+                    tt(xr(t + 1, XN + a + k, XN + b, 4), xr(t, XN + a + k, XN + b, 4), out, A.add, grp=g_("add%d" % h))
+            if how == "g":
+                dma("g", new, r("rz", a, b), 3 * n, add=True)
         if t + 1 < R:
-            send_nodes(t + 1)
+            quant_nodes(t + 1)
         lq, ls = r("lq", 256 * t, 256 * t + 256), r("ls", 256 * t, 256 * t + 256)
-        arrive("arq%d" % t, 4, [lq, ls], ["nq%d" % t, "ns%d" % t, "eq%d" % t, "es%d" % t])
+        arrive("arq%d" % t, 2, [lq, ls], ["q%d" % t])
         for b in range(4):
-            src = r("pd", 512 * b, 512 * b + 256)
+            src = r("pd", 512 * (b % 2), 512 * (b % 2) + 256)
             mm(src, r("qc", 128 * b, 128 * b + 128), r("sc", 128 * b, 128 * b + 128), lq, ls)
             if b < par["dx_v"][t]:
-                copy(r("dx", b, 1024, 4), src, grp=g_("dx"))
+                copy(r("dx", b, 1024, 4), src)
             else:
-                act(r("dx", b, 1024, 4), src, F.Copy, grp=g_("dx"))
+                act(r("dx", b, 1024, 4), src, F.Copy)
         arrive("arh%d" % t, 1, [hi], ["h%d" % t])
-        ttg(r("xb", X0, XN), r("dx"), hi, r("xb", X0, XN), A.max)
-        quant(r("qe", 128 * t + 128, 128 * t + 256), r("se", 128 * t + 128, 128 * t + 256), r("xb", X0, X0 + 512))
-        if t + 1 < R:
-            send_entries(t + 1)
+        tt(xr(t + 1, X0, XN), r("dx"), xr(t, X0, XN), A.max, off=hi)
 
-    mm(r("pz", 0, 256), r("qv"), r("sv"), r("qn", 768, 1024), r("sn", 768, 1024))
-    act(r("ys", E, C), r("pz", 0, 256), F.Copy)
-    dma("y", ("y", E, C, 1, None), r("ys", E, C), 128, grp="out_n", tag="end")
-    dma("y", ("oc", 4 * E, 4 * C, 1, None), r("qn", 768, 1024), 128, grp="out_n", tag="end")
-    for k in range(4):
-        dma("y", ("osc", E, C, 1, (4 * k, 4 * k + 4)), r("sn", 768, 1024, p=(32 * k, 32 * k + 4)), 1, grp="out_n", tag="end")
-    mm(r("pz", 512, 640), r("qv"), r("sv"), r("qe", 384, 512), r("se", 384, 512))
-    copy(r("ys", 0, E), r("pz", 512, 512 + E))
-    dma("y", ("oc", 0, 4 * E, 1, None), r("qe", 384, 448), 32, grp="out_e", tag="end")
-    for k in range(4):
-        dma("yaya"[k], ("osc", 0, E, 1, (4 * k, 4 * k + 4)), r("se", 384, 448, p=(32 * k, 32 * k + 4)), 1, grp="out_e", tag="end")
-    dma("a", ("y", 0, E, 1, None), r("ys", 0, E), 32, grp="out_e", tag="end")
+    for h, (a, b) in enumerate(((128, C), (0, 128))):
+        quant_x(R, a, b)
+        q, s = qs(R, a, b)
+        mm(r("pc", 512 * h, 512 * h + b - a), r("qv"), r("sv"), q, s)
+        line("ys%d" % h, r("ys", a, b), r("pc", 512 * h, 512 * h + b - a))
+        dma("y", ("oc", 4 * a, 4 * b, 1, None), q, (b - a) // 2, grp="out%d" % h, tag="end")
+        for k in range(4):
+            dma("yaya"[k] if h else "y", ("osc", a, b, 1, (4 * k, 4 * k + 4)), s[:4] + ((32 * k, 32 * k + 4),), 1,
+                grp="out%d" % h, tag="end")
+        dma("a" if h else "y", ("y", a, b, 1, None), r("ys", a, b), (b - a) // 2, grp="out%d" % h, tag="end")
     op("y", "end", (), [], [], 0, after=["end"])
     return ops
 
@@ -390,7 +455,7 @@ def graph(ops):
         wr = [(x[0], bits(x)) for x in o["writes"]]
         for name, m in rd:
             deps.update(j for j, w, mj in seen.get(name, [])
-                        if mj & m and (w or name in ("pz", "pd") and ops[j]["q"] != o["q"]))
+                        if mj & m and (w or name in BANKS and ops[j]["q"] != o["q"]))
         for name, m in wr:
             deps.update(j for j, w, mj in seen.get(name, []) if mj & m)
         for name, m in rd:
@@ -408,12 +473,63 @@ def graph(ops):
     return members
 
 
-def plan(par, order):
+def lay(ops, pre, post, rank, wake, back, alone=False):
+    n = len(ops)
+    left, ready, start, end, busy = [len(p) for p in pre], [0.0] * n, [0.0] * n, [0.0] * n, {}
+    open_ = set(i for i in range(n) if not left[i])
+    while open_:
+        i = min(open_, key=lambda j: (rank[j], j))
+        open_.remove(i)
+        q, hold, cost = ops[i]["q"], ops[i]["hold"], ops[i]["cost"]
+        lag = cost - hold if back else 0.0
+        t = ready[i] + lag
+        if q and not alone:
+            spans = busy.setdefault(q, [])
+            k = len(spans)
+            for j, (a, b) in enumerate(spans):
+                if b > t:
+                    if t + hold <= a:
+                        k = j
+                        break
+                    t = b
+            spans.insert(k, (t, t + hold))
+        start[i], end[i] = t - lag, t - lag + cost
+        for u in post[i]:
+            ready[u] = max(ready[u], end[i] + (wake if q else 0.0))
+            left[u] -= 1
+            if not left[u]:
+                open_.add(u)
+    return start, end
+
+
+def arrange(ops, wake, passes, shake):
+    n = len(ops)
+    deps, users = [sorted(o["deps"]) for o in ops], [[] for _ in ops]
+    for i in range(n):
+        for j in deps[i]:
+            users[j].append(i)
+    way = lay(ops, users, deps, [-i for i in range(n)], wake, True, True)[1]
+    best, z = None, 1
+    for _ in range(passes):
+        z = (z * 1103515245 + 12345) % 2147483648
+        rank, mid = [], max(way) * z / 2147483648
+        for w in way:
+            z = (z * 1103515245 + 12345) % 2147483648
+            rank.append(shake * (z / 2147483648 if abs(w - mid) < 2 * shake else 0.5) - w)
+        start, end = lay(ops, deps, users, rank, wake, False)
+        late = lay(ops, users, deps, [-e for e in end], wake, True)[1]
+        start, end = lay(ops, deps, users, [-e for e in late], wake, False)
+        if best is None or max(end) <= best[0]:
+            best, way = (max(end), sorted(range(n), key=lambda i: (start[i], i))), late
+    return best[1]
+
+
+def plan(par):
     ops = program(par, COSTS)
     members = graph(ops)
+    order = arrange(ops, COSTS["wake"], par["passes"], par["shake"])
     n = len(ops)
     place = {i: k for k, i in enumerate(order)}
-    assert len(place) == n and all(place[j] < place[i] for i in range(n) for j in ops[i]["deps"])
     known, at = {}, [0] * n
     for i in order:
         o = ops[i]
@@ -422,7 +538,7 @@ def plan(par, order):
             continue
         k = known.get(o["q"], 0)
         for j in sorted(o["deps"], key=lambda j: -place[j]):
-            if not k >> j & 1:
+            if not k >> j & 1 and ops[j]["call"] != "send":
                 o["waits"].append(ops[j]["key"])
                 for m in members[ops[j]["key"]]:
                     k |= 1 << m | at[m]
@@ -457,7 +573,7 @@ def plan(par, order):
             slot[1] |= 1 << m
         slot[2] += len(ms) * (1 if o["cls"] == "c" else 16)
         sems[key] = (slot[0], slot[2])
-    return ops, sems
+    return ops, order, sems
 
 
 PLAN = []
@@ -468,27 +584,28 @@ def rank_program(g, core, T, topo):
     if rank is None:
         return
     if not PLAN:
-        PLAN.append(plan(PARAMS, ORDER))
-    ops, sems = PLAN[0]
+        PLAN.append(plan(PARAMS))
+    ops, order, sems = PLAN[0]
     n = len(T.cores)
     nxt, prv = T.cores[(rank + 1) % n], T.cores[(rank - 1) % n]
     rid, pid = topo.addr(nxt)[:2]
     mask, out_engines, in_engines = topo.mask(core, nxt), len(topo.engines(core, nxt)), len(topo.engines(prv, core))
     queue = {"g": g, "v": g.vector, "a": g.scalar, "t": g.tensor, "y": g.sync}
 
-    def ap(x):
+    def ap(x, off=None):
         if not isinstance(x, tuple):
             return x
         name, a, b, s, p = x
         rows = slice(None) if p is None else slice(p[0], p[1])
-        return T[name][rows, a:b] if s == 1 else T[name][rows, a:b:s]
+        v = T[name][rows, a:b] if s == 1 else T[name][rows, a:b:s]
+        return v.indirect(ap(off)) if off else v
 
     def raw(x):
         codes = x[0] in SCRATCH and SCRATCH[x[0]][2] == Q4
         return ap(x).bitcast(dt.uint8) if codes else ap(x)
 
     sent = [0]
-    for i in ORDER:
+    for i in order:
         o = ops[i]
         if o["q"] is None:
             continue
@@ -500,32 +617,27 @@ def rank_program(g, core, T, topo):
         if call == "memset":
             ins = q.memset(ap(x[0]), x[1])
         elif call == "copy":
-            ins = q.tensor_copy(ap(x[0]), ap(x[1]))
+            ins = q.tensor_copy(ap(x[0]), ap(x[1], x[2]))
         elif call == "ts":
             if x[5] is None:
-                ins = q.tensor_scalar(ap(x[0]), ap(x[1]), ap(x[2]), None, x[4])
+                ins = q.tensor_scalar(ap(x[0]), ap(x[1], x[6]), ap(x[2]), None, x[4])
             else:
-                ins = q.tensor_scalar(ap(x[0]), ap(x[1]), ap(x[2]), ap(x[3]), x[4], x[5])
+                ins = q.tensor_scalar(ap(x[0]), ap(x[1], x[6]), ap(x[2]), ap(x[3]), x[4], x[5])
         elif call == "tt":
-            ins = q.tensor_tensor(ap(x[0]), ap(x[1]), ap(x[2]), x[3])
-        elif call == "ttg":
-            ins = q.tensor_tensor(ap(x[0]), ap(x[1]).indirect(ap(x[2])), ap(x[3]), x[4])
-        elif call == "gather":
-            ins = q.tensor_copy(ap(x[0]), ap(x[1]).indirect(ap(x[2])))
+            ins = q.tensor_tensor(ap(x[0]), ap(x[1], x[4]), ap(x[2]), x[3])
         elif call == "scatter":
-            ins = q.tensor_copy(ap(x[0]).indirect(ap(x[1])), ap(x[2]))
+            ins = q.tensor_copy(ap(x[0], x[1]), ap(x[2]))
         elif call == "pickq":
             ins = q.tensor_copy(ap(x[0]).bitcast(dt.uint32), ap(x[1]).bitcast(dt.uint32).indirect(ap(x[2])))
         elif call == "scan":
-            ins = q.tensor_tensor_scan(ap(x[0]), ap(x[1]), ap(x[2]), 0.0, x[3], x[4])
+            ins = q.tensor_tensor_scan(ap(x[0]), ap(x[1]), ap(x[2]), ap(x[3]), x[4], x[5])
         elif call == "turn":
             ins = q.transpose(ap(x[0]), ap(x[1]))
-        elif call == "sum":
-            ins = q.tensor_reduce(ap(x[0]), ap(x[1]), AxisListType.X, A.add)
+        elif call == "reduce":
+            ins = q.tensor_reduce(ap(x[0]), ap(x[1]), AxisListType.X, x[2])
         elif call == "quant":
             ins = q.quantize_mx(ap(x[0]), ap(x[1]), ap(x[2]))
         elif call == "act":
-            src = ap(x[1]).indirect(ap(x[6])) if x[6] else ap(x[1])
             kw = {}
             if x[3] != 1.0:
                 kw["scale"] = ap(x[3])
@@ -533,7 +645,7 @@ def rank_program(g, core, T, topo):
                 kw["bias"] = ap(x[4])
             if x[5]:
                 kw["accum_out"] = ap(x[5])
-            ins = q.activation(ap(x[0]), src, x[2], **kw)
+            ins = q.activation(ap(x[0]), ap(x[1], x[6]), x[2], **kw)
         elif call == "mm":
             ins = q.matmul_mx(ap(x[0]), ap(x[1]), ap(x[2]), ap(x[3]), ap(x[4]), True, True)
         elif call == "iota":
@@ -541,10 +653,13 @@ def rank_program(g, core, T, topo):
                 ins = q.iota(ap(x[0]), x[1], x[2], x[3])
             else:
                 ins = q.iota(ap(x[0]), x[1], x[2], x[3], allow_small_or_imprecise_dtypes=True)
-        elif call == "strip":
-            ins = q.affine_select(ap(x[0]), ap(x[0]), [[1, 528]], A.is_equal, 0.0, -3, -4)
+        elif call == "select":
+            ins = q.affine_select(ap(x[0]), ap(x[0]), x[1], x[2], x[3], x[4], x[5])
         elif call == "dma":
-            ins = q.dma_start(raw(x[0]), raw(x[1]))
+            if x[2]:
+                ins = q.dma_start(raw(x[0]), raw(x[1]), accum_op=A.add)
+            else:
+                ins = q.dma_start(raw(x[0]), raw(x[1]))
         elif call == "send":
             q.remote_dma(raw(x[0]), raw(x[1]), T.sem[x[2]], T.sem["sent"], pid, rid, mask)
             sent[0] += out_engines

@@ -6,11 +6,12 @@ C, E, P, R = 320, 64, 256, 3
 X0 = 16
 XN = X0 + 4 * E
 XW = X0 + 4 * C
-LOST = 2.0 ** 19
+UNIT = 2.0 ** -19
 BASE = 160000.0
 MAGIC = 1.5 * 2.0 ** 35
 TINY = 1e-37
 Q4, U8, U16, F32, BF, I32 = "float8_e4m3fn_x4", "uint8", "uint16", "float32", "bfloat16", "int32"
+BYTES = {Q4: 4, U8: 1, U16: 2, F32: 4, BF: 2, I32: 4}
 BANKS = ("pz", "pc", "pd")
 
 
@@ -18,7 +19,7 @@ def sb(n, d):
     return ("sbuf", [128, n], d)
 
 
-SCRATCH = {
+BUFFERS = {
     "xs": sb(4 * XW, BF), "ub": sb(512, BF), "vb": sb(512, BF), "pab": sb(32, I32),
     "wq": sb(512, Q4), "wp": sb(512, U8),
     "qu": sb(128, Q4), "su": sb(128, U8), "qup": sb(384, Q4), "sup": sb(384, U8),
@@ -28,7 +29,9 @@ SCRATCH = {
     "hout": sb(48, U16), "hin": sb(48, U16),
     "pi": sb(2, I32), "pj": sb(8, I32), "pf": sb(8, F32), "ps": sb(10, F32),
     "k64": sb(64, F32), "sf": sb(4, F32), "cf": sb(4, F32), "thr": sb(4, F32), "own": sb(192, F32),
-    "ra": sb(64, F32), "oa": sb(64, F32), "eq0": sb(64, F32), "thr0": sb(64, F32),
+    "lsa": sb(4, F32), "lbi": sb(4, F32), "cji": sb(64, F32), "kd": sb(64, F32), "rk": sb(4, F32),
+    "ra": sb(64, F32), "oa": sb(64, F32), "eq0": sb(64, F32), "thr0": sb(256, F32), "gone": sb(256, BF), "side": sb(448, F32),
+    "df": sb(64, F32), "dcon": sb(64, F32), "l3": sb(4, U16), "tal": sb(1, F32), "sb2": sb(4, F32), "ones": sb(256, BF),
     "cj": sb(64, F32), "y4": sb(64, F32), "f1": sb(64, F32), "cs4": sb(64, F32),
     "y16": sb(256, BF), "e1": sb(256, BF), "cs16": sb(256, BF), "ki": sb(36, F32),
     "mtab": sb(272, BF), "ttab": sb(272, BF), "ktab": sb(272, BF), "sbi": sb(4, F32), "sj": sb(4, F32),
@@ -40,7 +43,7 @@ SCRATCH = {
     "tr": sb(544, F32), "g1": sb(64, F32), "val": sb(64, F32), "loff": sb(64, U16), "ds": sb(64, F32),
     "d4": sb(64, U16), "dl": sb(16, U16), "drow": sb(256, F32),
     "lsc": sb(256, BF), "lqv": sb(64, F32), "lr": sb(64, F32), "b4": sb(64, U16),
-    "ma": sb(1024, BF), "mb": sb(1024, BF), "mm": sb(1024, BF), "rz": sb(1024, F32),
+    "ma": sb(2048, BF), "mb": sb(2048, BF), "anew": sb(1024, BF), "kt": sb(16, F32), "mm": sb(1024, BF), "rz": sb(1024, F32),
     "junk": sb(14 * 256, BF), "hs": sb(8, F32), "hh": sb(8, F32), "lo": sb(8, F32), "mu": sb(16, U16),
     "mrow": sb(256, BF), "gq": sb(1, F32), "gu": sb(2, U16), "tau": sb(1, F32), "kr": sb(16, F32), "kk": sb(1, F32),
     "over": sb(256, BF), "from": sb(256, BF), "bnd": sb(256, BF), "cum": sb(256, BF), "sq": sb(4, F32), "hu": sb(4, U16),
@@ -48,18 +51,34 @@ SCRATCH = {
     "hw": sb(64, F32), "h4": sb(64, F32), "dx": sb(1024, BF), "ys": sb(C, F32),
     "pz": ("psum", [128, 2048], F32), "pc": ("psum", [128, 1024], F32), "pd": ("psum", [128, 1024], F32),
 }
+SCRATCH = dict(BUFFERS)
 NPOOL = {"c": 100, "h": 30, "s": 12}
 SEMAPHORES = (["sent"] + ["arq%d" % t for t in range(R)] + ["arh%d" % t for t in range(R)]
               + ["%s%d" % (k, i) for k in ("c", "h", "s") for i in range(NPOOL[k])])
 
-PARAMS = {"cuts": (2, 2, 2), "layer": (2, 2, 2), "add": ("gg", "kg", "gk"), "relu_v": (0, 0, 0), "pieces": (2, 2, 2),
-          "mrow_v": (0, 0, 1), "g_plain": (0, 0, 0), "hist_v": (0, 0, 2), "seek_v": (0, 0, 0), "dx_v": (0, 0, 0),
-          "ga3_v": (0, 0, 0),
+PARAMS = {"cuts": (2, 2, 2), "layer": (2, 2, 2), "add": ("gk", "kk", "gk"), "relu_v": (0, 0, 0), "pieces": (1, 2, 1),
+          "mrow_v": (0, 0, 1), "g_plain": (0, 0, 0), "hist_v": (0, 0, 4), "seek_v": (0, 0, 0), "dx_v": (0, 0, 0),
+          "ga3_v": (0, 0, 0), "lost_v": (1, 1, 1), "rank_v": (0, 0, 0), "tau_v": (0, 0, 0), "l3_v": (1, 1, 1),
+          "pair": ((0, 0), (0, 0), (0, 0)), "place": (0, 1, 1, 1), "gload": "v",
+          "both": 1, "few": 1, "d_pick": (0, 0, 0), "over_a": (1, 1, 1), "loads": "y", "xload": ((0, 192), (192, 320)),
           "scalar": ("cs16", "gt1", "gt2", "d64", "ra", "sup0", "sup1", "wr", "ys0", "own2", "own3", "tie", "cso", "cs4",
-                     "c1", "sbi", "jm", "o1", "o2", "ni"),
-          "passes": 2500, "shake": 1500.0}
-COSTS = {"cyc": 0.83, "gather": 1.56, "scatter": 3.8, "wake": 180.0, "dma": 1150.0, "gdma": 1450.0, "remote": 1150.0,
-         "pe": 0.7, "issue": 60.0, "gissue": 300.0, "rissue": 150.0, "kb": 4.0, "least": 64.0, "least_a": 224.0}
+                     "c1", "sbi", "jm", "o1", "o2", "ni", "cj", "i4", "b15", "sb2", "dcon"),
+          "soft": 1.0, "reach": 2, "swaps": 9000, "passes": 1800, "shake": 1500.0}
+COSTS = {"cyc": 0.83, "gather": 1.56, "scatter": 3.8, "pe": 0.7, "least": 88.0, "least_a": 95.0, "call": 0.0,
+         "call_a": 0.0, "call_t": 0.0, "pick": 100.0, "pick_a": 65.0, "psum": 0.0, "lag": {"v": 50.0, "a": 150.0, "t": 70.0},
+         "near": 150.0, "far": 150.0, "parked": True, "dma": 1050.0, "gdma": 2400.0, "remote": 1200.0, "issue": 160.0,
+         "gissue": 300.0, "rissue": 100.0, "row": 0.0, "byte": 0.05, "add": 1.0, "away": 1.5, "first_r": 400.0,
+         "first_g": 500.0}
+STEADY = dict(COSTS, gather=1.65, least=102.0, least_a=175.0, pick=62.0, pick_a=105.0, lag={"a": 130.0}, near=155.0,
+              far=125.0, parked=False, dma=500.0, gdma=1850.0, remote=1700.0, add=2.2, rissue=50.0, first_r=1300.0)
+GUESSES = [STEADY, COSTS,
+           dict(COSTS, least=75.0, least_a=175.0, pick=105.0, pick_a=90.0, lag={"v": 70.0, "a": 255.0}, near=50.0,
+                far=50.0, dma=1750.0, gdma=2300.0, remote=1500.0, issue=30.0, rissue=250.0, byte=0.04, add=1.9,
+                first_r=1000.0),
+           dict(STEADY, gather=1.5, least=65.0, call=18.0, least_a=64.0, pick=72.0, pick_a=95.0, lag={}, near=125.0,
+                far=280.0, remote=500.0, dma=350.0, gdma=1650.0, issue=180.0, rissue=1200.0, add=2.5, first_r=0.0),
+           dict(STEADY, cyc=1.12, gather=1.8, pick=85.0, pick_a=140.0, lag={"a": 180.0}, near=205.0, far=170.0,
+                dma=700.0, gdma=2200.0, remote=2000.0)]
 
 
 def r(name, a=0, b=None, s=1, p=None):
@@ -90,17 +109,24 @@ def program(par, cm):
     ops = []
     cyc = cm["cyc"]
 
-    def op(q, call, args, reads, writes, cost, hold=None, grp=None, cls="c", after=None, tag=None):
+    def op(q, call, args, reads, writes, cost, hold=None, data=0.0, grp=None, cls="c", after=None, tag=None):
         reads = [x for x in reads if isinstance(x, tuple) and x[0] in SCRATCH]
         writes = [x for x in writes if x[0] in SCRATCH]
-        ops.append({"q": q, "call": call, "args": args, "reads": reads, "writes": writes, "cost": cost,
-                    "hold": cost if hold is None else hold, "grp": grp, "cls": cls, "after": after, "tag": tag})
+        if hold is None:
+            hold, cost = cost, cost + cm["lag"].get(q, 0.0)
+        ops.append({"q": q, "call": call, "args": args, "reads": reads, "writes": writes, "cost": cost, "hold": hold,
+                    "data": data, "grp": grp, "cls": cls, "after": after, "tag": tag})
 
     def plain(out, ins):
-        return max(cm["least"], width(out) * (0.5 if narrow(out, *ins) else 1.0)) * cyc
+        n = width(out) * (0.5 if narrow(out, *ins) else 1.0)
+        return (max(cm["least"], n) + cm["call"] + cm["psum"] * any(x[0] in BANKS for x in ins)) * cyc
+
+    def moved(x, factor):
+        rows = 128 if x[4] is None else len(range(*x[4]))
+        return -(-rows // 16) * (cm["row"] + width(x) * BYTES[SCRATCH[x[0]][2]] * cm["byte"] * factor)
 
     def gath(out):
-        return 50 + width(out) * cm["gather"] * cyc
+        return cm["pick"] + width(out) * cm["gather"] * cyc
 
     def memset(out, v, **k):
         op("v", "memset", (out, v), [], [out], plain(out, []), **k)
@@ -113,7 +139,8 @@ def program(par, cm):
            gath(out) if off else plain(out, [in0]), **k)
 
     def tt(out, in0, in1, o, off=None, **k):
-        c = gath(out) if off else max(cm["least"], (1 if in0[0] in BANKS else 2) * width(out)) * cyc
+        bank = in0[0] in BANKS
+        c = gath(out) if off else (max(cm["least"], (2 - bank) * width(out)) + cm["call"] + cm["psum"] * bank) * cyc
         op("v", "tt", (out, in0, in1, o, off), [in0, in1, off], [out], c, **k)
 
     def scan(out, d0, d1, o0, o1, init=0.0, **k):
@@ -123,13 +150,14 @@ def program(par, cm):
         op("v", "turn", (out, in_), [in_], [out], plain(out, [in_]), **k)
 
     def reduce(out, in_, o, **k):
-        op("v", "reduce", (out, in_, o), [in_], [out], max(cm["least"], width(in_)) * cyc, **k)
+        op("v", "reduce", (out, in_, o), [in_], [out], (max(cm["least"], width(in_)) + cm["call"]) * cyc, **k)
 
     def quant(q, s, in_, **k):
         op("v", "quant", (q, s, in_), [in_], [q, s], (12 + 0.22 * width(in_)) * cyc / 0.83, **k)
 
     def act(out, in_, f, scale=1.0, bias=None, acc=None, off=None, **k):
-        c = (65 + width(out) * cm["gather"] * cyc) if off else max(cm["least_a"], width(out)) * cyc
+        c = (max(cm["least_a"], width(out)) + cm["call_a"] + cm["psum"] * (in_[0] in BANKS)) * cyc
+        c = cm["pick_a"] + width(out) * cm["gather"] * cyc if off else c
         op("a", "act", (out, in_, f, scale, bias, acc, off), [in_, scale, bias, off],
            [out] + ([acc] if acc else []), c + (20 if acc else 0), **k)
 
@@ -146,7 +174,7 @@ def program(par, cm):
             ts(out, in_, scale, bias, A.mult, A.add, off=off, **k)
 
     def mm(out, lq, ls, rq, rs, **k):
-        op("t", "mm", (out, lq, ls, rq, rs), [lq, ls, rq, rs], [out], (width(out) + 16) * cm["pe"], **k)
+        op("t", "mm", (out, lq, ls, rq, rs), [lq, ls, rq, rs], [out], (width(out) + 16) * cm["pe"] + cm["call_t"], **k)
 
     def iota(out, pat, base, mult=0, **k):
         op("g", "iota", (out, pat, base, mult), [], [out], (130 + 1.66 * width(out)) * cyc / 0.83, **k)
@@ -156,11 +184,13 @@ def program(par, cm):
 
     def dma(q, out, in_, kb, add=False, **k):
         op(q, "dma", (out, in_, add), [in_] + ([out] if add else []), [out],
-           cm["gdma" if q == "g" else "dma"] + kb * cm["kb"], hold=cm["gissue" if q == "g" else "issue"],
+           cm["gdma" if q == "g" else "dma"], hold=cm["gissue" if q == "g" else "issue"],
+           data=moved(out if out[0] in SCRATCH else in_, cm["add"] if add else 1.0),
            cls="s" if q == "g" else "h", **k)
 
     def send(out, in_, sem, kb, tag):
-        op("g", "send", (out, in_, sem), [in_], [], cm["remote"] + 1.5 * kb * cm["kb"], hold=cm["rissue"], cls="r", tag=tag)
+        op("g", "send", (out, in_, sem), [in_], [], cm["remote"], hold=cm["rissue"], data=moved(out, cm["away"]),
+           cls="r", tag=tag)
 
     def arrive(sem, n, refs, tags):
         op(None, "arrive", (sem, n), [], refs, 0, cls="r", after=tags)
@@ -169,7 +199,8 @@ def program(par, cm):
         return r(name, j, j + 1)
 
     def xr(t, a, b, s=1):
-        return r("xs", XW * t + a, XW * t + b, s)
+        k = XW * par["place"][t]
+        return r("xs", k + a, k + b, s)
 
     def quant_x(t, a, b):
         quant(r("qx", C * t + a, C * t + b), r("sx", C * t + a, C * t + b), xr(t, X0 + 4 * a, X0 + 4 * b))
@@ -180,17 +211,18 @@ def program(par, cm):
     def quant_nodes(t):
         n = P // par["cuts"][t]
         for a in range(E, C, n):
-            quant_x(t, a, a + n)
+            quant_x(t, 0 if par["xload"][0][0] == 0 and t == 0 and a == E else a, a + n)
 
-    dma("a", r("ub"), ("u", 0, 512, 1, None), 128)
-    dma("y", xr(0, XN, XN + 512), ("x", 4 * E, 4 * E + 512, 1, None), 128, tag="x")
-    dma("y", xr(0, XN + 512, XW), ("x", 4 * E + 512, 4 * C, 1, None), 128, tag="x")
-    dma("a", r("pab", 0, 16), ("pa", 0, 16, 1, None), 8, grp="pab")
-    dma("a", r("pab", 16, 32), ("pb", 0, 16, 1, None), 8, grp="pab")
-    dma("y", xr(0, X0, XN), ("x", 0, 4 * E, 1, None), 64)
-    dma("g", r("wq"), ("wc", 0, 2048, 1, None), 256, after=["x"])
-    dma("y", r("wp"), ("ws", 0, 512, 1, None), 64, after=["x"])
-    dma("y", r("vb"), ("v", 0, 512, 1, None), 128, after=["x"])
+    lq_ = par["loads"]
+    dma(lq_, r("ub"), ("u", 0, 512, 1, None), 128)
+    for a, b in par["xload"]:
+        dma("y", xr(0, X0 + 4 * a, X0 + 4 * b), ("x", 4 * a, 4 * b, 1, None), 128, tag="x" if b > E else None)
+        if b == C:
+            dma(lq_, r("pab", 0, 16), ("pa", 0, 16, 1, None), 8, grp="pab" if lq_ == "a" else None)
+            dma(lq_, r("pab", 16, 32), ("pb", 0, 16, 1, None), 8, grp="pab" if lq_ == "a" else None)
+    dma("g" if par["gload"] == "c" else "y", r("wq"), ("wc", 0, 2048, 1, None), 256, after=["x"])
+    dma("g" if par["gload"] == "s" else "y", r("wp"), ("ws", 0, 512, 1, None), 64, after=["x"])
+    dma("g" if par["gload"] == "v" else "y", r("vb"), ("v", 0, 512, 1, None), 128, after=["x"])
 
     iota(col("pi", 0), [[0, 1]], 0, 1)
     iota(r("k64"), [[1, 64]], 0)
@@ -203,7 +235,7 @@ def program(par, cm):
     copy(r("pf", 2, 6), r("pj", 2, 6))
     lev, flag, pi16, p16, p8, sel = [col("pf", j) for j in range(6)]
     slope, odd, tb1, tbase, jm, i4, b15, o1, o2, ni = [col("ps", j) for j in range(10)]
-    line("slope", slope, flag, -1025.0, 2052.0)
+    line("slope", slope, flag, -1025.0 * UNIT, 2052.0 * UNIT)
     ts(odd, flag, 4.0, p16, A.mult, A.not_equal)
     line("tb1", tb1, sel, 16.0, lev)
     line("tbase", tbase, odd, 272.0, tb1)
@@ -230,23 +262,39 @@ def program(par, cm):
         op("v", "pickq", (q, r("qu"), o), [r("qu"), o], [q], gath(q), grp="pick%d" % a)
         line("sup%d" % a, r("sup", 128 * a, 128 * b), r("su"), off=o, grp="pick%d" % a)
     for t in range(R):
-        iota(xr(t, 0, X0), [[0, X0]], 0)
+        if t == 0 or par["place"][t] != par["place"][t - 1]:
+            iota(xr(t, 0, X0), [[0, X0]], 0)
     quant_nodes(0)
 
     ts(r("sf"), r("k64", 0, 4), lev, slope, A.is_equal, A.mult, grp="sf")
-    ts(r("cf"), r("k64", 0, 4), lev, BASE, A.is_equal, A.mult, grp="sf")
-    ts(r("thr"), r("k64", 1, 5), lev, 1e29, A.is_equal, A.mult)
+    ts(r("cf"), r("k64", 0, 4), lev, BASE * UNIT, A.is_equal, A.mult, grp="sf")
+    if any(par["lost_v"] + par["l3_v"]) and not par["few"]:
+        ts(r("thr"), r("k64", 1, 5), lev, 1e29, A.is_equal, A.mult)
+    if not all(par["lost_v"]) and not par["few"]:
+        ts(r("lsa"), r("k64", 1, 5), lev, -1.0, A.not_equal, A.mult, grp="ls")
+        ts(r("lbi"), r("k64", 1, 5), lev, None, A.is_equal, grp="ls")
     line("tw", r("tw", 0, 64), r("k64"), col("sf", 0), col("cf", 0))
     for l in range(1, 4):
-        line("own%d" % l, r("own", 64 * l - 64, 64 * l), r("k64"), col("sf", l), col("cf", l))
-    copy(r("abl"), r("pab"))
+        out = r("side", 64 * l, 64 * l + 64) if par["both"] and l > 1 else r("own", 64 * l - 64, 64 * l)
+        line("own%d" % l, out, r("k64"), col("sf", l), col("cf", l))
+    if par["both"]:
+        iota(r("side", 384, 448), [[0, 64]], 0)
+        for a, b, c in ((0, 4, 0), (4, 12, 16), (12, 20, 4), (20, 28, 24), (28, 32, 12)):
+            copy(r("abl", a, b), r("pab", c, c + b - a))
+    else:
+        for a in range(0, 32, 32 if lq_ == "a" else 16):
+            copy(r("abl", a, a + (32 if lq_ == "a" else 16)), r("pab", a, a + (32 if lq_ == "a" else 16)))
     tt(r("oa"), r("tw", 0, 64), r("own", 0, 64), A.max, off=r("abl", 0, 4))
     line("ra", r("ra"), r("tw", 0, 64), off=r("abl", 0, 4))
-    tt(r("eq0"), r("tw", 0, 64), r("ra"), A.is_equal, off=r("abl", 16, 20))
-    line("thr0", r("thr0"), r("eq0"), 1e29)
+    tt(r("eq0"), r("tw", 0, 64), r("ra"), A.is_equal, off=r("abl", 4, 8) if par["both"] else r("abl", 16, 20))
+    line("thr0", r("thr0", 0, 64), r("eq0"), 1e29)
+    if par["few"]:
+        ts(r("thr0", 64, 192), r("side", 128, 256) if par["both"] else r("own", 64, 192), 0.0, 1e29, A.is_gt, A.mult)
+        iota(r("thr0", 192, 256), [[0, 64]], 0)
     iota(r("tw", 320, 336), [[0, 16]], 0)
-    iota(r("cj"), [[0, 16], [256, 4]], int(4 - 2 * BASE))
-    select(r("cj"), [[-1, 4], [0, 4], [1, 4]], A.not_equal, -8 * BASE, -1, 0)
+    iota(r("cji"), [[0, 16], [256, 4]], int(4 - 2 * BASE))
+    select(r("cji"), [[-1, 4], [0, 4], [1, 4]], A.not_equal, -8 * BASE, -1, 0)
+    line("cj", r("cj"), r("cji"), UNIT)
     iota(r("y4"), [[0, 16], [2048, 4]], 0)
 
     iota(r("econ"), [[0, 2], [1, 4], [0, 8]], X0)
@@ -269,18 +317,31 @@ def program(par, cm):
     iota(r("mtab", 0, 257), [[1, 257]], 0)
     iota(r("ttab", 0, 64), [[0, 64]], 1)
     iota(r("ttab", 64, 257), [[0, 193]], 33)
-    iota(r("ktab", 0, 64), [[-1, 64]], 64)
-    iota(r("ktab", 64, 257), [[0, 193]], 64)
+    if not all(par["over_a"]):
+        iota(r("ktab", 0, 64), [[-1, 64]], 64)
+        iota(r("ktab", 64, 257), [[0, 193]], 64)
     line("sbi", r("sbi"), r("k64", 0, 64, 16), -1.0, ni)
+    if any(par["over_a"]):
+        line("sb2", r("sb2"), r("sbi"), 2.0, -128.0)
+        iota(r("ones"), [[0, 256]], 1)
+    if any(par["d_pick"]):
+        ts(r("l3"), r("k64", 3, 7), 3.0, i4, A.min, A.add)
+        iota(r("df"), [[1, 4], [0, 16]], X0 - 4)
+        line("dcon", r("dcon"), r("df"), UNIT)
     if any(par["seek_v"]):
         line("sj", r("sj"), r("sbi"), -1.0)
     line("tie", r("tie"), r("k64"), -1.0 / 64, 63.0 / 64)
     line("cso", r("cso"), r("e1", 0, 64), 128.0, -16384.0)
-    iota(r("keep"), [[0, 4], [64, 64]], 0)
+    if any(par["rank_v"]) or not par["few"]:
+        iota(r("keep"), [[0, 4], [64, 64]], 0)
+    if any(any(x) for x in par["pair"]):
+        iota(r("anew", 0, 256), [[0, 128], [1, 2]], -1)
+        for a in range(768, -1, -256):
+            act(r("anew", a, a + 256), r("anew", 0, 256), F.Copy, scale=1e29)
     ts(r("f1"), r("y4"), lev, jm, A.add, A.not_equal)
     line("cs4", r("cs4"), r("f1"), 10240.0, -8192.0)
 
-    iota(r("ebig"), [[0, 528]], 1)
+    memset(r("ebig"), 1.0)
     select(r("ebig"), [[1, 528]], A.is_equal, 0.0, -3, -4)
     for b in range(4):
         quant(r("qc", 128 * b, 128 * b + 128), r("sc", 128 * b, 128 * b + 128), r("ebig", 3 - b, 515 - b))
@@ -293,41 +354,59 @@ def program(par, cm):
         score = lambda a, b: r("pc", a // n * 512 + a % n, a // n * 512 + a % n + b - a)
         for a in range(0, P, n):
             mm(score(a, a + n), *up, *qs(t, E + a, E + a + n))
-            for k in range(a // 64, (a + n) // 64):
-                if k:
-                    ts(r("lost", 64 * k - 64, 64 * k), score(64 * k, 64 * k + 64), col("thr", k), LOST, A.is_lt, A.mult)
-                else:
-                    tt(r("l0"), score(0, 64), r("thr0"), A.is_lt)
+            if par["few"]:
+                out = r("side", 2 * a, 2 * a + n) if par["both"] else r("gone", a, a + n)
+                tt(out, score(a, a + n), r("thr0", a, a + n), A.is_lt)
+            for k in range(a // 64, (a + n) // 64 * (1 - par["few"])):
+                out, s = r("lost", 64 * k - 64, 64 * k), score(64 * k, 64 * k + 64)
+                if k == 0:
+                    tt(r("l0"), s, r("thr0", 0, 64), A.is_lt)
+                elif par["lost_v" if k < 3 else "l3_v"][t]:
+                    ts(out, s, col("thr", k), None, A.is_lt)
+                elif k < 3:
+                    act(out, s, F.Sign, scale=col("lsa", k), bias=col("lbi", k))
             act(r("nsg", a, a + n), score(a, a + n), F.Sign, scale=-1.0, bias=-TINY)
-        quant_x(t, 0, 128)
+        if t or par["xload"][0][0]:
+            quant_x(t, 0, 128)
         send(r("lq", 256 * t, 256 * t + 256), r("qx", C * t, C * t + 256), "arq%d" % t, 128, "q%d" % t)
         send(r("ls", 256 * t, 256 * t + 256), r("sx", C * t, C * t + 256), "arq%d" % t, 32, "q%d" % t)
-        tt(r("tw", 64, 128), r("oa"), r("l0"), A.mult)
+        tt(r("tw", 64, 128), r("oa"), r("side" if par["both"] else "gone", 0, 64) if par["few"] else r("l0"), A.mult)
         for k in range(1, 4):
             win, a, b = r("tw", 0, 64 + 64 * k), 64 * k - 64, 64 * k
             la, lb = r("abl", 4 * k, 4 * k + 4), r("abl", 16 + 4 * k, 20 + 4 * k)
-            if k < 3:
-                tt(r("ga", a, b), win, r("own", a + 64, b + 64), A.max, off=la)
-            elif par["ga3_v"][t]:
-                copy(r("ga", a, b), win, off=la)
+            if par["both"]:
+                tt(r("ga", 0, 128), win, r("side", 128 * k - 64, 128 * k + 64), A.max, off=r("abl", 8 * k, 8 * k + 8))
+                tt(r("tw", 128 + a, 128 + b), r("ga", 0, 64), r("ga", 64, 128), A.min)
             else:
-                act(r("ga", a, b), win, F.Copy, off=la)
-            tt(r("gb", a, b), win, r("lost", a, b), A.max, off=lb)
-            tt(r("tw", 128 + a, 128 + b), r("ga", a, b), r("gb", a, b), A.min)
+                if k < 3:
+                    tt(r("ga", a, b), win, r("own", a + 64, b + 64), A.max, off=la)
+                elif par["ga3_v"][t]:
+                    copy(r("ga", a, b), win, off=la)
+                else:
+                    act(r("ga", a, b), win, F.Copy, off=la)
+                lost = r("lost", a, b) if k < 3 or par["l3_v"][t] else r("nsg", 192, 256)
+                tt(r("gb", a, b), win, r("gone", a + 64, b + 64) if par["few"] else lost, A.max, off=lb)
+                tt(r("tw", 128 + a, 128 + b), r("ga", a, b), r("gb", a, b), A.min)
             a, b, e = ((0, 128, 128), (128, 192, 192), (192, 256, 288))[k - 1]
-            turn(r("tr", a, b), r("tw", 64 + a, 64 + b))
-            turn(r("tr", 256 + a, 256 + e), r("tw", 48 + a, 48 + e))
+            if par["few"] and k < 3:
+                a, b, e = 0, 192 * (k - 1), 192
+            if b:
+                turn(r("tr", a, b), r("tw", 64 + a, 64 + b))
+                turn(r("tr", 256 + a, 256 + e), r("tw", 48 + a, 48 + e))
         tt(r("g1"), r("tr"), r("cj"), A.add, off=trh)
         tt(r("val"), r("tr"), r("g1"), A.add, off=trl)
         scan(r("ds"), r("y4"), r("val"), A.min, A.max)
-        for e in range(4):
-            ts(r("d4", 16 * e, 16 * e + 16), r("ds", 3, 64, 4), float(X0 - 4 + e), None, A.add)
-        ts(r("loff"), r("val"), 0.25, None, A.mult, off=lofl)
+        if par["d_pick"][t]:
+            tt(r("df"), r("ds"), r("dcon"), A.add, off=r("l3"))
+            ts(r("d4"), r("df"), 1 / UNIT, None, A.mult)
+        else:
+            for e in range(4):
+                ts(r("d4", 16 * e, 16 * e + 16), r("ds", 3, 64, 4), 1 / UNIT, float(X0 - 4 + e), A.mult, A.add)
+        ts(r("loff"), r("val"), 0.25 / UNIT, None, A.mult, off=lofl)
         if t == R - 1:
-            ts(r("dl"), r("ds", 3, 64, 4), 0.25, None, A.mult)
+            ts(r("dl"), r("ds", 3, 64, 4), 0.25 / UNIT, None, A.mult)
             act(r("drow"), r("mtab", 0, 257), F.Identity, bias=-1.0, off=r("dl"))
-            for k in range(8):
-                dma("y", ("od", 0, 256, 1, (k, k + 1)), r("drow", p=(16 * k, 16 * k + 1)), 1, grp="out_od", tag="end")
+            dma("y", ("od", 0, 256, 1, None), r("drow", p=(0, 128, 16)), 8, tag="end")
         scan(r("lsc"), r("cs16"), r("nsg"), A.add, A.max)
         tt(r("lqv"), r("lsc"), r("d64"), A.mult, off=bl)
         tt(r("lr"), r("cb"), r("lqv"), A.subtract)
@@ -350,18 +429,34 @@ def program(par, cm):
             copy(r("mrow"), mtab, off=r("mu"))
         else:
             act(r("mrow"), mtab, F.Copy, off=r("mu"))
-        if par["g_plain"][t]:
-            act(r("junk", 2048, 2304), r("mrow"), F.Sign, bias=col("sbi", 0), acc=r("gq"))
+        if par["g_plain"][t] == 2:
+            ts(r("junk", 2048, 2304), r("mrow"), pi16, None, A.is_gt)
+            reduce(r("gq"), r("junk", 2048, 2304), A.add)
+            copy(col("gu", 0), r("gq"))
         else:
-            act(r("junk", 2048, 2304), mtab, F.Sign, bias=col("sbi", 0), acc=r("gq"), off=r("mu"))
-        ts(col("gu", 0), r("gq"), 0.5, 128.0, A.mult, A.add)
-        act(r("junk", 2304, 2320), r("ttab", 0, 257), F.Identity, scale=1.0 / 32, acc=r("tau"), off=col("gu", 0))
-        copy(r("kr"), r("ktab", 0, 257), off=col("gu", 0))
-        reduce(r("kk"), r("kr"), A.min)
-        ts(r("over"), r("mrow"), r("tau"), None, A.is_gt)
-        ts(r("from"), r("mrow"), 1.0, r("tau"), A.add, A.is_gt)
-        scan(r("bnd"), r("over"), r("over"), A.add, A.max, init=r("kk"))
-        scan(r("cum"), r("from"), r("bnd"), A.add, A.min)
+            if par["g_plain"][t]:
+                act(r("junk", 2048, 2304), r("mrow"), F.Sign, bias=col("sbi", 0), acc=r("gq"))
+            else:
+                act(r("junk", 2048, 2304), mtab, F.Sign, bias=col("sbi", 0), acc=r("gq"), off=r("mu"))
+            ts(col("gu", 0), r("gq"), 0.5, 128.0, A.mult, A.add)
+        if par["tau_v"][t]:
+            ts(r("kt"), r("ttab", 0, 257), 1.0 / 32, None, A.mult, off=col("gu", 0))
+            reduce(r("tau"), r("kt"), A.add)
+        else:
+            act(r("kt"), r("ttab", 0, 257), F.Identity, scale=1.0 / 32, acc=r("tau"), off=col("gu", 0))
+        if par["over_a"][t]:
+            act(r("kr"), r("ttab", 0, 257), F.Identity, scale=1.0 / 32, bias=-1.0 / 16, acc=r("tal"), off=col("gu", 0))
+            act(r("over"), r("mrow"), F.Sign, scale=-1.0, bias=r("tau"), acc=r("kk"))
+            ts(r("from"), r("mrow"), r("tal"), 2.0, A.is_gt, A.mult)
+            scan(r("bnd"), r("ones"), r("over"), A.add, A.subtract, init=r("kk"))
+            scan(r("cum"), r("from"), r("bnd"), A.add, A.min, init=128.0)
+        else:
+            copy(r("kr"), r("ktab", 0, 257), off=col("gu", 0))
+            reduce(r("kk"), r("kr"), A.min)
+            ts(r("over"), r("mrow"), r("tau"), None, A.is_gt)
+            ts(r("from"), r("mrow"), 1.0, r("tau"), A.add, A.is_gt)
+            scan(r("bnd"), r("over"), r("over"), A.add, A.max, init=r("kk"))
+            scan(r("cum"), r("from"), r("bnd"), A.add, A.min)
         nv = par["seek_v"][t]
         for c in range(4):
             out = r("junk", 2560 + 256 * c, 2816 + 256 * c)
@@ -369,30 +464,45 @@ def program(par, cm):
                 ts(out, r("cum"), col("sj", c), None, A.is_lt)
                 reduce(col("sq", c), out, A.add, grp=g_("seek"))
             else:
-                act(out, r("cum"), F.Sign, bias=col("sbi", c), acc=col("sq", c), grp=g_("seek"))
+                act(out, r("cum"), F.Sign, bias=col("sb2" if par["over_a"][t] else "sbi", c), acc=col("sq", c), grp=g_("seek"))
         if nv:
             copy(r("hu", 0, nv), r("sq", 0, nv), grp=g_("hu"))
-        ts(r("hu", nv, 4), r("sq", nv, 4), -0.5, 128.0, A.mult, A.add, grp=g_("hu"))
+        if nv < 4:
+            ts(r("hu", nv, 4), r("sq", nv, 4), -0.5, 128.0, A.mult, A.add, grp=g_("hu"))
         tt(r("kc"), r("mrow"), r("tie"), A.add, off=r("hu"))
         line("wr", r("wr"), mtab, 4.0, off=r("hu"))
         scan(r("ko"), r("cso"), r("kc"), A.add, A.max)
-        for c in range(4):
-            ts(r("above", 64 * c, 64 * c + 64), r("kc"), o2, col("ko", 16 * c + 15), A.add, A.is_gt, grp=g_("rank"))
-        scan(r("rq"), r("keep"), r("above"), A.min, A.add)
-        copy(r("ru"), r("rq", 63, 256, 64))
-        op("v", "scatter", (r("hw"), r("ru"), r("wr")), [r("ru"), r("wr")], [r("hw")], 50 + 64 * cm["scatter"] * cyc)
+        if par["rank_v"][t]:
+            for c in range(4):
+                ts(r("above", 64 * c, 64 * c + 64), r("kc"), o2, col("ko", 16 * c + 15), A.add, A.is_gt, grp=g_("rank"))
+            scan(r("rq"), r("keep"), r("above"), A.min, A.add)
+            copy(r("ru"), r("rq", 63, 256, 64))
+        else:
+            act(r("kd"), r("kc"), F.Identity, bias=o2)
+            for c in range(4):
+                act(r("above", 64 * c, 64 * c + 64), r("kd"), F.Sign, scale=-1.0, bias=col("ko", 16 * c + 15),
+                    acc=col("rk", c), grp=g_("rank"))
+            ts(r("ru"), r("rk"), -0.5, 31.5, A.mult, A.add)
+        op("v", "scatter", (r("hw"), r("ru"), r("wr")), [r("ru"), r("wr")], [r("hw")], cm["pick"] + 64 * cm["scatter"] * cyc)
         scan(r("h4"), r("cs4"), r("hw"), A.add, A.max)
         ho, hi = r("hout", 16 * t, 16 * t + 16), r("hin", 16 * t, 16 * t + 16)
         ts(ho, r("h4", 3, 64, 4), jm, -6144.0, A.add, A.add)
         send(hi, ho, "arh%d" % t, 4, "h%d" % t)
-        parts, n = par["layer"][t], 512 // par["pieces"][t]
+        parts, n = par["layer"][t], int(512 / par["pieces"][t])
         for h in range(2):
-            win = xr(t, 0, XN + 256 + 512 * h)
-            for a in range(512 * h, 512 * h + 512, n):
-                act(r("ma", a, a + n), win, F.Copy, off=r("a4", a // 16, (a + n) // 16))
-                tt(r("mb", a, a + n), win, r("ma", a, a + n), A.max, off=r("b4", a // 16, (a + n) // 16))
+            win = xr(t, 0, XN + 256 + 512 * max(h, n // 1024))
+            for a in range(512 * h, 512 * h + 512 * (n < 1024 or h == 0), n):
+                la, lb = r("a4", a // 16, (a + n) // 16), r("b4", a // 16, (a + n) // 16)
+                if par["pair"][t][h]:
+                    act(r("ma", 2 * a, 2 * a + 2 * n, 2), win, F.Copy, off=la)
+                    act(r("ma", 2 * a + 1, 2 * a + 2 * n, 2), win, F.Copy, off=lb)
+                    scan(r("mb", 2 * a, 2 * a + 2 * n), r("anew", 0, 2 * n), r("ma", 2 * a, 2 * a + 2 * n), A.add, A.max)
+                else:
+                    act(r("ma", 2 * a, 2 * a + n), win, F.Copy, off=la)
+                    tt(r("mb", 2 * a + 1, 2 * a + 2 * n, 2), win, r("ma", 2 * a, 2 * a + n), A.max, off=lb)
             for e in range(4):
-                tt(r("mm", 512 * h + e, 512 * h + 512, 4), win, r("mb", 512 * h + 128 * e, 512 * h + 128 * e + 128), A.add,
+                a = 1024 * h + 256 * e
+                tt(r("mm", 512 * h + e, 512 * h + 512, 4), win, r("mb", a + 1, a + 256, 2), A.add,
                    off=r("d4", 16 * e + 8 * h, 16 * e + 8 * h + 8), grp=g_("m%d" % (h * (parts - 1))))
         n = P // parts
         for h in range(parts):
@@ -401,7 +511,7 @@ def program(par, cm):
             quant(qm, sm, r("mm", a, b))
             old, new = xr(t, XN + a, XN + b), xr(t + 1, XN + a, XN + b)
             how = par["add"][t][h]
-            if how == "g":
+            if how == "g" and new != old:
                 dma("y", new, old, n)
             for k in range(4):
                 z, out = r("pz", 512 * k, 512 * k + n), r("rz", a + k, b, 4)
@@ -414,7 +524,7 @@ def program(par, cm):
                 if how == "k":
                     tt(xr(t + 1, XN + a + k, XN + b, 4), xr(t, XN + a + k, XN + b, 4), out, A.add, grp=g_("add%d" % h))
             if how == "g":
-                dma("g", new, r("rz", a, b), 3 * n, add=True)
+                dma("g", new, r("rz", a, b), 1.5 * n, add=True)
         if t + 1 < R:
             quant_nodes(t + 1)
         lq, ls = r("lq", 256 * t, 256 * t + 256), r("ls", 256 * t, 256 * t + 256)
@@ -473,14 +583,43 @@ def graph(ops):
     return members
 
 
-def lay(ops, pre, post, rank, wake, back, alone=False):
-    n = len(ops)
+def steps(par, cm):
+    ops = program(par, cm)
+    graph(ops)
+    near = lambda a, b: a["q"] == b["q"] and a["cls"] == "c"
+    return [(o["q"], o["hold"], o["cost"], o["data"], o["cls"],
+             [(j, cm["near" if near(ops[j], o) else "far"] if o["q"] else 0.0) for j in sorted(o["deps"])]) for o in ops]
+
+
+def replay(calls, order, cm):
+    free, end, engines, first = {}, [0.0] * len(calls), 0.0, {"r": cm["first_r"], "s": cm["first_g"]}
+    for i in order:
+        q, hold, cost, data, cls, deps = calls[i]
+        t = free.get(q, 0.0)
+        if deps and cm["parked"]:
+            e, wake = max((end[j], w) for j, w in deps)
+            t = e + wake if e > t else t
+        elif deps:
+            t = max(t, max(end[j] + w for j, w in deps))
+        if data:
+            t += first.pop(cls, 0.0)
+            engines = max(engines, t + 0.7 * cost) + data
+            end[i] = engines + 0.3 * cost
+        else:
+            end[i] = t + cost
+        if q:
+            free[q] = t + hold
+    return max(end)
+
+
+def lay(calls, pre, post, rank, back, alone=False):
+    n = len(calls)
     left, ready, start, end, busy = [len(p) for p in pre], [0.0] * n, [0.0] * n, [0.0] * n, {}
     open_ = set(i for i in range(n) if not left[i])
     while open_:
-        i = min(open_, key=lambda j: (rank[j], j))
+        i = min(open_, key=lambda j: rank[j])
         open_.remove(i)
-        q, hold, cost = ops[i]["q"], ops[i]["hold"], ops[i]["cost"]
+        q, hold, cost = calls[i]
         lag = cost - hold if back else 0.0
         t = ready[i] + lag
         if q and not alone:
@@ -494,43 +633,71 @@ def lay(ops, pre, post, rank, wake, back, alone=False):
                     t = b
             spans.insert(k, (t, t + hold))
         start[i], end[i] = t - lag, t - lag + cost
-        for u in post[i]:
-            ready[u] = max(ready[u], end[i] + (wake if q else 0.0))
+        for u, wake in post[i]:
+            ready[u] = max(ready[u], end[i] + wake)
             left[u] -= 1
             if not left[u]:
                 open_.add(u)
     return start, end
 
 
-def arrange(ops, wake, passes, shake):
-    n = len(ops)
-    deps, users = [sorted(o["deps"]) for o in ops], [[] for _ in ops]
-    for i in range(n):
-        for j in deps[i]:
-            users[j].append(i)
-    way = lay(ops, users, deps, [-i for i in range(n)], wake, True, True)[1]
-    best, z = None, 1
-    for _ in range(passes):
+def arrange(par, z=1):
+    guesses = [(steps(par, cm), cm) for cm in GUESSES]
+    n, shake = len(guesses[0][0]), par["shake"]
+    calls, last, deps = [], list(range(n)), []
+    for i, (q, hold, cost, data, cls, d) in enumerate(guesses[0][0]):
+        calls.append((q, hold, 0.7 * cost if data else cost))
+    for i, (q, hold, cost, data, cls, d) in enumerate(guesses[0][0]):
+        if data:
+            last[i] = len(calls)
+            calls.append(("engines", data, data + 0.3 * cost))
+    deps = ([[(last[j], w * par["soft"]) for j, w in c[5]] for c in guesses[0][0]]
+            + [[(i, 0.0)] for i in range(n) if last[i] != i])
+    users = [[] for _ in calls]
+    for i, d in enumerate(deps):
+        for j, w in d:
+            users[j].append((i, w))
+    way = lay(calls, users, deps, [-i for i in range(len(calls))], True, True)[1]
+    best = None
+    for _ in range(par["passes"]):
         z = (z * 1103515245 + 12345) % 2147483648
         rank, mid = [], max(way) * z / 2147483648
         for w in way:
             z = (z * 1103515245 + 12345) % 2147483648
             rank.append(shake * (z / 2147483648 if abs(w - mid) < 2 * shake else 0.5) - w)
-        start, end = lay(ops, deps, users, rank, wake, False)
-        late = lay(ops, users, deps, [-e for e in end], wake, True)[1]
-        start, end = lay(ops, deps, users, [-e for e in late], wake, False)
-        if best is None or max(end) <= best[0]:
-            best, way = (max(end), sorted(range(n), key=lambda i: (start[i], i))), late
-    return best[1]
+        start, end = lay(calls, deps, users, rank, False)
+        late = lay(calls, users, deps, [-e for e in end], True)[1]
+        start, end = lay(calls, deps, users, [-e for e in late], False)
+        order = sorted(range(n), key=lambda i: (start[i], i))
+        time = sum(replay(c, order, cm) / cm["cyc"] for c, cm in guesses)
+        if best is None or time <= best[0]:
+            best, way = (time, order), late
+    time, order = best
+    needs = [set(j for j, w in c[5]) for c in guesses[0][0]]
+    for _ in range(par["swaps"]):
+        z = (z * 1103515245 + 12345) % 2147483648
+        a = (z >> 8) % n
+        b, hops = a, 1 + (z >> 20) % par["reach"]
+        while hops and b + 1 < n:
+            b += 1
+            hops -= calls[order[b]][0] == calls[order[a]][0]
+        if hops:
+            continue
+        if z >> 19 & 1 and not any(order[a] in needs[k] for k in order[a + 1:b + 1]):
+            new = order[:a] + order[a + 1:b + 1] + [order[a]] + order[b + 1:]
+        elif not any(k in needs[order[b]] for k in order[a:b]):
+            new = order[:a] + [order[b]] + order[a:b] + order[b + 1:]
+        else:
+            continue
+        t = sum(replay(c, new, cm) / cm["cyc"] for c, cm in guesses)
+        if t <= time:
+            time, order = t, new
+    return order
 
 
-def plan(par):
-    ops = program(par, COSTS)
-    members = graph(ops)
-    order = arrange(ops, COSTS["wake"], par["passes"], par["shake"])
-    n = len(ops)
+def waits(ops, members, order):
     place = {i: k for k, i in enumerate(order)}
-    known, at = {}, [0] * n
+    known, at = {}, [0] * len(ops)
     for i in order:
         o = ops[i]
         o["waits"] = []
@@ -544,6 +711,14 @@ def plan(par):
                     k |= 1 << m | at[m]
         known[o["q"]] = k
         at[i] = k
+    return at
+
+
+def plan(par):
+    ops = program(par, COSTS)
+    members = graph(ops)
+    order = arrange(par)
+    at = waits(ops, members, order)
     waited = set(w for o in ops for w in o["waits"])
     pools = {c: [] for c in NPOOL}
     sems = {}
@@ -576,6 +751,8 @@ def plan(par):
     return ops, order, sems
 
 
+USED = set(x[0] for o in program(PARAMS, COSTS) for x in o["reads"] + o["writes"]) | {"lq", "ls", "hin"}
+SCRATCH = {k: v for k, v in BUFFERS.items() if k in USED}
 PLAN = []
 
 
@@ -596,7 +773,7 @@ def rank_program(g, core, T, topo):
         if not isinstance(x, tuple):
             return x
         name, a, b, s, p = x
-        rows = slice(None) if p is None else slice(p[0], p[1])
+        rows = slice(None) if p is None else slice(*p)
         v = T[name][rows, a:b] if s == 1 else T[name][rows, a:b:s]
         return v.indirect(ap(off)) if off else v
 

from concourse.mybir import dt, AluOpType, AxisListType, ActivationFunctionType

A = AluOpType
F = ActivationFunctionType
C, E, P, R = 320, 64, 256, 3
X0 = 16
XN = X0 + 4 * E
XW = X0 + 4 * C
UNIT = 2.0 ** -19
BASE = 160000.0
MAGIC = 1.5 * 2.0 ** 35
TINY = 1e-37
Q4, U8, U16, F32, BF, I32 = "float8_e4m3fn_x4", "uint8", "uint16", "float32", "bfloat16", "int32"
BYTES = {Q4: 4, U8: 1, U16: 2, F32: 4, BF: 2, I32: 4}
BANKS = ("pz", "pc", "pd")


def sb(n, d):
    return ("sbuf", [128, n], d)


BUFFERS = {
    "xs": sb(4 * XW, BF), "ub": sb(512, BF), "vb": sb(512, BF), "pab": sb(32, I32),
    "wq": sb(512, Q4), "wp": sb(512, U8),
    "qu": sb(128, Q4), "su": sb(128, U8), "qup": sb(384, Q4), "sup": sb(384, U8),
    "qv": sb(128, Q4), "sv": sb(128, U8), "qc": sb(512, Q4), "sc": sb(512, U8),
    "qx": sb(4 * C, Q4), "sx": sb(4 * C, U8),
    "qm": sb(256, Q4), "sm": sb(256, U8), "lq": sb(768, Q4), "ls": sb(768, U8),
    "hout": sb(48, U16), "hin": sb(48, U16),
    "pi": sb(2, I32), "pj": sb(8, I32), "pf": sb(8, F32), "ps": sb(10, F32),
    "k64": sb(64, F32), "sf": sb(4, F32), "cf": sb(4, F32), "thr": sb(4, F32), "own": sb(192, F32),
    "lsa": sb(4, F32), "lbi": sb(4, F32), "cji": sb(64, F32), "kd": sb(64, F32), "rk": sb(4, F32),
    "ra": sb(64, F32), "oa": sb(64, F32), "eq0": sb(64, F32), "thr0": sb(256, F32), "gone": sb(256, BF), "side": sb(448, F32),
    "df": sb(64, F32), "dcon": sb(64, F32), "l3": sb(4, U16), "tal": sb(1, F32), "sb2": sb(4, F32), "ones": sb(256, BF),
    "cj": sb(64, F32), "y4": sb(64, F32), "f1": sb(64, F32), "cs4": sb(64, F32),
    "y16": sb(256, BF), "e1": sb(256, BF), "cs16": sb(256, BF), "ki": sb(36, F32),
    "mtab": sb(272, BF), "ttab": sb(272, BF), "ktab": sb(272, BF), "sbi": sb(4, F32), "sj": sb(4, F32),
    "tie": sb(64, F32), "cso": sb(64, F32), "keep": sb(256, BF), "ebig": sb(528, BF), "gt": sb(304, BF),
    "ul": sb(24, U16), "kl": sb(20, U16),
    "abl": sb(32, U16), "a4": sb(64, U16), "a4x": sb(16, F32), "dd": sb(16, F32), "econ": sb(64, F32),
    "a4f": sb(64, F32), "d64": sb(64, F32), "c1": sb(64, F32), "cb": sb(64, F32),
    "l0": sb(64, F32), "lost": sb(192, BF), "nsg": sb(256, BF), "tw": sb(336, F32), "ga": sb(192, F32), "gb": sb(192, F32),
    "tr": sb(544, F32), "g1": sb(64, F32), "val": sb(64, F32), "loff": sb(64, U16), "ds": sb(64, F32),
    "d4": sb(64, U16), "dl": sb(16, U16), "drow": sb(256, F32),
    "lsc": sb(256, BF), "lqv": sb(64, F32), "lr": sb(64, F32), "b4": sb(64, U16),
    "ma": sb(2048, BF), "mb": sb(2048, BF), "anew": sb(1024, BF), "kt": sb(16, F32), "mm": sb(1024, BF), "rz": sb(1024, F32),
    "junk": sb(14 * 256, BF), "hs": sb(8, F32), "hh": sb(8, F32), "lo": sb(8, F32), "mu": sb(16, U16),
    "mrow": sb(256, BF), "gq": sb(1, F32), "gu": sb(2, U16), "tau": sb(1, F32), "kr": sb(16, F32), "kk": sb(1, F32),
    "over": sb(256, BF), "from": sb(256, BF), "bnd": sb(256, BF), "cum": sb(256, BF), "sq": sb(4, F32), "hu": sb(4, U16),
    "kc": sb(64, F32), "ko": sb(64, F32), "wr": sb(64, F32), "above": sb(256, BF), "rq": sb(256, BF), "ru": sb(4, U16),
    "hw": sb(64, F32), "h4": sb(64, F32), "dx": sb(1024, BF), "ys": sb(C, F32),
    "pz": ("psum", [128, 2048], F32), "pc": ("psum", [128, 1024], F32), "pd": ("psum", [128, 1024], F32),
}
SCRATCH = dict(BUFFERS)
NPOOL = {"c": 100, "h": 30, "s": 12}
SEMAPHORES = (["sent"] + ["arq%d" % t for t in range(R)] + ["arh%d" % t for t in range(R)]
              + ["%s%d" % (k, i) for k in ("c", "h", "s") for i in range(NPOOL[k])])

PARAMS = {"cuts": (2, 2, 2), "layer": (2, 2, 2), "add": ("gk", "kk", "gk"), "relu_v": (0, 0, 0), "pieces": (1, 2, 1),
          "mrow_v": (0, 0, 1), "g_plain": (0, 0, 0), "hist_v": (0, 0, 4), "seek_v": (0, 0, 0), "dx_v": (0, 0, 0),
          "ga3_v": (0, 0, 0), "lost_v": (1, 1, 1), "rank_v": (0, 0, 0), "tau_v": (0, 0, 0), "l3_v": (1, 1, 1),
          "pair": ((0, 0), (0, 0), (0, 0)), "place": (0, 1, 1, 1), "gload": "v",
          "both": 1, "few": 1, "d_pick": (0, 0, 0), "over_a": (1, 1, 1), "loads": "y", "xload": ((0, 192), (192, 320)),
          "scalar": ("cs16", "gt1", "gt2", "d64", "ra", "sup0", "sup1", "wr", "ys0", "own2", "own3", "tie", "cso", "cs4",
                     "c1", "sbi", "jm", "o1", "o2", "ni", "cj", "i4", "b15", "sb2", "dcon"),
          "soft": 1.0, "reach": 2, "swaps": 9000, "passes": 1800, "shake": 1500.0}
COSTS = {"cyc": 0.83, "gather": 1.56, "scatter": 3.8, "pe": 0.7, "least": 88.0, "least_a": 95.0, "call": 0.0,
         "call_a": 0.0, "call_t": 0.0, "pick": 100.0, "pick_a": 65.0, "psum": 0.0, "lag": {"v": 50.0, "a": 150.0, "t": 70.0},
         "near": 150.0, "far": 150.0, "parked": True, "dma": 1050.0, "gdma": 2400.0, "remote": 1200.0, "issue": 160.0,
         "gissue": 300.0, "rissue": 100.0, "row": 0.0, "byte": 0.05, "add": 1.0, "away": 1.5, "first_r": 400.0,
         "first_g": 500.0}
STEADY = dict(COSTS, gather=1.65, least=102.0, least_a=175.0, pick=62.0, pick_a=105.0, lag={"a": 130.0}, near=155.0,
              far=125.0, parked=False, dma=500.0, gdma=1850.0, remote=1700.0, add=2.2, rissue=50.0, first_r=1300.0)
GUESSES = [STEADY, COSTS,
           dict(COSTS, least=75.0, least_a=175.0, pick=105.0, pick_a=90.0, lag={"v": 70.0, "a": 255.0}, near=50.0,
                far=50.0, dma=1750.0, gdma=2300.0, remote=1500.0, issue=30.0, rissue=250.0, byte=0.04, add=1.9,
                first_r=1000.0),
           dict(STEADY, gather=1.5, least=65.0, call=18.0, least_a=64.0, pick=72.0, pick_a=95.0, lag={}, near=125.0,
                far=280.0, remote=500.0, dma=350.0, gdma=1650.0, issue=180.0, rissue=1200.0, add=2.5, first_r=0.0),
           dict(STEADY, cyc=1.12, gather=1.8, pick=85.0, pick_a=140.0, lag={"a": 180.0}, near=205.0, far=170.0,
                dma=700.0, gdma=2200.0, remote=2000.0)]


def r(name, a=0, b=None, s=1, p=None):
    return (name, a, SCRATCH[name][1][1] if b is None else b, s, p)


def bits(ref):
    name, a, b, s, p = ref
    if name in BANKS:
        a, b, s = a // 512 * 512, (b + 511) // 512 * 512, 1
    if s == 1:
        return (1 << b) - (1 << a)
    m = 0
    for c in range(a, b, s):
        m |= 1 << c
    return m


def width(ref):
    return len(range(ref[1], ref[2], ref[3]))


def narrow(*refs):
    return all(SCRATCH[x[0]][2] in (BF, U16) for x in refs)


def program(par, cm):
    ops = []
    cyc = cm["cyc"]

    def op(q, call, args, reads, writes, cost, hold=None, data=0.0, grp=None, cls="c", after=None, tag=None):
        reads = [x for x in reads if isinstance(x, tuple) and x[0] in SCRATCH]
        writes = [x for x in writes if x[0] in SCRATCH]
        if hold is None:
            hold, cost = cost, cost + cm["lag"].get(q, 0.0)
        ops.append({"q": q, "call": call, "args": args, "reads": reads, "writes": writes, "cost": cost, "hold": hold,
                    "data": data, "grp": grp, "cls": cls, "after": after, "tag": tag})

    def plain(out, ins):
        n = width(out) * (0.5 if narrow(out, *ins) else 1.0)
        return (max(cm["least"], n) + cm["call"] + cm["psum"] * any(x[0] in BANKS for x in ins)) * cyc

    def moved(x, factor):
        rows = 128 if x[4] is None else len(range(*x[4]))
        return -(-rows // 16) * (cm["row"] + width(x) * BYTES[SCRATCH[x[0]][2]] * cm["byte"] * factor)

    def gath(out):
        return cm["pick"] + width(out) * cm["gather"] * cyc

    def memset(out, v, **k):
        op("v", "memset", (out, v), [], [out], plain(out, []), **k)

    def copy(out, in_, off=None, **k):
        op("v", "copy", (out, in_, off), [in_, off], [out], gath(out) if off else plain(out, [in_]), **k)

    def ts(out, in0, s1, s2, o0, o1=None, off=None, **k):
        op("v", "ts", (out, in0, s1, s2, o0, o1, off), [in0, s1, s2, off], [out],
           gath(out) if off else plain(out, [in0]), **k)

    def tt(out, in0, in1, o, off=None, **k):
        bank = in0[0] in BANKS
        c = gath(out) if off else (max(cm["least"], (2 - bank) * width(out)) + cm["call"] + cm["psum"] * bank) * cyc
        op("v", "tt", (out, in0, in1, o, off), [in0, in1, off], [out], c, **k)

    def scan(out, d0, d1, o0, o1, init=0.0, **k):
        op("v", "scan", (out, d0, d1, init, o0, o1), [d0, d1, init], [out], plain(out, [d0, d1]), **k)

    def turn(out, in_, **k):
        op("v", "turn", (out, in_), [in_], [out], plain(out, [in_]), **k)

    def reduce(out, in_, o, **k):
        op("v", "reduce", (out, in_, o), [in_], [out], (max(cm["least"], width(in_)) + cm["call"]) * cyc, **k)

    def quant(q, s, in_, **k):
        op("v", "quant", (q, s, in_), [in_], [q, s], (12 + 0.22 * width(in_)) * cyc / 0.83, **k)

    def act(out, in_, f, scale=1.0, bias=None, acc=None, off=None, **k):
        c = (max(cm["least_a"], width(out)) + cm["call_a"] + cm["psum"] * (in_[0] in BANKS)) * cyc
        c = cm["pick_a"] + width(out) * cm["gather"] * cyc if off else c
        op("a", "act", (out, in_, f, scale, bias, acc, off), [in_, scale, bias, off],
           [out] + ([acc] if acc else []), c + (20 if acc else 0), **k)

    def line(name, out, in_, scale=1.0, bias=None, off=None, **k):
        if name in par["scalar"]:
            act(out, in_, F.Copy if bias is None else F.Identity, scale=scale, bias=bias, off=off, **k)
        elif bias is None and scale == 1.0:
            copy(out, in_, off=off, **k)
        elif bias is None:
            ts(out, in_, scale, None, A.mult, off=off, **k)
        elif scale == 1.0:
            ts(out, in_, bias, None, A.add, off=off, **k)
        else:
            ts(out, in_, scale, bias, A.mult, A.add, off=off, **k)

    def mm(out, lq, ls, rq, rs, **k):
        op("t", "mm", (out, lq, ls, rq, rs), [lq, ls, rq, rs], [out], (width(out) + 16) * cm["pe"] + cm["call_t"], **k)

    def iota(out, pat, base, mult=0, **k):
        op("g", "iota", (out, pat, base, mult), [], [out], (130 + 1.66 * width(out)) * cyc / 0.83, **k)

    def select(out, pat, cmp, fill, base, mult, **k):
        op("g", "select", (out, pat, cmp, fill, base, mult), [out], [out], (170 + 1.66 * width(out)) * cyc / 0.83, **k)

    def dma(q, out, in_, kb, add=False, **k):
        op(q, "dma", (out, in_, add), [in_] + ([out] if add else []), [out],
           cm["gdma" if q == "g" else "dma"], hold=cm["gissue" if q == "g" else "issue"],
           data=moved(out if out[0] in SCRATCH else in_, cm["add"] if add else 1.0),
           cls="s" if q == "g" else "h", **k)

    def send(out, in_, sem, kb, tag):
        op("g", "send", (out, in_, sem), [in_], [], cm["remote"], hold=cm["rissue"], data=moved(out, cm["away"]),
           cls="r", tag=tag)

    def arrive(sem, n, refs, tags):
        op(None, "arrive", (sem, n), [], refs, 0, cls="r", after=tags)

    def col(name, j):
        return r(name, j, j + 1)

    def xr(t, a, b, s=1):
        k = XW * par["place"][t]
        return r("xs", k + a, k + b, s)

    def quant_x(t, a, b):
        quant(r("qx", C * t + a, C * t + b), r("sx", C * t + a, C * t + b), xr(t, X0 + 4 * a, X0 + 4 * b))

    def qs(t, a, b):
        return r("qx", C * t + a, C * t + b), r("sx", C * t + a, C * t + b)

    def quant_nodes(t):
        n = P // par["cuts"][t]
        for a in range(E, C, n):
            quant_x(t, 0 if par["xload"][0][0] == 0 and t == 0 and a == E else a, a + n)

    lq_ = par["loads"]
    dma(lq_, r("ub"), ("u", 0, 512, 1, None), 128)
    for a, b in par["xload"]:
        dma("y", xr(0, X0 + 4 * a, X0 + 4 * b), ("x", 4 * a, 4 * b, 1, None), 128, tag="x" if b > E else None)
        if b == C:
            dma(lq_, r("pab", 0, 16), ("pa", 0, 16, 1, None), 8, grp="pab" if lq_ == "a" else None)
            dma(lq_, r("pab", 16, 32), ("pb", 0, 16, 1, None), 8, grp="pab" if lq_ == "a" else None)
    dma("g" if par["gload"] == "c" else "y", r("wq"), ("wc", 0, 2048, 1, None), 256, after=["x"])
    dma("g" if par["gload"] == "s" else "y", r("wp"), ("ws", 0, 512, 1, None), 64, after=["x"])
    dma("g" if par["gload"] == "v" else "y", r("vb"), ("v", 0, 512, 1, None), 128, after=["x"])

    iota(col("pi", 0), [[0, 1]], 0, 1)
    iota(r("k64"), [[1, 64]], 0)
    for j, m in enumerate((3, 4)):
        ts(col("pj", j), col("pi", 0), m, None, A.bitwise_and, grp="pj")
    copy(r("pf", 0, 2), r("pj", 0, 2))
    for j, m in ((2, 15), (3, 16), (4, 7)):
        ts(col("pj", j), col("pi", 0), m, None, A.bitwise_and, grp="pk")
    ts(col("pj", 5), col("pi", 0), 2, 3, A.logical_shift_right, A.bitwise_and, grp="pk")
    copy(r("pf", 2, 6), r("pj", 2, 6))
    lev, flag, pi16, p16, p8, sel = [col("pf", j) for j in range(6)]
    slope, odd, tb1, tbase, jm, i4, b15, o1, o2, ni = [col("ps", j) for j in range(10)]
    line("slope", slope, flag, -1025.0 * UNIT, 2052.0 * UNIT)
    ts(odd, flag, 4.0, p16, A.mult, A.not_equal)
    line("tb1", tb1, sel, 16.0, lev)
    line("tbase", tbase, odd, 272.0, tb1)
    line("jm", jm, sel, 2048.0, lev)
    line("i4", i4, pi16, 4.0)
    line("b15", b15, p8, 16.0, 15.0)
    line("o1", o1, pi16, -4.0, 61.0)
    line("o2", o2, pi16, -512.0, 7680.0)
    line("ni", ni, pi16, -1.0, -0.5)

    iota(r("ki", 0, 24), [[1, 3], [16, 8]], 0)
    iota(r("ki", 24, 32), [[4, 2], [64, 4]], 0)
    iota(r("ki", 32, 36), [[8, 2], [0, 2]], 0)
    copy(r("ul"), r("ki", 0, 24))
    trl, trh, lofl, cl, bl = [r("kl", 4 * j, 4 * j + 4) for j in range(5)]
    ts(r("kl", 0, 8), r("ki", 24, 32), tbase, None, A.add)
    ts(lofl, r("k64", 0, 4), i4, None, A.add)
    ts(cl, r("ki", 32, 36), p8, None, A.add)
    ts(bl, r("ki", 32, 36), 16.0, b15, A.mult, A.add)

    quant(r("qu"), r("su"), r("ub"))
    for a, b in ((0, 1), (1, R)):
        o, q = r("ul", 8 * a, 8 * b), r("qup", 128 * a, 128 * b)
        op("v", "pickq", (q, r("qu"), o), [r("qu"), o], [q], gath(q), grp="pick%d" % a)
        line("sup%d" % a, r("sup", 128 * a, 128 * b), r("su"), off=o, grp="pick%d" % a)
    for t in range(R):
        if t == 0 or par["place"][t] != par["place"][t - 1]:
            iota(xr(t, 0, X0), [[0, X0]], 0)
    quant_nodes(0)

    ts(r("sf"), r("k64", 0, 4), lev, slope, A.is_equal, A.mult, grp="sf")
    ts(r("cf"), r("k64", 0, 4), lev, BASE * UNIT, A.is_equal, A.mult, grp="sf")
    if any(par["lost_v"] + par["l3_v"]) and not par["few"]:
        ts(r("thr"), r("k64", 1, 5), lev, 1e29, A.is_equal, A.mult)
    if not all(par["lost_v"]) and not par["few"]:
        ts(r("lsa"), r("k64", 1, 5), lev, -1.0, A.not_equal, A.mult, grp="ls")
        ts(r("lbi"), r("k64", 1, 5), lev, None, A.is_equal, grp="ls")
    line("tw", r("tw", 0, 64), r("k64"), col("sf", 0), col("cf", 0))
    for l in range(1, 4):
        out = r("side", 64 * l, 64 * l + 64) if par["both"] and l > 1 else r("own", 64 * l - 64, 64 * l)
        line("own%d" % l, out, r("k64"), col("sf", l), col("cf", l))
    if par["both"]:
        iota(r("side", 384, 448), [[0, 64]], 0)
        for a, b, c in ((0, 4, 0), (4, 12, 16), (12, 20, 4), (20, 28, 24), (28, 32, 12)):
            copy(r("abl", a, b), r("pab", c, c + b - a))
    else:
        for a in range(0, 32, 32 if lq_ == "a" else 16):
            copy(r("abl", a, a + (32 if lq_ == "a" else 16)), r("pab", a, a + (32 if lq_ == "a" else 16)))
    tt(r("oa"), r("tw", 0, 64), r("own", 0, 64), A.max, off=r("abl", 0, 4))
    line("ra", r("ra"), r("tw", 0, 64), off=r("abl", 0, 4))
    tt(r("eq0"), r("tw", 0, 64), r("ra"), A.is_equal, off=r("abl", 4, 8) if par["both"] else r("abl", 16, 20))
    line("thr0", r("thr0", 0, 64), r("eq0"), 1e29)
    if par["few"]:
        ts(r("thr0", 64, 192), r("side", 128, 256) if par["both"] else r("own", 64, 192), 0.0, 1e29, A.is_gt, A.mult)
        iota(r("thr0", 192, 256), [[0, 64]], 0)
    iota(r("tw", 320, 336), [[0, 16]], 0)
    iota(r("cji"), [[0, 16], [256, 4]], int(4 - 2 * BASE))
    select(r("cji"), [[-1, 4], [0, 4], [1, 4]], A.not_equal, -8 * BASE, -1, 0)
    line("cj", r("cj"), r("cji"), UNIT)
    iota(r("y4"), [[0, 16], [2048, 4]], 0)

    iota(r("econ"), [[0, 2], [1, 4], [0, 8]], X0)
    ts(r("a4x"), r("pab", 0, 16), 4.0, None, A.mult)
    tt(r("dd"), r("pab", 16, 32), r("pab", 0, 16), A.subtract)
    tt(r("a4f"), r("a4x"), r("econ"), A.add, off=cl)
    copy(r("a4"), r("a4f"))
    line("d64", r("d64"), r("dd"), 2.0, off=cl)
    line("c1", r("c1"), r("d64"), o1)
    tt(r("cb"), r("c1"), r("a4f"), A.add)
    iota(r("y16"), [[0, 16], [1, 16]], 0)
    ts(r("e1"), r("y16"), pi16, 132.0, A.not_equal, A.mult)
    line("cs16", r("cs16"), r("e1"), 1.0, -128.0)

    iota(r("gt", 0, 112), [[0, 112]], 0)
    ts(r("gt", 33, 49), r("k64", 0, 16), pi16, None, A.is_equal, grp="gt")
    ts(r("gt", 49, 65), r("k64", 0, 16), pi16, 4096.0, A.is_equal, A.mult, grp="gt")
    line("gt1", r("gt", 97, 161), r("gt", 33, 97))
    line("gt2", r("gt", 161, 289), r("gt", 33, 161))
    iota(r("mtab", 0, 257), [[1, 257]], 0)
    iota(r("ttab", 0, 64), [[0, 64]], 1)
    iota(r("ttab", 64, 257), [[0, 193]], 33)
    if not all(par["over_a"]):
        iota(r("ktab", 0, 64), [[-1, 64]], 64)
        iota(r("ktab", 64, 257), [[0, 193]], 64)
    line("sbi", r("sbi"), r("k64", 0, 64, 16), -1.0, ni)
    if any(par["over_a"]):
        line("sb2", r("sb2"), r("sbi"), 2.0, -128.0)
        iota(r("ones"), [[0, 256]], 1)
    if any(par["d_pick"]):
        ts(r("l3"), r("k64", 3, 7), 3.0, i4, A.min, A.add)
        iota(r("df"), [[1, 4], [0, 16]], X0 - 4)
        line("dcon", r("dcon"), r("df"), UNIT)
    if any(par["seek_v"]):
        line("sj", r("sj"), r("sbi"), -1.0)
    line("tie", r("tie"), r("k64"), -1.0 / 64, 63.0 / 64)
    line("cso", r("cso"), r("e1", 0, 64), 128.0, -16384.0)
    if any(par["rank_v"]) or not par["few"]:
        iota(r("keep"), [[0, 4], [64, 64]], 0)
    if any(any(x) for x in par["pair"]):
        iota(r("anew", 0, 256), [[0, 128], [1, 2]], -1)
        for a in range(768, -1, -256):
            act(r("anew", a, a + 256), r("anew", 0, 256), F.Copy, scale=1e29)
    ts(r("f1"), r("y4"), lev, jm, A.add, A.not_equal)
    line("cs4", r("cs4"), r("f1"), 10240.0, -8192.0)

    memset(r("ebig"), 1.0)
    select(r("ebig"), [[1, 528]], A.is_equal, 0.0, -3, -4)
    for b in range(4):
        quant(r("qc", 128 * b, 128 * b + 128), r("sc", 128 * b, 128 * b + 128), r("ebig", 3 - b, 515 - b))
    quant(r("qv"), r("sv"), r("vb"))

    for t in range(R):
        g_ = lambda s: "%s_%d" % (s, t)
        up = r("qup", 128 * t, 128 * t + 128), r("sup", 128 * t, 128 * t + 128)
        n = P // par["cuts"][t]
        score = lambda a, b: r("pc", a // n * 512 + a % n, a // n * 512 + a % n + b - a)
        for a in range(0, P, n):
            mm(score(a, a + n), *up, *qs(t, E + a, E + a + n))
            if par["few"]:
                out = r("side", 2 * a, 2 * a + n) if par["both"] else r("gone", a, a + n)
                tt(out, score(a, a + n), r("thr0", a, a + n), A.is_lt)
            for k in range(a // 64, (a + n) // 64 * (1 - par["few"])):
                out, s = r("lost", 64 * k - 64, 64 * k), score(64 * k, 64 * k + 64)
                if k == 0:
                    tt(r("l0"), s, r("thr0", 0, 64), A.is_lt)
                elif par["lost_v" if k < 3 else "l3_v"][t]:
                    ts(out, s, col("thr", k), None, A.is_lt)
                elif k < 3:
                    act(out, s, F.Sign, scale=col("lsa", k), bias=col("lbi", k))
            act(r("nsg", a, a + n), score(a, a + n), F.Sign, scale=-1.0, bias=-TINY)
        if t or par["xload"][0][0]:
            quant_x(t, 0, 128)
        send(r("lq", 256 * t, 256 * t + 256), r("qx", C * t, C * t + 256), "arq%d" % t, 128, "q%d" % t)
        send(r("ls", 256 * t, 256 * t + 256), r("sx", C * t, C * t + 256), "arq%d" % t, 32, "q%d" % t)
        tt(r("tw", 64, 128), r("oa"), r("side" if par["both"] else "gone", 0, 64) if par["few"] else r("l0"), A.mult)
        for k in range(1, 4):
            win, a, b = r("tw", 0, 64 + 64 * k), 64 * k - 64, 64 * k
            la, lb = r("abl", 4 * k, 4 * k + 4), r("abl", 16 + 4 * k, 20 + 4 * k)
            if par["both"]:
                tt(r("ga", 0, 128), win, r("side", 128 * k - 64, 128 * k + 64), A.max, off=r("abl", 8 * k, 8 * k + 8))
                tt(r("tw", 128 + a, 128 + b), r("ga", 0, 64), r("ga", 64, 128), A.min)
            else:
                if k < 3:
                    tt(r("ga", a, b), win, r("own", a + 64, b + 64), A.max, off=la)
                elif par["ga3_v"][t]:
                    copy(r("ga", a, b), win, off=la)
                else:
                    act(r("ga", a, b), win, F.Copy, off=la)
                lost = r("lost", a, b) if k < 3 or par["l3_v"][t] else r("nsg", 192, 256)
                tt(r("gb", a, b), win, r("gone", a + 64, b + 64) if par["few"] else lost, A.max, off=lb)
                tt(r("tw", 128 + a, 128 + b), r("ga", a, b), r("gb", a, b), A.min)
            a, b, e = ((0, 128, 128), (128, 192, 192), (192, 256, 288))[k - 1]
            if par["few"] and k < 3:
                a, b, e = 0, 192 * (k - 1), 192
            if b:
                turn(r("tr", a, b), r("tw", 64 + a, 64 + b))
                turn(r("tr", 256 + a, 256 + e), r("tw", 48 + a, 48 + e))
        tt(r("g1"), r("tr"), r("cj"), A.add, off=trh)
        tt(r("val"), r("tr"), r("g1"), A.add, off=trl)
        scan(r("ds"), r("y4"), r("val"), A.min, A.max)
        if par["d_pick"][t]:
            tt(r("df"), r("ds"), r("dcon"), A.add, off=r("l3"))
            ts(r("d4"), r("df"), 1 / UNIT, None, A.mult)
        else:
            for e in range(4):
                ts(r("d4", 16 * e, 16 * e + 16), r("ds", 3, 64, 4), 1 / UNIT, float(X0 - 4 + e), A.mult, A.add)
        ts(r("loff"), r("val"), 0.25 / UNIT, None, A.mult, off=lofl)
        if t == R - 1:
            ts(r("dl"), r("ds", 3, 64, 4), 0.25 / UNIT, None, A.mult)
            act(r("drow"), r("mtab", 0, 257), F.Identity, bias=-1.0, off=r("dl"))
            dma("y", ("od", 0, 256, 1, None), r("drow", p=(0, 128, 16)), 8, tag="end")
        scan(r("lsc"), r("cs16"), r("nsg"), A.add, A.max)
        tt(r("lqv"), r("lsc"), r("d64"), A.mult, off=bl)
        tt(r("lr"), r("cb"), r("lqv"), A.subtract)
        copy(r("b4"), r("lr"))
        for j in range(4):
            for q in range(2):
                h, n = 2 * j + q, 256 - 64 * j
                out, win, off = r("junk", 256 * h, 256 * h + n), r("gt", 32 - 32 * q, 289 - 32 * q), r("loff", 20 * j, 16 * j + 16)
                if h >= 8 - par["hist_v"][t]:
                    copy(out, win, off=off)
                    reduce(col("hs", h), out, A.add, grp=g_("hist"))
                else:
                    act(out, win, F.Identity, acc=col("hs", h), off=off, grp=g_("hist"))
        ts(r("hh"), r("hs"), MAGIC, MAGIC, A.add, A.subtract)
        ts(r("mu", 1, 16, 2), r("hs"), 2.0 ** -12, None, A.mult)
        tt(r("lo"), r("hs"), r("hh"), A.subtract)
        copy(r("mu", 0, 16, 2), r("lo"))
        mtab = r("mtab", 0, 257)
        if par["mrow_v"][t]:
            copy(r("mrow"), mtab, off=r("mu"))
        else:
            act(r("mrow"), mtab, F.Copy, off=r("mu"))
        if par["g_plain"][t] == 2:
            ts(r("junk", 2048, 2304), r("mrow"), pi16, None, A.is_gt)
            reduce(r("gq"), r("junk", 2048, 2304), A.add)
            copy(col("gu", 0), r("gq"))
        else:
            if par["g_plain"][t]:
                act(r("junk", 2048, 2304), r("mrow"), F.Sign, bias=col("sbi", 0), acc=r("gq"))
            else:
                act(r("junk", 2048, 2304), mtab, F.Sign, bias=col("sbi", 0), acc=r("gq"), off=r("mu"))
            ts(col("gu", 0), r("gq"), 0.5, 128.0, A.mult, A.add)
        if par["tau_v"][t]:
            ts(r("kt"), r("ttab", 0, 257), 1.0 / 32, None, A.mult, off=col("gu", 0))
            reduce(r("tau"), r("kt"), A.add)
        else:
            act(r("kt"), r("ttab", 0, 257), F.Identity, scale=1.0 / 32, acc=r("tau"), off=col("gu", 0))
        if par["over_a"][t]:
            act(r("kr"), r("ttab", 0, 257), F.Identity, scale=1.0 / 32, bias=-1.0 / 16, acc=r("tal"), off=col("gu", 0))
            act(r("over"), r("mrow"), F.Sign, scale=-1.0, bias=r("tau"), acc=r("kk"))
            ts(r("from"), r("mrow"), r("tal"), 2.0, A.is_gt, A.mult)
            scan(r("bnd"), r("ones"), r("over"), A.add, A.subtract, init=r("kk"))
            scan(r("cum"), r("from"), r("bnd"), A.add, A.min, init=128.0)
        else:
            copy(r("kr"), r("ktab", 0, 257), off=col("gu", 0))
            reduce(r("kk"), r("kr"), A.min)
            ts(r("over"), r("mrow"), r("tau"), None, A.is_gt)
            ts(r("from"), r("mrow"), 1.0, r("tau"), A.add, A.is_gt)
            scan(r("bnd"), r("over"), r("over"), A.add, A.max, init=r("kk"))
            scan(r("cum"), r("from"), r("bnd"), A.add, A.min)
        nv = par["seek_v"][t]
        for c in range(4):
            out = r("junk", 2560 + 256 * c, 2816 + 256 * c)
            if c < nv:
                ts(out, r("cum"), col("sj", c), None, A.is_lt)
                reduce(col("sq", c), out, A.add, grp=g_("seek"))
            else:
                act(out, r("cum"), F.Sign, bias=col("sb2" if par["over_a"][t] else "sbi", c), acc=col("sq", c), grp=g_("seek"))
        if nv:
            copy(r("hu", 0, nv), r("sq", 0, nv), grp=g_("hu"))
        if nv < 4:
            ts(r("hu", nv, 4), r("sq", nv, 4), -0.5, 128.0, A.mult, A.add, grp=g_("hu"))
        tt(r("kc"), r("mrow"), r("tie"), A.add, off=r("hu"))
        line("wr", r("wr"), mtab, 4.0, off=r("hu"))
        scan(r("ko"), r("cso"), r("kc"), A.add, A.max)
        if par["rank_v"][t]:
            for c in range(4):
                ts(r("above", 64 * c, 64 * c + 64), r("kc"), o2, col("ko", 16 * c + 15), A.add, A.is_gt, grp=g_("rank"))
            scan(r("rq"), r("keep"), r("above"), A.min, A.add)
            copy(r("ru"), r("rq", 63, 256, 64))
        else:
            act(r("kd"), r("kc"), F.Identity, bias=o2)
            for c in range(4):
                act(r("above", 64 * c, 64 * c + 64), r("kd"), F.Sign, scale=-1.0, bias=col("ko", 16 * c + 15),
                    acc=col("rk", c), grp=g_("rank"))
            ts(r("ru"), r("rk"), -0.5, 31.5, A.mult, A.add)
        op("v", "scatter", (r("hw"), r("ru"), r("wr")), [r("ru"), r("wr")], [r("hw")], cm["pick"] + 64 * cm["scatter"] * cyc)
        scan(r("h4"), r("cs4"), r("hw"), A.add, A.max)
        ho, hi = r("hout", 16 * t, 16 * t + 16), r("hin", 16 * t, 16 * t + 16)
        ts(ho, r("h4", 3, 64, 4), jm, -6144.0, A.add, A.add)
        send(hi, ho, "arh%d" % t, 4, "h%d" % t)
        parts, n = par["layer"][t], int(512 / par["pieces"][t])
        for h in range(2):
            win = xr(t, 0, XN + 256 + 512 * max(h, n // 1024))
            for a in range(512 * h, 512 * h + 512 * (n < 1024 or h == 0), n):
                la, lb = r("a4", a // 16, (a + n) // 16), r("b4", a // 16, (a + n) // 16)
                if par["pair"][t][h]:
                    act(r("ma", 2 * a, 2 * a + 2 * n, 2), win, F.Copy, off=la)
                    act(r("ma", 2 * a + 1, 2 * a + 2 * n, 2), win, F.Copy, off=lb)
                    scan(r("mb", 2 * a, 2 * a + 2 * n), r("anew", 0, 2 * n), r("ma", 2 * a, 2 * a + 2 * n), A.add, A.max)
                else:
                    act(r("ma", 2 * a, 2 * a + n), win, F.Copy, off=la)
                    tt(r("mb", 2 * a + 1, 2 * a + 2 * n, 2), win, r("ma", 2 * a, 2 * a + n), A.max, off=lb)
            for e in range(4):
                a = 1024 * h + 256 * e
                tt(r("mm", 512 * h + e, 512 * h + 512, 4), win, r("mb", a + 1, a + 256, 2), A.add,
                   off=r("d4", 16 * e + 8 * h, 16 * e + 8 * h + 8), grp=g_("m%d" % (h * (parts - 1))))
        n = P // parts
        for h in range(parts):
            a, b = 4 * n * h, 4 * n * h + 4 * n
            qm, sm = r("qm", n * h, n * h + n), r("sm", n * h, n * h + n)
            quant(qm, sm, r("mm", a, b))
            old, new = xr(t, XN + a, XN + b), xr(t + 1, XN + a, XN + b)
            how = par["add"][t][h]
            if how == "g" and new != old:
                dma("y", new, old, n)
            for k in range(4):
                z, out = r("pz", 512 * k, 512 * k + n), r("rz", a + k, b, 4)
                mm(z, r("wq", 128 * k, 128 * k + 128), r("wp", 128 * k, 128 * k + 128), qm, sm)
                grp = None if how == "k" else g_("rz%d" % h)
                if k < par["relu_v"][t]:
                    ts(out, z, 0.0, 0.015625, A.max, A.mult, grp=grp)
                else:
                    act(out, z, F.Relu, scale=0.015625, grp=grp)
                if how == "k":
                    tt(xr(t + 1, XN + a + k, XN + b, 4), xr(t, XN + a + k, XN + b, 4), out, A.add, grp=g_("add%d" % h))
            if how == "g":
                dma("g", new, r("rz", a, b), 1.5 * n, add=True)
        if t + 1 < R:
            quant_nodes(t + 1)
        lq, ls = r("lq", 256 * t, 256 * t + 256), r("ls", 256 * t, 256 * t + 256)
        arrive("arq%d" % t, 2, [lq, ls], ["q%d" % t])
        for b in range(4):
            src = r("pd", 512 * (b % 2), 512 * (b % 2) + 256)
            mm(src, r("qc", 128 * b, 128 * b + 128), r("sc", 128 * b, 128 * b + 128), lq, ls)
            if b < par["dx_v"][t]:
                copy(r("dx", b, 1024, 4), src)
            else:
                act(r("dx", b, 1024, 4), src, F.Copy)
        arrive("arh%d" % t, 1, [hi], ["h%d" % t])
        tt(xr(t + 1, X0, XN), r("dx"), xr(t, X0, XN), A.max, off=hi)

    for h, (a, b) in enumerate(((128, C), (0, 128))):
        quant_x(R, a, b)
        q, s = qs(R, a, b)
        mm(r("pc", 512 * h, 512 * h + b - a), r("qv"), r("sv"), q, s)
        line("ys%d" % h, r("ys", a, b), r("pc", 512 * h, 512 * h + b - a))
        dma("y", ("oc", 4 * a, 4 * b, 1, None), q, (b - a) // 2, grp="out%d" % h, tag="end")
        for k in range(4):
            dma("yaya"[k] if h else "y", ("osc", a, b, 1, (4 * k, 4 * k + 4)), s[:4] + ((32 * k, 32 * k + 4),), 1,
                grp="out%d" % h, tag="end")
        dma("a" if h else "y", ("y", a, b, 1, None), r("ys", a, b), (b - a) // 2, grp="out%d" % h, tag="end")
    op("y", "end", (), [], [], 0, after=["end"])
    return ops


def graph(ops):
    members = {}
    for i, o in enumerate(ops):
        o["key"] = o["grp"] if o["grp"] else "op%d" % i
        members.setdefault(o["key"], []).append(i)
    seen = {}
    for i, o in enumerate(ops):
        deps = set()
        rd = [(x[0], bits(x)) for x in o["reads"]]
        wr = [(x[0], bits(x)) for x in o["writes"]]
        for name, m in rd:
            deps.update(j for j, w, mj in seen.get(name, [])
                        if mj & m and (w or name in BANKS and ops[j]["q"] != o["q"]))
        for name, m in wr:
            deps.update(j for j, w, mj in seen.get(name, []) if mj & m)
        for name, m in rd:
            seen.setdefault(name, []).append((i, False, m))
        for name, m in wr:
            seen.setdefault(name, []).append((i, True, m))
        if o["after"]:
            deps.update(j for j in range(i) if ops[j]["tag"] in o["after"])
        o["deps"] = set(j for j in deps if ops[j]["key"] != o["key"])
    for o in ops:
        full = set()
        for j in o["deps"]:
            full.update(members[ops[j]["key"]])
        o["deps"] = full
    return members


def steps(par, cm):
    ops = program(par, cm)
    graph(ops)
    near = lambda a, b: a["q"] == b["q"] and a["cls"] == "c"
    return [(o["q"], o["hold"], o["cost"], o["data"], o["cls"],
             [(j, cm["near" if near(ops[j], o) else "far"] if o["q"] else 0.0) for j in sorted(o["deps"])]) for o in ops]


def replay(calls, order, cm):
    free, end, engines, first = {}, [0.0] * len(calls), 0.0, {"r": cm["first_r"], "s": cm["first_g"]}
    for i in order:
        q, hold, cost, data, cls, deps = calls[i]
        t = free.get(q, 0.0)
        if deps and cm["parked"]:
            e, wake = max((end[j], w) for j, w in deps)
            t = e + wake if e > t else t
        elif deps:
            t = max(t, max(end[j] + w for j, w in deps))
        if data:
            t += first.pop(cls, 0.0)
            engines = max(engines, t + 0.7 * cost) + data
            end[i] = engines + 0.3 * cost
        else:
            end[i] = t + cost
        if q:
            free[q] = t + hold
    return max(end)


def lay(calls, pre, post, rank, back, alone=False):
    n = len(calls)
    left, ready, start, end, busy = [len(p) for p in pre], [0.0] * n, [0.0] * n, [0.0] * n, {}
    open_ = set(i for i in range(n) if not left[i])
    while open_:
        i = min(open_, key=lambda j: rank[j])
        open_.remove(i)
        q, hold, cost = calls[i]
        lag = cost - hold if back else 0.0
        t = ready[i] + lag
        if q and not alone:
            spans = busy.setdefault(q, [])
            k = len(spans)
            for j, (a, b) in enumerate(spans):
                if b > t:
                    if t + hold <= a:
                        k = j
                        break
                    t = b
            spans.insert(k, (t, t + hold))
        start[i], end[i] = t - lag, t - lag + cost
        for u, wake in post[i]:
            ready[u] = max(ready[u], end[i] + wake)
            left[u] -= 1
            if not left[u]:
                open_.add(u)
    return start, end


def arrange(par, z=1):
    guesses = [(steps(par, cm), cm) for cm in GUESSES]
    n, shake = len(guesses[0][0]), par["shake"]
    calls, last, deps = [], list(range(n)), []
    for i, (q, hold, cost, data, cls, d) in enumerate(guesses[0][0]):
        calls.append((q, hold, 0.7 * cost if data else cost))
    for i, (q, hold, cost, data, cls, d) in enumerate(guesses[0][0]):
        if data:
            last[i] = len(calls)
            calls.append(("engines", data, data + 0.3 * cost))
    deps = ([[(last[j], w * par["soft"]) for j, w in c[5]] for c in guesses[0][0]]
            + [[(i, 0.0)] for i in range(n) if last[i] != i])
    users = [[] for _ in calls]
    for i, d in enumerate(deps):
        for j, w in d:
            users[j].append((i, w))
    way = lay(calls, users, deps, [-i for i in range(len(calls))], True, True)[1]
    best = None
    for _ in range(par["passes"]):
        z = (z * 1103515245 + 12345) % 2147483648
        rank, mid = [], max(way) * z / 2147483648
        for w in way:
            z = (z * 1103515245 + 12345) % 2147483648
            rank.append(shake * (z / 2147483648 if abs(w - mid) < 2 * shake else 0.5) - w)
        start, end = lay(calls, deps, users, rank, False)
        late = lay(calls, users, deps, [-e for e in end], True)[1]
        start, end = lay(calls, deps, users, [-e for e in late], False)
        order = sorted(range(n), key=lambda i: (start[i], i))
        time = sum(replay(c, order, cm) / cm["cyc"] for c, cm in guesses)
        if best is None or time <= best[0]:
            best, way = (time, order), late
    time, order = best
    needs = [set(j for j, w in c[5]) for c in guesses[0][0]]
    for _ in range(par["swaps"]):
        z = (z * 1103515245 + 12345) % 2147483648
        a = (z >> 8) % n
        b, hops = a, 1 + (z >> 20) % par["reach"]
        while hops and b + 1 < n:
            b += 1
            hops -= calls[order[b]][0] == calls[order[a]][0]
        if hops:
            continue
        if z >> 19 & 1 and not any(order[a] in needs[k] for k in order[a + 1:b + 1]):
            new = order[:a] + order[a + 1:b + 1] + [order[a]] + order[b + 1:]
        elif not any(k in needs[order[b]] for k in order[a:b]):
            new = order[:a] + [order[b]] + order[a:b] + order[b + 1:]
        else:
            continue
        t = sum(replay(c, new, cm) / cm["cyc"] for c, cm in guesses)
        if t <= time:
            time, order = t, new
    return order


def waits(ops, members, order):
    place = {i: k for k, i in enumerate(order)}
    known, at = {}, [0] * len(ops)
    for i in order:
        o = ops[i]
        o["waits"] = []
        if o["q"] is None:
            continue
        k = known.get(o["q"], 0)
        for j in sorted(o["deps"], key=lambda j: -place[j]):
            if not k >> j & 1 and ops[j]["call"] != "send":
                o["waits"].append(ops[j]["key"])
                for m in members[ops[j]["key"]]:
                    k |= 1 << m | at[m]
        known[o["q"]] = k
        at[i] = k
    return at


def plan(par):
    ops = program(par, COSTS)
    members = graph(ops)
    order = arrange(par)
    at = waits(ops, members, order)
    waited = set(w for o in ops for w in o["waits"])
    pools = {c: [] for c in NPOOL}
    sems = {}
    for i in order:
        o = ops[i]
        key = o["key"]
        if key in sems or key not in waited:
            continue
        if o["call"] == "arrive":
            sems[key] = (o["args"][0], -o["args"][1])
            continue
        ms = members[key]
        common = -1
        for m in ms:
            common &= at[m]
        pool = pools[o["cls"]]
        slot = None
        for s in pool:
            if s[1] & common == s[1]:
                slot = s
                break
        if slot is None:
            slot = ["%s%d" % (o["cls"], len(pool)), 0, 0]
            pool.append(slot)
            assert len(pool) <= NPOOL[o["cls"]]
        for m in ms:
            slot[1] |= 1 << m
        slot[2] += len(ms) * (1 if o["cls"] == "c" else 16)
        sems[key] = (slot[0], slot[2])
    return ops, order, sems


USED = set(x[0] for o in program(PARAMS, COSTS) for x in o["reads"] + o["writes"]) | {"lq", "ls", "hin"}
SCRATCH = {k: v for k, v in BUFFERS.items() if k in USED}
PLAN = []


def rank_program(g, core, T, topo):
    rank = T.rank_of(core)
    if rank is None:
        return
    if not PLAN:
        PLAN.append(plan(PARAMS))
    ops, order, sems = PLAN[0]
    n = len(T.cores)
    nxt, prv = T.cores[(rank + 1) % n], T.cores[(rank - 1) % n]
    rid, pid = topo.addr(nxt)[:2]
    mask, out_engines, in_engines = topo.mask(core, nxt), len(topo.engines(core, nxt)), len(topo.engines(prv, core))
    queue = {"g": g, "v": g.vector, "a": g.scalar, "t": g.tensor, "y": g.sync}

    def ap(x, off=None):
        if not isinstance(x, tuple):
            return x
        name, a, b, s, p = x
        rows = slice(None) if p is None else slice(*p)
        v = T[name][rows, a:b] if s == 1 else T[name][rows, a:b:s]
        return v.indirect(ap(off)) if off else v

    def raw(x):
        codes = x[0] in SCRATCH and SCRATCH[x[0]][2] == Q4
        return ap(x).bitcast(dt.uint8) if codes else ap(x)

    sent = [0]
    for i in order:
        o = ops[i]
        if o["q"] is None:
            continue
        q, call, x = queue[o["q"]], o["call"], o["args"]
        for w in o["waits"]:
            name, count = sems[w]
            q.wait_ge(T.sem[name], count if count > 0 else -count * in_engines)
        ins = None
        if call == "memset":
            ins = q.memset(ap(x[0]), x[1])
        elif call == "copy":
            ins = q.tensor_copy(ap(x[0]), ap(x[1], x[2]))
        elif call == "ts":
            if x[5] is None:
                ins = q.tensor_scalar(ap(x[0]), ap(x[1], x[6]), ap(x[2]), None, x[4])
            else:
                ins = q.tensor_scalar(ap(x[0]), ap(x[1], x[6]), ap(x[2]), ap(x[3]), x[4], x[5])
        elif call == "tt":
            ins = q.tensor_tensor(ap(x[0]), ap(x[1], x[4]), ap(x[2]), x[3])
        elif call == "scatter":
            ins = q.tensor_copy(ap(x[0], x[1]), ap(x[2]))
        elif call == "pickq":
            ins = q.tensor_copy(ap(x[0]).bitcast(dt.uint32), ap(x[1]).bitcast(dt.uint32).indirect(ap(x[2])))
        elif call == "scan":
            ins = q.tensor_tensor_scan(ap(x[0]), ap(x[1]), ap(x[2]), ap(x[3]), x[4], x[5])
        elif call == "turn":
            ins = q.transpose(ap(x[0]), ap(x[1]))
        elif call == "reduce":
            ins = q.tensor_reduce(ap(x[0]), ap(x[1]), AxisListType.X, x[2])
        elif call == "quant":
            ins = q.quantize_mx(ap(x[0]), ap(x[1]), ap(x[2]))
        elif call == "act":
            kw = {}
            if x[3] != 1.0:
                kw["scale"] = ap(x[3])
            if x[4] is not None:
                kw["bias"] = ap(x[4])
            if x[5]:
                kw["accum_out"] = ap(x[5])
            ins = q.activation(ap(x[0]), ap(x[1], x[6]), x[2], **kw)
        elif call == "mm":
            ins = q.matmul_mx(ap(x[0]), ap(x[1]), ap(x[2]), ap(x[3]), ap(x[4]), True, True)
        elif call == "iota":
            if SCRATCH[x[0][0]][2] == I32:
                ins = q.iota(ap(x[0]), x[1], x[2], x[3])
            else:
                ins = q.iota(ap(x[0]), x[1], x[2], x[3], allow_small_or_imprecise_dtypes=True)
        elif call == "select":
            ins = q.affine_select(ap(x[0]), ap(x[0]), x[1], x[2], x[3], x[4], x[5])
        elif call == "dma":
            if x[2]:
                ins = q.dma_start(raw(x[0]), raw(x[1]), accum_op=A.add)
            else:
                ins = q.dma_start(raw(x[0]), raw(x[1]))
        elif call == "send":
            q.remote_dma(raw(x[0]), raw(x[1]), T.sem[x[2]], T.sem["sent"], pid, rid, mask)
            sent[0] += out_engines
        if ins is not None and o["key"] in sems:
            ins.then_inc(T.sem[sems[o["key"]][0]], 1 if o["cls"] == "c" else 16)
    g.wait_ge(T.sem["sent"], sent[0])
